import numpy as np, ml_dtypes
CORES = [9,25,41,57]
N = 4
import mx_ref
BF = ml_dtypes.bfloat16
def gcols(t, e):
    v = np.concatenate([t.reshape(8, 16, -1, 4), np.zeros((8, 16, 1, 4), BF)], axis=2)
    return np.ascontiguousarray(np.stack([v[g][:, e[g]] for g in range(8)])).reshape(128, -1)
def tile(rs):
    return np.stack(rs, axis=2).reshape(128, -1).astype(BF)
def pick(q, e):
    c = np.concatenate([q[0].reshape(128, -1, 4), np.zeros((128, 1, 4), np.uint8)], axis=1); s = np.concatenate([q[1], np.ones((16, 1), np.uint8)], axis=1)
    return (np.ascontiguousarray(c[:, e].reshape(128, -1)), np.ascontiguousarray(s[:, e]))
def join(*qs):
    return (np.concatenate([q[0] for q in qs], axis=1), np.concatenate([q[1] for q in qs], axis=1))
def put(q, e, v):
    c, s = q[0].reshape(128, -1, 4).copy(), q[1].copy(); c[:, e] = v[0].reshape(128, -1, 4); s[:, e] = v[1]
    return (c.reshape(128, -1), s)
def pk(c, s):
    return (np.ascontiguousarray(c), mx_ref.live(s))
def emit(q):
    return q[0], q[1]
def packed(v, rng):
    q = [mx_ref.quantize(np.ascontiguousarray(v[r])) for r in range(N)]
    return np.stack([a for a, b in q]), np.stack([mx_ref.plane(b, rng) for a, b in q])
def values_of_codes():
    e, c = np.zeros((128, 128, 4), np.float32), np.zeros((128, 2, 4), np.uint8)
    e[np.arange(128), np.arange(128), 0] = 1
    c[:127, :, 0] = np.arange(256).reshape(2, 128).T[:127]
    return mx_ref.matmul(mx_ref.quantize(e.reshape(128, 512).astype(BF)), (c.reshape(128, 8), np.full((16, 2), 127, np.uint8))).T.reshape(-1).astype(np.float64)
CODE_VALUE, SCALE_VALUE = values_of_codes(), 2.0 ** (np.arange(256) - 127.0)
def decode(q):
    return (CODE_VALUE[q[0]].reshape(16, 8, -1, 4) * SCALE_VALUE[q[1]][:, None, :, None] + 0.0).reshape(128, -1).astype(np.float32)
def f(rng, *shape):
    return mx_ref.flush((rng.standard_normal(shape, dtype=np.float32) * np.exp2(rng.integers(-2, 3, shape[:-1] + (1,)))).astype(BF))
def wide(rng, *shape, cols=0):
    v = rng.standard_normal(shape, dtype=np.float32) * np.exp2(rng.integers(-12, 13, shape)).astype(np.float32)
    if cols: v *= np.repeat(np.exp2(rng.integers(-cols, cols + 1, shape[:-2] + (1, shape[-1] // 4))) * (rng.random(shape[:-2] + (1, shape[-1] // 4)) > 0.0625), 4, axis=-1).astype(np.float32)
    return mx_ref.flush(v.astype(BF))
C, K = 448, 256
STEP = [1, 2, 3]
def numbers_of(rng):
    return {"x": np.array(f(rng, N, 128, 4 * C)), "u": np.array(f(rng, N, 128, 512)), "v": np.array(f(rng, N, 128, 512))}
def same(rng, w):
    c, s = packed(np.stack([w] * N), rng)
    return {"wc": c, "ws": np.stack([s[0]] * N)}
def weights(rng, still=[]):
    w = np.array(f(rng, 128, 2048)).reshape(8, 16, 4, 8, 16, 4)
    for i in still:
        w[:, i] = 0
        w[:, :, :, :, i] = 0
    return same(rng, w.reshape(128, 2048))
def setup_inputs(rng):
    return {**numbers_of(rng), **weights(rng)}
def setup_inputs_ties(rng):
    d = numbers_of(rng)
    x = d["x"].reshape(N, 8, 16, C, 4)
    x[:, :, 0] = 0
    x[:, :, 0, :, 0] = rng.integers(0, 3, (N, 8, C)).astype(np.float32).astype(BF)
    u = d["u"].reshape(N, 128, 128, 4)
    u[:, :, ::16] = 0
    o = rng.permutation(N)
    for r in range(N):
        for h in range(0, 128, 16): u[r, h, h, 0] = 0.0 if r == o[0] else -1.0 if r == o[1] else 1.0
    return {"x": x.reshape(N, 128, 4 * C), "u": u.reshape(N, 128, 512), "v": d["v"], **weights(rng, [0])}
def setup_inputs_near(rng):
    d = numbers_of(rng)
    x = d["x"].astype(np.float32).reshape(N, 8, 16, C, 4)
    x[:, :, 0] = 0
    x[:, :, 8:] = 0
    s = rng.integers(0, 16, (N, 8, C))
    c = rng.permuted(np.tile(np.arange(8) % 2 * 2.0 - 1.0, (N, 1)), axis=1)
    u = d["u"].reshape(N, 128, 128, 4)
    u[:, :, ::16] = 0
    o = rng.permutation(N) % 4
    for r in range(N):
        k = 1.0 if o[r] == 0 else 2.0 ** -30
        if o[r] < 2:
            x[r, :, 0, :, 0] = c[r][:, None]
            x[r, :, 11, :, 0] = 2.0 ** -10
        else:
            for g in rng.permutation(8)[:4]:
                far = int(rng.integers(C))
                x[r, g, :8, far] = 0
                x[r, g, 0, far, 0] = 2.0 ** 30 * rng.choice([-1.0, 1.0])
        if o[r] == 2:
            t = rng.integers(0, 2, (8, C)) == 1
            x[r, :, 9, :, 0] = np.where(t, 1.125 * 2.0 ** -30 * c[r][:, None], 0.0)
            x[r, :, 10, :, 0] = np.where(t, 0.0, 2.0 ** -30 * c[r][:, None])
        else: x[r, :, 8] = ((s[r][:, :, None] >> np.arange(4)) & 1) * np.exp2(np.arange(4) - 23.0)
        for h in range(0, 128, 16):
            u[r, h, h, 0] = k
            if o[r] == 2:
                u[r, h + 9, h, 0] = k * 1.125
                u[r, h + 10, h, 0] = k * 1.25
            else: u[r, h + 8, h] = k
            if o[r] < 2: u[r, h + 11, h, 0] = k
    return {"x": x.reshape(N, 128, 4 * C).astype(BF), "u": u.reshape(N, 128, 512), "v": d["v"], **weights(rng, [0, 8, 9, 10, 11, 12, 13, 14, 15])}
def setup_inputs_huge(rng):
    d = numbers_of(rng)
    o = rng.permutation(N)
    c = rng.integers(0, 2, (N, 1, 1, C, 1)) * 2.0 - 1.0
    c[o < N // 2] = -1.0
    x = (0.6 + 0.09 * rng.random((N, 8, 16, C, 4))) * c
    x[o == 0] = -0.9 - 0.1 * rng.random((1, 8, 16, C, 4))
    a = 1.0 - 0.1 * rng.random((N, 8, 16, 8, 4))
    for r in range(N): a[r] *= (rng.permutation(8) % 2 * 2.0 - 1.0)[None, None, :, None]
    u = d["u"].reshape(N, 128, 128, 4)
    u[:, :, ::16] = (2.0 ** 30 * a).reshape(N, 128, 8, 4).astype(np.float32).astype(BF)
    w = np.zeros((128, 4, 128, 4), np.float32)
    i = np.arange(128)
    for b in range(4): w[i, b, i, b] = 4
    return {"x": (2.0 ** 30 * x).astype(np.float32).reshape(N, 128, 4 * C).astype(BF), "u": u.reshape(N, 128, 512), "v": d["v"], **same(rng, w.reshape(128, 2048).astype(BF))}
def setup_inputs_jam(rng):
    d = numbers_of(rng)
    x = d["x"].reshape(N, 8, 16, C, 4)
    o = rng.permutation(N) % 4
    a = np.argsort(rng.random((N, 8, C)), axis=2) < K
    i = np.arange(C)
    for r in range(N):
        if o[r] == 0:
            a[r, ::2] = i >= C - K
            a[r, 1::2] = i < K
        if o[r] == 1: a[r] = a[r, 0].copy()
        if o[r] == 2:
            for g in range(8): a[r, g] = (i + int(rng.integers(C))) % C < K
    x[:, :, :2] = 0
    x[:, :, 0, :, 0] = np.where(a, -4.0, -3.0).astype(np.float32).astype(BF)
    x[:, :, 1, :, 0] = 1.0
    t = (1.0 + (2 * rng.integers(0, 64, (N, 8, 8, C, 4)) + 1) / 128.0) * np.exp2(rng.integers(-14, -8, (N, 8, 8, C, 4))) * (rng.integers(0, 2, (N, 8, 8, C, 4)) * 2.0 - 1.0)
    x[:, :, 8:] = t.astype(np.float32).astype(BF)
    x[:, :, 8, :, 0] = 1.96875
    u = d["u"].reshape(N, 128, 128, 4)
    u[:, :, ::16] = 0
    for h in range(0, 128, 16): u[:, h, h, 0] = -1.0
    for r in range(N):
        if o[r] == 3:
            x[r, :, 0, :, 0] = -4.0
            x[r, :, 9] = 0
            x[r, :, 9, :, 0] = (np.where(a[r], 4.0, 3.0) * np.exp2(-13.0 - np.arange(8) % 4)[:, None]).astype(np.float32).astype(BF)
            for h in range(0, 128, 16): u[r, h + 9, h, 0] = 1.0
    w = np.array(f(rng, 128, 2048)).reshape(8, 16, 4, 8, 16, 4)
    w[:, :, :, :, :2] = 0
    w[:, :, :, :, 8:] = 0
    return {"x": x.reshape(N, 128, 4 * C), "u": u.reshape(N, 128, 512), "v": d["v"], **same(rng, fall(w))}
def fall(v):
    for g in range(8): v[g, 1, 0, g, 0, 0] = 128.0
    return v.reshape(128, 2048)
def setup_inputs_spread(rng):
    d = setup_inputs(rng)
    d["x"] = wide(rng, N, 128, 4 * C, cols=6)
    return d
def check_inputs(d):
    b = []
    for k in ("x", "u", "v"):
        a = np.abs(d[k].astype(np.float32))
        if not (np.isfinite(a).all() and ((a == 0) | (a >= 2.0 ** -30) & (a <= 2.0 ** 30)).all()): b.append("a value of " + k)
    if ((d["wc"] & 0x7F) == 0x7F).any(): b.append("a code of wc that is no number")
    for k in ("wc", "ws"):
        if (d[k] != d[k][:1]).any(): b.append(k + " isn't the same on all ranks")
    none, least, most = [emit(mx_ref.quantize(np.full((128, 16), k, np.float32).astype(BF)))[1][0, 0] for k in (0.0, 2.0 ** -30, 2.0 ** 30)]
    for r in range(N):
        s = mx_ref.live(d["ws"][r])
        if ((s != none) & ((s < least) | (s > most))).any(): b.append("a scale of ws")
    return b
def places(s):
    a = np.sort(np.argsort(-s, axis=2, kind="stable")[:, :, :K], axis=2)
    j = np.arange(K)
    c = a.copy()
    at = np.stack([j] * N)
    for g in range(7):
        n = np.sum(a[:, g + 1][:, None, :] < a[:, g][:, :, None], axis=2)
        p = np.maximum.accumulate(n - j, axis=1) + j
        for r in range(N):
            m = int(np.sum(p[r] < K))
            p[r, m:] = np.setdiff1d(j, p[r, :m])
            at[r] = p[r][at[r]]
            c[r, g + 1] = a[r, g + 1][at[r]]
    return c
def reference(x, u, v, wc, ws):
    qu = [mx_ref.quantize(u[r]) for r in range(N)]
    lay = [pk(wc[r], ws[r]) for r in range(N)]
    now = [x[r] for r in range(N)]
    for e in STEP:
        q = [mx_ref.quantize(now[r]) for r in range(N)]
        own = [decode(q[r]) for r in range(N)]
        c = places(np.stack([mx_ref.matmul(qu[r], q[r])[::16] for r in range(N)]) + np.float32(0.0))
        made = []
        for r in range(N):
            z = mx_ref.quantize(gcols(own[r].astype(BF), c[r]))
            h = tile([np.maximum(mx_ref.matmul(pick(lay[r], np.arange(128 * b, 128 * b + 128)), z), np.float32(0.0)) * np.float32(0.015625) for b in range(4)])
            made.append(decode(mx_ref.quantize(h)))
        for r in range(N):
            a, b = own[r].reshape(8, 16, C, 4).copy(), made[r ^ e].reshape(8, 16, K, 4)
            for g in range(8): a[g][:, c[r, g]] += b[g]
            now[r] = a.reshape(128, 4 * C).astype(BF)
    y, pl = np.zeros((N, 128, C), np.float32), np.zeros((N, 8, K), np.float32)
    oc, osc = np.zeros((N, 128, 4 * C), np.uint8), np.zeros((N, 16, C), np.uint8)
    for r in range(N):
        q = mx_ref.quantize(now[r])
        y[r] = mx_ref.matmul(mx_ref.quantize(v[r]), q)
        pl[r] = c[r]
        oc[r], osc[r] = emit(q)
    return {"y": y, "pl": pl, "oc": oc, "osc": osc}

@@ -1,0 +1,459 @@
+from concourse.mybir import dt, AluOpType, AxisListType, ActivationFunctionType
+
+C, K, ROUNDS = 448, 256, (1, 2, 3)
+F32, BF, I32, U16, Q4, U8 = "float32", "bfloat16", "int32", "uint16", "float8_e4m3fn_x4", "uint8"
+SB = {
+    "xin": (4 * C, BF), "uin": (512, BF), "vin": (512, BF), "qu0": (128, Q4), "su0": (128, U8), "qu": (128, Q4), "su": (128, U8),
+    "qv": (128, Q4), "sv": (128, U8), "qw": (512, Q4), "sw": (512, U8),
+    "o16": (8, U16), "o15": (8, U16), "et": (516, BF), "qe": (512, Q4), "se": (512, U8),
+    "ct": (1536, BF), "qc": (384, Q4), "scc": (384, U8), "ctie": (C, BF),
+    "xt": (4 * C, BF), "qx": (C, Q4), "sx": (C, U8), "ff": (4 * C, BF),
+    "junk": (C, BF), "ge": (C, BF), "sig": (C, BF), "neq": (C, BF), "ns": (C, BF),
+    "mt": (4 * C, BF), "qm": (C, Q4), "sm": (C, U8), "pos": (28, U16), "t0": (960, F32), "ta": (K, F32), "tb": (K, F32), "cs2": (K, F32),
+    "bt": (512, BF), "qb": (128, Q4), "sb": (128, U8), "loff": (128, U16), "offc": (16, U16), "thf": (C, F32), "offt": (28, U16), "pf": (K, F32),
+    "zt": (4 * K, BF), "qz": (K, Q4), "sz": (K, U8), "ht": (4 * K, BF), "dp": (4 * 272, BF), "d3": (C, BF), "yo": (C, F32),
+}
+for _k in range(3):
+    SB["qh%d" % _k], SB["sh%d" % _k], SB["ql%d" % _k], SB["sl%d" % _k] = (K, Q4), (K, U8), (K, Q4), (K, U8)
+POOLS = {
+    "kf": (F32, {"kc": 16, "half": 145, "two": 145, "zer": C, "btab": 290, "ya": 64, "yt": 64, "j16": 16, "nn": 16, "ra": 16, "rb": 16, "rc": 16,
+                 "t2": 16, "tab": 64, "mbig": 64, "rat": 64, "mc": 32, "mge": 32, "m448": 32, "rep": 128, "ca": 16, "cb": 16, "cd": 16, "ce": 16,
+                 "cmul": 512, "csum": 512, "c1024": C, "kk": 28, "k2": 28, "mg": 128, "ia": 128, "ic": 128, "idt": 128, "kio": K}),
+    "ki": (I32, {"pint": 2, "rint": 2, "hint": 1, "o16i": 8}),
+    "wf": (F32, {"sc": 64, "m1": 96, "tr1": 128, "tr2": 128, "tr3": 64, "tr4": 128, "cand": 64, "cand2": 64, "steps": 6, "vs": C, "cap": C,
+                 "vv": C, "cs": C, "x1": 28, "e1": 28, "u1": 28, "o1": 28, "x2": 28, "x3": 28, "g1": 128, "g2": 128, "l1": 128, "cs3": K, "cs4": C}),
+    "wi": (I32, {"xi": 28, "zi": 28, "ai": 28, "ni": 28, "ci": 16, "cj": 16, "pa": K, "pb": K}),
+}
+AT = {}
+for _p, (_d, _m) in POOLS.items():
+    _o = 0
+    for _n, _w in _m.items():
+        AT[_n] = (_p, _o, _w)
+        _o += -(-_w // 8) * 8
+    SB[_p] = (_o, _d)
+SCRATCH = {n: ("sbuf", [128, w], d) for n, (w, d) in SB.items()}
+for _k in range(8):
+    SCRATCH["b%d" % _k] = ("psum", [128, 512], F32)
+SEMAPHORES = ["sV", "sS", "sP", "sG", "snd", "arr0", "arr1", "arr2"] + ["d%d" % i for i in range(16)]
+
+BIG = 2.0 ** 80
+EPS = 2.0 ** -10
+OFF = 1024.0
+
+
+def rank_program(g, core, T, topo):
+    rank = T.rank_of(core)
+    if rank is None:
+        return
+    A, ACT = AluOpType, ActivationFunctionType
+    Q = {"V": g.vector, "S": g.scalar, "P": g.tensor, "G": g, "Y": g.sync}
+    count = {"sV": 0, "sS": 0, "sP": 0, "sG": 0}
+    known = {e: {} for e in Q}
+    clock = {}
+    log = {}
+    ndma = [0]
+
+    def v(n, a=0, b=None, s=1):
+        buf, o, w = AT[n] if n in AT else (n, 0, T[n].shape[1])
+        b = w if b is None else b
+        return (T[buf][:, o + a:o + b:s] if s > 1 else T[buf][:, o + a:o + b], n, a, b, s)
+
+    def c1(n, a):
+        return v(n, a, a + 1)
+
+    def meet(x, y):
+        if x[3] <= y[2] or y[3] <= x[2]:
+            return False
+        return not (x[4] == y[4] and x[4] > 1 and (x[2] - y[2]) % x[4])
+
+    def wait(e, sem, val):
+        if known[e].get(sem, 0) >= val:
+            return
+        Q[e].wait_ge(T.sem[sem], val)
+        known[e][sem] = val
+        for s2, v2 in clock.get((sem, val), {}).items():
+            if known[e].get(s2, 0) < v2:
+                known[e][s2] = v2
+
+    def op(e, call, reads, writes, dma=False):
+        need = {}
+        both = [(x, False) for x in reads] + [(x, True) for x in writes]
+        for view, wr in both:
+            psum = view[1][0] == "b" and view[1][1:].isdigit()
+            for (o, ow, oe, sem, val) in log.get(view[1], []):
+                if (psum and oe != e) or ((wr or ow) and meet(view, o)):
+                    need[sem] = max(need.get(sem, 0), val)
+        for sem, val in need.items():
+            wait(e, sem, val)
+        if dma:
+            sem, val = "d%d" % ndma[0], 16
+            ndma[0] += 1
+            call().then_inc(T.sem[sem], 16)
+        else:
+            sem = "s" + e
+            count[sem] += 1
+            val = count[sem]
+            call().then_inc(T.sem[sem], 1)
+        clock[(sem, val)] = dict(known[e])
+        for view, wr in both:
+            old = log.get(view[1], [])
+            if wr and view[4] == 1:
+                old = [r for r in old if not (view[2] <= r[0][2] and r[0][3] <= view[3])]
+            log[view[1]] = old + [(view, wr, e, sem, val)]
+
+    def aps(*xs):
+        return [x for x in xs if isinstance(x, tuple)]
+
+    def ap(x):
+        return x[0] if isinstance(x, tuple) else x
+
+    def ts(o, i, s1, op0, s2=None, op1=None):
+        if op1 is None:
+            op("V", lambda: g.vector.tensor_scalar(o[0], i[0], ap(s1), None, op0), aps(i, s1), [o])
+        else:
+            op("V", lambda: g.vector.tensor_scalar(o[0], i[0], ap(s1), ap(s2), op0, op1), aps(i, s1, s2), [o])
+
+    def tt(o, a, b, op0, off=None):
+        src = a[0].indirect(off[0]) if off else a[0]
+        op("V", lambda: g.vector.tensor_tensor(o[0], src, b[0], op0), aps(a, b, off), [o])
+
+    def cp(o, i, off=None):
+        src = i[0].indirect(off[0]) if off else i[0]
+        op("V", lambda: g.vector.tensor_copy(o[0], src), aps(i, off), [o])
+
+    def scat(o, off, i):
+        op("V", lambda: g.vector.tensor_copy(o[0].indirect(off[0]), i[0]), [i, off], [o])
+
+    def scan(o, d0, d1, init, op0, op1):
+        op("V", lambda: g.vector.tensor_tensor_scan(o[0], d0[0], d1[0], ap(init), op0, op1), aps(d0, d1, init), [o])
+
+    def red(o, i, op0):
+        op("V", lambda: g.vector.tensor_reduce(o[0], i[0], AxisListType.X, op0), [i], [o])
+
+    def tr(o, i):
+        op("V", lambda: g.vector.transpose(o[0], i[0]), [i], [o])
+
+    def ms(o, val):
+        op("V", lambda: g.vector.memset(o[0], val), [], [o])
+
+    def quant(q, s, i):
+        op("V", lambda: g.vector.quantize_mx(q[0], s[0], i[0]), [i], [q, s])
+
+    def mm(o, lq, ls, rq, rs):
+        op("P", lambda: g.tensor.matmul_mx(o[0], lq[0], ls[0], rq[0], rs[0], True, True), [lq, ls, rq, rs], [o])
+
+    def act(o, i, func, bias=None, scale=None, acc=None, off=None):
+        src = i[0].indirect(off[0]) if off else i[0]
+        kw = {}
+        if bias is not None:
+            kw["bias"] = ap(bias)
+        if scale is not None:
+            kw["scale"] = ap(scale)
+        if acc is not None:
+            kw["accum_out"] = acc[0]
+        op("S", lambda: g.scalar.activation(o[0], src, func, **kw), aps(i, bias, scale, off), aps(o, acc))
+
+    def iota(o, pat, base, cm):
+        if o[1] in POOLS["ki"][1]:
+            op("G", lambda: g.iota(o[0], pat, base, cm), [], [o])
+        else:
+            op("G", lambda: g.iota(o[0], pat, base, cm, allow_small_or_imprecise_dtypes=True), [], [o])
+
+    def sel(o, i, pat, cmp, fill, base, cm):
+        op("G", lambda: g.affine_select(o[0], i[0], pat, cmp, fill, base, cm), [i], [o])
+
+    def dma(e, o, i, reads, writes):
+        op(e, lambda: Q[e].dma_start(o, i), reads, writes, dma=True)
+
+    dma("S", T.uin[:], T.u[:], [], [v("uin")])
+    dma("Y", T.xin[:], T.x[:], [], [v("xin")])
+    dma("Y", T.qw[:].bitcast(dt.uint8), T.wc[:], [v("xin")], [v("qw")])
+    dma("Y", T.sw[:], T.ws[:], [], [v("sw")])
+    dma("Y", T.vin[:], T.v[:], [], [v("vin")])
+
+    RF, RM1, RP1, HM0, HM1, R0, UN0, UNA, UNB, UNC, R2, O15 = [c1("kc", i) for i in range(12)]
+    G16 = [[-16, 8], [0, 16]]
+    ms(v("et"), 0.0)
+    iota(v("pint"), [[15, 2]], 0, 1)
+    iota(v("o16i"), [[16, 8]], 0, 0)
+    iota(v("j16"), [[1, 16]], 0, 0)
+    sel(v("et"), v("et"), [[1, 516]], A.not_equal, 1.0, -3, -4)
+    iota(v("ct"), [[0, 1536]], 0, 0)
+    ms(v("half"), 0.5)
+    ms(v("two"), 2.0)
+    ms(v("zer"), 0.0)
+    scan(v("btab", 0, 145), v("half"), v("zer", 0, 145), -2.0 ** 72, A.mult, A.add)
+    scan(v("btab", 145, 290), v("two"), v("zer", 0, 145), 2.0 ** -74, A.mult, A.add)
+    ts(v("rint"), v("pint"), 15, A.bitwise_and)
+    ts(v("hint"), c1("pint", 0), 16, A.bitwise_and)
+    cp(v("o16"), v("o16i"))
+    for i in range(2):
+        act(v("ya", 16 * i, 16 * i + 16), v("btab", 17, 289, 17), ACT.Copy)
+        act(v("ya", 32 + 16 * i, 48 + 16 * i), v("btab", 1, 17), ACT.Copy)
+    cp(v("kc", 0, 2), v("rint"))
+    ts(RP1, c1("rint", 0), 1.0, A.add)
+    ts(HM1, v("hint"), 8.0, A.subtract, BIG / 8, A.mult)
+    ts(HM0, v("hint"), 8.0, A.subtract, -BIG / 8, A.mult)
+    ts(v("nn"), v("j16"), 1.0 / 17, A.mult, RP1, A.add)
+    tr(v("yt"), v("ya"))
+    T1 = c1("yt", 0)
+    ts(v("ca"), v("j16"), RF, A.not_equal)
+    ts(v("cb"), v("j16"), RP1, A.is_equal, 4095.0, A.mult)
+    ts(v("cd"), v("j16"), RM1, A.not_equal)
+    ts(v("ce"), v("j16"), RP1, A.is_equal, 2.0 ** 40, A.mult)
+    ts(v("rep", 0, 16), v("j16"), RF, A.is_equal)
+    ts(UN0, RF, 15.0, A.is_equal)
+    ts(v("ra"), v("nn"), 144.5 / 17, A.is_gt, 3.0, A.mult)
+    ts(v("rb"), v("nn"), 143.5 / 17, A.is_gt, -1.5, A.mult)
+    tt(v("cmul", 0, 16), v("ca"), v("cb"), A.add)
+    tt(v("csum", 0, 16), v("cd"), v("ce"), A.max)
+    ts(UNB, UN0, 2.0 ** -12, A.max)
+    quant(v("qu0"), v("su0"), v("uin"))
+    tt(v("rc"), v("ra"), v("rb"), A.add)
+    for w in (16, 32, 64):
+        for n in ("rep", "cmul", "csum"):
+            act(v(n, w, 2 * w), v(n, 0, w), ACT.Copy)
+    op("V", lambda: g.vector.tensor_copy(T.qu[:, 0:128].bitcast(dt.uint32), T.qu0[:, 0:128].bitcast(dt.uint32).indirect(T.o16[:, 0:8])),
+       [v("qu0"), v("o16")], [v("qu")])
+    ts(v("ra"), v("rc"), 0.5, A.add)
+    act(v("su"), v("su0"), ACT.Copy, off=v("o16"))
+    for i in range(4):
+        ts(v("mbig", 16 * i, 16 * i + 16), v("zer", 0, 16), (HM0, HM1)[i % 2], A.add)
+    scan(v("t2"), v("ra"), v("zer", 0, 16), T1, A.mult, A.add)
+    cp(c1("tr1", 31), c1("yt", 32))
+    ms(c1("tr1", 96), -2.0 ** 71)
+    ts(v("tab", 32, 64), v("mbig", 0, 32), T1, A.min)
+    for i in range(2):
+        ts(v("tab", 16 * i, 16 * i + 16), v("t2"), (HM0, HM1)[i], A.min)
+    act(v("mg"), v("zer", 0, 128), ACT.Identity, bias=UNB)
+    for w in (128, 256):
+        for n in ("cmul", "csum"):
+            act(v(n, w, 2 * w), v(n, 0, w), ACT.Copy)
+    ms(v("rat", 32, 64), 0.0)
+    for i in range(2):
+        ts(v("rat", 16 * i, 16 * i + 16), v("j16"), 1.0, A.add)
+    ts(v("mc"), v("mbig", 0, 32), -64.0, A.min, -1000.0, A.max)
+    for o in (0, 512):
+        sel(v("ct", o, o + 512, 4), v("ct", o, o + 512, 4), G16, A.not_equal, -EPS, -8, 1)
+    sel(v("ct", 0, 64, 4), v("ct", 0, 64, 4), [[0, 16]], A.not_equal, 1.0, 0, 1)
+    sel(v("ct", 64, 512, 4), v("ct", 64, 512, 4), [[-16, 7], [0, 16]], A.not_equal, 1.0, 0, 1)
+    sel(v("ct", 512, 1024, 4), v("ct", 512, 1024, 4), G16, A.not_equal, 1.0, 0, 1)
+    for t in range(2):
+        sel(v("ct", 1024 + t, 1536, 4), v("rep"), [[16, 8], [0, 16]], A.is_gt, 0.0, 0, -1)
+    iota(v("kk"), [[32, 28]], 2050, 0)
+    iota(v("ia"), [[0, 8], [16, 16]], 0, 0)
+    sel(v("mg"), v("mg"), G16, A.is_ge, 0.0, 0, 1)
+    sel(v("mg"), v("mg"), [[16, 8], [0, 16]], A.is_ge, 0.0, 15, -1)
+    iota(v("kio"), [[1, K]], 2, 0)
+
+    def constants(i):
+        if i == 0:
+            for b in range(4):
+                quant(v("qe", 128 * b, 128 * b + 128), v("se", 128 * b, 128 * b + 128), v("et", 3 - b, 515 - b))
+            act(v("c1024"), v("zer"), ACT.Identity, bias=EPS)
+        if i == 1:
+            act(v("ctie"), v("zer"), ACT.Copy)
+        if i == 2:
+            act(v("bt", 0, C), v("zer"), ACT.Copy)
+        if i in (3, 4):
+            ms(v("mt", 2 * C * (i - 3), 2 * C * (i - 2)), 0.0)
+        if i == 5:
+            ts(R0, RF, 0.0, A.is_equal, 1448.0, A.mult)
+            ts(v("mge"), v("mbig", 0, 32), -1.0, A.mult, 256.0, A.max)
+            ts(O15, RF, 16.0, A.mult, 15.0, A.add)
+            ts(UNC, UN0, 2.0 ** -40, A.max, -1024.0, A.mult)
+            ts(UNA, UN0, 2.0 ** -12, A.max, 1024.0, A.mult)
+            ts(v("m448"), v("mbig", 0, 32), R0, A.min, -1000.0, A.add)
+            ts(v("o15"), v("zer", 0, 8), O15, A.add)
+        if i == 6:
+            quant(v("qc"), v("scc"), v("ct"))
+        if i == 7:
+            act(v("ic"), v("ia"), ACT.Identity, bias=RF)
+            sel(v("idt"), v("ic"), [[16, 8], [0, 16]], A.is_ge, -1.0, 15, -1)
+            ms(c1("ctie", 0), -0.1875)
+            ms(v("bt", C, 512), 0.0)
+            ms(v("dp", 0, 4 * 272, 272), 0.0)
+            ts(v("k2"), v("kk"), RF, A.add, RF, A.add)
+
+    S = lambda i: c1("sc", i)
+    P0, P1 = v("b0", 0, C), v("b1", 0, C)
+
+    def count_at(thr, c):
+        act(v("junk"), P0, ACT.Sign, bias=thr, scale=-1.0, acc=c)
+
+    for k, e in enumerate(ROUNDS):
+        partner = T.cores[rank ^ e]
+        quant(v("qx"), v("sx"), v("xin" if k == 0 else "xt"))
+        mm(P0, v("qu"), v("su"), v("qx"), v("sx"))
+        mm(P1, v("qu"), v("su"), v("qx"), v("sx"))
+        count_at(T1, S(0))
+        if k == 0:
+            constants(0)
+        else:
+            ms(v("thf"), 1.0)
+        for b in range(4):
+            mm(v("b%d" % (2 + b), 0, C), v("qe", 128 * b, 128 * b + 128), v("se", 128 * b, 128 * b + 128), v("qx"), v("sx"))
+        ts(S(1), S(0), -64.0, A.is_gt, -2 * BIG, A.mult)
+        ts(v("m1", 0, 64), v("tab"), S(1), A.add)
+        tr(v("tr1", 32, 96), v("m1", 0, 64))
+        red(S(2), v("tr1", 31, 64), A.max)
+        count_at(S(2), S(3))
+        if k == 0:
+            constants(1)
+        red(c1("tr2", 96), v("tr1", 64, 97), A.max)
+        ts(S(4), S(2), -0.5, A.mult, S(2), A.max)
+        ts(S(6), c1("tr2", 96), -0.5, A.mult, c1("tr2", 96), A.max)
+        ts(S(5), S(4), 2.0 ** -72, A.max, 0.125, A.mult)
+        ts(S(7), S(6), 2.0 ** -72, A.max, 0.125, A.mult)
+        ts(v("cand"), v("rat"), S(5), A.mult, S(2), A.add)
+        ts(c1("tr2", 31), RP1, S(7), A.mult, c1("tr2", 96), A.add)
+        tt(v("cand2"), v("cand"), v("mbig"), A.min)
+        ts(S(8), S(3), -64.0, A.is_gt, -2 * BIG, A.mult)
+        ts(v("m1", 0, 64), v("cand2"), S(8), A.add)
+        tr(v("tr2", 32, 96), v("m1", 0, 64))
+        red(S(20), v("tr2", 31, 64), A.max)
+        RW = S(12)
+        for i in range(5):
+            thr, cnt = S(20 + i), S(30 + i)
+            count_at(thr, cnt)
+            if i == 0:
+                if k == 0:
+                    constants(2)
+                red(S(9), v("tr2", 64, 97), A.max)
+                ts(S(10), S(9), -0.5, A.mult, S(9), A.max)
+                ts(S(11), S(10), 2.0 ** -72, A.max, 0.125, A.mult)
+                ts(RW, RP1, S(11), A.mult)
+                ts(v("steps"), v("btab", 198, 219, 4), S(11), A.mult)
+                ts(c1("tr3", 32), RW, 1.0 / 16, A.mult, S(9), A.add)
+            else:
+                ts(c1("tr3", 32), RW, -15.0 / 16 * 16.0 ** -i, A.mult, thr, A.add)
+                if k == 0:
+                    act(v("ff", C * (i - 1), C * i), v("b%d" % (1 + i), 0, C), ACT.Copy)
+                    constants(i + 2)
+                else:
+                    cp(v("ff", C * (i - 1), C * i), v("b%d" % (1 + i), 0, C))
+            ts(v("m1", 0, 32), v("mc"), cnt, A.is_ge, c1("steps", 5 - i), A.mult)
+            tr(v("tr3", 0, 32), v("m1", 0, 32))
+            red(S(21 + i), v("tr3", 0, 33), A.add)
+        thr, cnt, cge, TH, NEED = S(25), S(35), S(36), S(38), S(39)
+        count_at(thr, cnt)
+        ts(v("ge"), P1, thr, A.is_ge)
+        ts(c1("tr4", 31), RW, -16.0 ** -5, A.mult, thr, A.add)
+        red(cge, v("ge"), A.add)
+        ts(S(37), cge, cnt, A.add, EPS, A.mult)
+        ts(v("m1", 0, 32), v("mge"), cge, A.is_le, c1("steps", 0), A.mult)
+        ts(v("m1", 64, 96), v("m448"), cge, A.subtract, EPS, A.mult)
+        ts(v("m1", 32, 64), v("mge"), cge, A.is_le, S(37), A.mult)
+        tr(v("tr4", 32, 128), v("m1"))
+        red(TH, v("tr4", 31, 64), A.add)
+        red(NEED, v("tr4", 64, 128), A.max)
+        act(v("sig"), P0, ACT.Sign, bias=TH, scale=-1.0)
+        ts(v("neq"), P1, TH, A.is_equal, -EPS, A.mult)
+        if k == 0:
+            constants(7)
+        scan(v("ns"), v("neq"), v("ctie"), NEED, A.add, A.add)
+        M0 = v("mt", 0, 4 * C, 4)
+        tt(M0, v("sig"), v("ns"), A.is_le)
+        quant(v("qm"), v("sm"), v("mt"))
+        mm(v("b6", 0, C), v("qc", 0, 128), v("scc", 0, 128), v("qm"), v("sm"))
+        mm(v("b7", 0, C), v("qc", 128, 256), v("scc", 128, 256), v("qm"), v("sm"))
+        scan(v("vs"), M0, v("c1024"), -225.0 * EPS, A.add, A.add)
+        scan(v("cap"), v("b6", 0, C), v("zer"), OFF, A.add, A.add)
+        scan(v("vv"), v("b7", 0, C), v("cap"), OFF, A.add, A.min)
+        MC, NM = S(40), S(41)
+        scan(v("cs"), v("csum", 0, C), v("vv"), OFF, A.mult, A.add)
+        act(MC, c1("vv", C - 1), ACT.Identity, bias=0.5 - 2 * OFF - 1538.0, scale=2.0)
+        act(NM, c1("vv", C - 1), ACT.Identity, bias=2 * OFF + 2049.5, scale=-2.0)
+        tt(v("x1"), v("cs", 14, C, 16), v("cs", 15, C, 16), A.max)
+        ts(v("xi"), v("x1"), UNC, A.mult, 1024.0 * (2 * OFF + 513) + 1, A.add)
+        ts(v("ai"), v("xi"), 10, A.logical_shift_right, 1022, A.bitwise_and)
+        ts(v("ni"), v("xi"), 1, A.bitwise_and)
+        ts(v("zi"), v("xi"), 2047, A.bitwise_and)
+        ts(v("u1"), v("ai"), -1.0, A.mult, NM, A.add)
+        tt(v("o1"), v("ni"), v("k2"), A.mult)
+        tt(v("e1"), v("zi"), v("ai"), A.add)
+        tt(v("x2"), v("u1"), v("o1"), A.max)
+        tt(v("x3"), v("x2"), v("e1"), A.max)
+        ts(v("pos"), v("x3"), MC, A.add, 0.5, A.mult)
+        scat(v("t0"), v("pos"), v("vs"))
+        scan(v("cs2"), v("cmul", 0, K), v("t0", 0, K), 0.0, A.mult, A.max)
+        tt(v("g1", 16, 112), v("cs2"), v("mg", 16, 112), A.mult, off=v("o15", 0, 6))
+        HI, LO = v("bt", 64, 448, 4), v("bt", 65, 448, 4)
+        ts(HI, v("g1", 16, 112), 1.5 * 2.0 ** 27, A.add, -1.5 * 2.0 ** 27, A.add)
+        ts(v("g2", 16, 112), v("g1", 16, 112), 1.5 * 2.0 ** 23, A.add, -1.5 * 2.0 ** 23, A.add)
+        tt(LO, v("g2", 16, 112), HI, A.subtract)
+        quant(v("qb"), v("sb"), v("bt"))
+        mm(v("b6", 0, 128), v("qc", 256, 384), v("scc", 256, 384), v("qb"), v("sb"))
+        if k == 0:
+            ms(v("thf"), 1.0)
+        tt(v("l1", 16, 112), v("b6", 16, 112), v("idt", 16, 112), A.add)
+        cp(v("loff", 16, 112), v("l1", 16, 112))
+        src = "t0"
+        for h in range(6, 0, -1):
+            dst = "ta" if h % 2 == 0 else "tb"
+            cp(v(dst, 0, 128), v(src, 0, K), off=v("loff", 16 * h, 16 * h + 8))
+            act(v(dst, 128, K), v(src, 0, K), ACT.Copy, off=v("loff", 16 * h + 8, 16 * h + 16))
+            src = dst
+        scan(v("cs3"), v("cmul", 0, K), v(src), 0.0, A.mult, A.max)
+        ts(v("ci"), v("cs3", 15, K, 16), UNA, A.mult, 224.0, A.add)
+        ts(v("cj"), v("ci"), 1023, A.bitwise_and)
+        cp(v("offc"), v("cj"))
+        qh, sh, ql, sl, arr = "qh%d" % k, "sh%d" % k, "ql%d" % k, "sl%d" % k, "arr%d" % k
+        rid, pid, _ = topo.addr(partner)
+        mask, ne = topo.mask(core, partner), len(topo.engines(core, partner))
+        banks = ((0, 1, 2, 3), (0, 4, 6, 7))
+        for h in range(2):
+            lo, hi, off = 128 * h, 128 * h + 128, v("offc", 8 * h, 8 * h + 8)
+            for b in range(2):
+                act(v("zt", 4 * lo + 2 + b, 4 * hi, 4), v("ff", C * (2 + b), C * (3 + b)), ACT.Copy, off=off)
+                cp(v("zt", 4 * lo + b, 4 * hi, 4), v("ff", C * b, C * (b + 1)), off=off)
+            quant(v("qz", lo, hi), v("sz", lo, hi), v("zt", 4 * lo, 4 * hi))
+            if h == 0:
+                for b in (0, 2, 1, 3):
+                    mm(v("b%d" % banks[0][b], 0, 128), v("qw", 128 * b, 128 * b + 128), v("sw", 128 * b, 128 * b + 128), v("qz", lo, hi), v("sz", lo, hi))
+        for h in range(2):
+            lo, hi = 128 * h, 128 * h + 128
+            for b in ((0, 1), (1, 0))[h]:
+                ts(v("ht", 4 * lo + b, 4 * hi, 4), v("b%d" % banks[h][b], 0, 128), 0.0, A.max, 0.015625, A.mult)
+                act(v("ht", 4 * lo + 2 + b, 4 * hi, 4), v("b%d" % banks[h][2 + b], 0, 128), ACT.Relu, scale=0.015625)
+                if h == 0 and b == 0:
+                    for b2 in (3, 1, 2, 0):
+                        mm(v("b%d" % banks[1][b2], 0, 128), v("qw", 128 * b2, 128 * b2 + 128), v("sw", 128 * b2, 128 * b2 + 128), v("qz", 128, K), v("sz", 128, K))
+            quant(v(qh, lo, hi), v(sh, lo, hi), v("ht", 4 * lo, 4 * hi))
+            wait("G", "sV", count["sV"])
+            g.remote_dma(T[ql][:, lo:hi].bitcast(dt.uint8), T[qh][:, lo:hi].bitcast(dt.uint8), T.sem[arr], T.sem.snd, pid, rid, mask)
+        g.remote_dma(T[sl][:], T[sh][:], T.sem[arr], T.sem.snd, pid, rid, mask)
+        scat(v("thf"), v("offc"), v("kio"))
+        scan(v("cs4"), v("cmul", 0, C), v("thf"), 0.0, A.mult, A.max)
+        ts(v("offt"), v("cs4", 15, C, 16), UNB, A.mult, -1.0, A.add)
+        if k == 0:
+            quant(v("qv"), v("sv"), v("vin"))
+        if k == 2:
+            ts(v("pa"), v(src), 1024.0, A.mult, 224.0, A.add)
+            ts(v("pb"), v("pa"), 1023, A.bitwise_and)
+            cp(v("pf"), v("pb"))
+            dma("Y", T.pl[:], T.pf[0:128:16, :], [v("pf")], [])
+        wait("P", arr, 3 * ne)
+        for b in range(4):
+            bank = v("b%d" % (0, 1, 6, 7)[b], 0, K)
+            mm(bank, v("qe", 128 * b, 128 * b + 128), v("se", 128 * b, 128 * b + 128), v(ql), v(sl))
+            act(v("dp", 272 * b + 1, 272 * b + 1 + K), bank, ACT.Copy)
+            if b < 3:
+                tt(v("xt", b, 4 * C, 4), v("dp", 272 * b, 272 * b + 257), v("ff", C * b, C * (b + 1)), A.add, off=v("offt"))
+        act(v("d3"), v("dp", 272 * 3, 272 * 3 + 257), ACT.Copy, off=v("offt"))
+        tt(v("xt", 3, 4 * C, 4), v("b5", 0, C), v("d3"), A.add)
+
+    quant(v("qx"), v("sx"), v("xt"))
+    for h in range(2):
+        mm(v("b%d" % h, 0, C // 2), v("qv"), v("sv"), v("qx", h * C // 2, (h + 1) * C // 2), v("sx", h * C // 2, (h + 1) * C // 2))
+    dma("Y", T.oc[:], T.qx[:].bitcast(dt.uint8), [v("qx")], [])
+    cp(v("yo", 0, C // 2), v("b0", 0, C // 2))
+    act(v("yo", C // 2, C), v("b1", 0, C // 2), ACT.Copy)
+    dma("Y", T.y[:], T.yo[:], [v("yo")], [])
+    for i in range(4):
+        dma("S", T.osc[4 * i:4 * i + 4, :], T.sx[32 * i:32 * i + 4, :], [v("sx")], [])
+    wait("G", "snd", 9 * ne)
+    for i in range(ndma[0]):
+        wait("G", "d%d" % i, 16)
+    for s in count:
+        wait("G", s, count[s])

@@ -9,7 +9,7 @@ SB = {
     "ct": (1536, BF), "qc": (384, Q4), "scc": (384, U8), "ctie": (C, BF),
     "xt": (4 * C, BF), "qx": (C, Q4), "sx": (C, U8), "ff": (4 * C, BF),
     "junk": (C, BF), "ge": (C, BF), "sig": (C, BF), "neq": (C, BF), "ns": (C, BF),
-    "mt": (4 * C, BF), "qm": (C, Q4), "sm": (C, U8), "pos": (28, U16), "t0": (960, F32), "ta": (K, F32), "tb": (K, F32), "cs2": (K, F32),
+    "mt": (4 * C, BF), "qm": (C, Q4), "sm": (C, U8), "pos": (32, U16), "t0": (960, F32), "ta": (K, F32), "tb": (K, F32), "cs2": (K, F32),
     "bt": (512, BF), "qb": (128, Q4), "sb": (128, U8), "loff": (128, U16), "offc": (16, U16), "thf": (C, F32), "offt": (28, U16), "pf": (K, F32),
     "zt": (4 * K, BF), "qz": (K, Q4), "sz": (K, U8), "ht": (4 * K, BF), "dp": (4 * 272, BF), "d3": (C, BF), "yo": (C, F32),
 }
@@ -17,12 +17,12 @@ for _k in range(3):
     SB["qh%d" % _k], SB["sh%d" % _k], SB["ql%d" % _k], SB["sl%d" % _k] = (K, Q4), (K, U8), (K, Q4), (K, U8)
 POOLS = {
     "kf": (F32, {"kc": 16, "half": 145, "two": 145, "zer": C, "btab": 290, "ya": 64, "yt": 64, "j16": 16, "nn": 16, "ra": 16, "rb": 16, "rc": 16,
-                 "t2": 16, "tab": 64, "mbig": 64, "rat": 64, "mc": 32, "mge": 32, "m448": 32, "rep": 128, "ca": 16, "cb": 16, "cd": 16, "ce": 16,
-                 "cmul": 512, "csum": 512, "c1024": C, "kk": 28, "k2": 28, "mg": 128, "ia": 128, "ic": 128, "idt": 128, "kio": K}),
+                 "t2": 16, "t3": 16, "tab": 96, "mbig": 64, "rat": 64, "mc": 64, "mge": 32, "m448": 32, "rep": 128, "ca": 16, "cb": 16, "cd": 16,
+                 "ce": 16, "cmul": 512, "csum": 512, "c1024": C, "kk": 28, "k2": 28, "mg": 128, "ia": 128, "ic": 128, "idt": 128, "kio": K, "c3": 42}),
     "ki": (I32, {"pint": 2, "rint": 2, "hint": 1, "o16i": 8}),
-    "wf": (F32, {"sc": 64, "m1": 96, "tr1": 128, "tr2": 128, "tr3": 64, "tr4": 128, "cand": 64, "cand2": 64, "steps": 6, "vs": C, "cap": C,
-                 "vv": C, "cs": C, "x1": 28, "e1": 28, "u1": 28, "o1": 28, "x2": 28, "x3": 28, "g1": 128, "g2": 128, "l1": 128, "cs3": K, "cs4": C}),
-    "wi": (I32, {"xi": 28, "zi": 28, "ai": 28, "ni": 28, "ci": 16, "cj": 16, "pa": K, "pb": K}),
+    "wf": (F32, {"sc": 64, "m1": 96, "m2": 64, "m3": 32, "m4": 96, "tr1": 136, "tr2": 128, "tr3": 64, "tr4": 128, "cand": 64, "cand2": 64, "steps": 6,
+                 "vs": C, "cap": C, "vv": C, "cs": C, "x1": 28, "tri": 84, "x3": 84, "l1": 128, "cs3": K, "cs4": C, "pb": K}),
+    "wi": (I32, {"xi": 28, "zi": 28, "ai": 28, "ni": 28, "g1": 128, "gh": 128, "gl": 128, "pa": K}),
 }
 AT = {}
 for _p, (_d, _m) in POOLS.items():
@@ -171,7 +171,7 @@ def rank_program(g, core, T, topo):
     dma("Y", T.sw[:], T.ws[:], [], [v("sw")])
     dma("Y", T.vin[:], T.v[:], [], [v("vin")])
 
-    RF, RM1, RP1, HM0, HM1, R0, UN0, UNA, UNB, UNC, R2, O15 = [c1("kc", i) for i in range(12)]
+    RF, RM1, RP1, HM0, HM1, R0, UN0, UNA, UNB, UNC, TA, TW, O15 = [c1("kc", i) for i in range(13)]
     G16 = [[-16, 8], [0, 16]]
     ms(v("et"), 0.0)
     iota(v("pint"), [[15, 2]], 0, 1)
@@ -198,16 +198,16 @@ def rank_program(g, core, T, topo):
     tr(v("yt"), v("ya"))
     T1 = c1("yt", 0)
     ts(v("ca"), v("j16"), RF, A.not_equal)
-    ts(v("cb"), v("j16"), RP1, A.is_equal, 4095.0, A.mult)
+    ts(v("cb"), v("j16"), RP1, A.is_equal, 2.0 ** 20, A.mult)
     ts(v("cd"), v("j16"), RM1, A.not_equal)
     ts(v("ce"), v("j16"), RP1, A.is_equal, 2.0 ** 40, A.mult)
     ts(v("rep", 0, 16), v("j16"), RF, A.is_equal)
     ts(UN0, RF, 15.0, A.is_equal)
     ts(v("ra"), v("nn"), 144.5 / 17, A.is_gt, 3.0, A.mult)
     ts(v("rb"), v("nn"), 143.5 / 17, A.is_gt, -1.5, A.mult)
-    tt(v("cmul", 0, 16), v("ca"), v("cb"), A.add)
+    tt(v("cmul", 0, 16), v("ca"), v("cb"), A.max)
     tt(v("csum", 0, 16), v("cd"), v("ce"), A.max)
-    ts(UNB, UN0, 2.0 ** -12, A.max)
+    ts(UNB, UN0, 2.0 ** -20, A.max)
     quant(v("qu0"), v("su0"), v("uin"))
     tt(v("rc"), v("ra"), v("rb"), A.add)
     for w in (16, 32, 64):
@@ -217,22 +217,27 @@ def rank_program(g, core, T, topo):
        [v("qu0"), v("o16")], [v("qu")])
     ts(v("ra"), v("rc"), 0.5, A.add)
     act(v("su"), v("su0"), ACT.Copy, off=v("o16"))
+    ts(TA, T1, -0.5, A.mult, T1, A.max)
     for i in range(4):
         ts(v("mbig", 16 * i, 16 * i + 16), v("zer", 0, 16), (HM0, HM1)[i % 2], A.add)
+    ts(TW, TA, 2.0 ** -72, A.max, 0.125, A.mult)
+    ms(v("rat", 32, 64), 0.0)
+    for i in range(2):
+        ts(v("rat", 16 * i, 16 * i + 16), v("j16"), 1.0, A.add)
     scan(v("t2"), v("ra"), v("zer", 0, 16), T1, A.mult, A.add)
     cp(c1("tr1", 31), c1("yt", 32))
-    ms(c1("tr1", 96), -2.0 ** 71)
+    ts(v("t3"), v("rat", 0, 16), TW, A.mult, T1, A.add)
+    ts(c1("tr1", 128), RP1, 2.0 ** 67, A.mult, -2.0 ** 71, A.add)
+    ms(c1("tr2", 97), -2.0 ** 71)
     ts(v("tab", 32, 64), v("mbig", 0, 32), T1, A.min)
     for i in range(2):
         ts(v("tab", 16 * i, 16 * i + 16), v("t2"), (HM0, HM1)[i], A.min)
+        ts(v("tab", 64 + 16 * i, 80 + 16 * i), v("t3"), (HM0, HM1)[i], A.min)
     act(v("mg"), v("zer", 0, 128), ACT.Identity, bias=UNB)
     for w in (128, 256):
         for n in ("cmul", "csum"):
             act(v(n, w, 2 * w), v(n, 0, w), ACT.Copy)
-    ms(v("rat", 32, 64), 0.0)
-    for i in range(2):
-        ts(v("rat", 16 * i, 16 * i + 16), v("j16"), 1.0, A.add)
-    ts(v("mc"), v("mbig", 0, 32), -64.0, A.min, -1000.0, A.max)
+    ts(v("mc"), v("mbig"), -64.0, A.min, -1000.0, A.max)
     for o in (0, 512):
         sel(v("ct", o, o + 512, 4), v("ct", o, o + 512, 4), G16, A.not_equal, -EPS, -8, 1)
     sel(v("ct", 0, 64, 4), v("ct", 0, 64, 4), [[0, 16]], A.not_equal, 1.0, 0, 1)
@@ -241,6 +246,7 @@ def rank_program(g, core, T, topo):
     for t in range(2):
         sel(v("ct", 1024 + t, 1536, 4), v("rep"), [[16, 8], [0, 16]], A.is_gt, 0.0, 0, -1)
     iota(v("kk"), [[32, 28]], 2050, 0)
+    iota(v("c3"), [[0, 14], [30000, 3]], 0, 0)
     iota(v("ia"), [[0, 8], [16, 16]], 0, 0)
     sel(v("mg"), v("mg"), G16, A.is_ge, 0.0, 0, 1)
     sel(v("mg"), v("mg"), [[16, 8], [0, 16]], A.is_ge, 0.0, 15, -1)
@@ -250,19 +256,25 @@ def rank_program(g, core, T, topo):
         if i == 0:
             for b in range(4):
                 quant(v("qe", 128 * b, 128 * b + 128), v("se", 128 * b, 128 * b + 128), v("et", 3 - b, 515 - b))
-            act(v("c1024"), v("zer"), ACT.Identity, bias=EPS)
+            act(v("c1024"), v("zer"), ACT.Identity, bias=1024.0)
         if i == 1:
             act(v("ctie"), v("zer"), ACT.Copy)
         if i == 2:
             act(v("bt", 0, C), v("zer"), ACT.Copy)
         if i in (3, 4):
             ms(v("mt", 2 * C * (i - 3), 2 * C * (i - 2)), 0.0)
+        if i == 3:
+            ms(c1("ctie", 0), -0.1875)
+            ms(v("bt", C, 512), 0.0)
+        if i == 4:
+            ms(v("dp", 0, 4 * 272, 272), 0.0)
+            ts(v("k2"), v("kk"), RF, A.add, RF, A.add)
         if i == 5:
             ts(R0, RF, 0.0, A.is_equal, 1448.0, A.mult)
             ts(v("mge"), v("mbig", 0, 32), -1.0, A.mult, 256.0, A.max)
             ts(O15, RF, 16.0, A.mult, 15.0, A.add)
             ts(UNC, UN0, 2.0 ** -40, A.max, -1024.0, A.mult)
-            ts(UNA, UN0, 2.0 ** -12, A.max, 1024.0, A.mult)
+            ts(UNA, UN0, 2.0 ** -20, A.max, EPS, A.mult)
             ts(v("m448"), v("mbig", 0, 32), R0, A.min, -1000.0, A.add)
             ts(v("o15"), v("zer", 0, 8), O15, A.add)
         if i == 6:
@@ -270,13 +282,10 @@ def rank_program(g, core, T, topo):
         if i == 7:
             act(v("ic"), v("ia"), ACT.Identity, bias=RF)
             sel(v("idt"), v("ic"), [[16, 8], [0, 16]], A.is_ge, -1.0, 15, -1)
-            ms(c1("ctie", 0), -0.1875)
-            ms(v("bt", C, 512), 0.0)
-            ms(v("dp", 0, 4 * 272, 272), 0.0)
-            ts(v("k2"), v("kk"), RF, A.add, RF, A.add)
 
     S = lambda i: c1("sc", i)
     P0, P1 = v("b0", 0, C), v("b1", 0, C)
+    H = C // 2
 
     def count_at(thr, c):
         act(v("junk"), P0, ACT.Sign, bias=thr, scale=-1.0, acc=c)
@@ -294,23 +303,20 @@ def rank_program(g, core, T, topo):
         for b in range(4):
             mm(v("b%d" % (2 + b), 0, C), v("qe", 128 * b, 128 * b + 128), v("se", 128 * b, 128 * b + 128), v("qx"), v("sx"))
         ts(S(1), S(0), -64.0, A.is_gt, -2 * BIG, A.mult)
-        ts(v("m1", 0, 64), v("tab"), S(1), A.add)
-        tr(v("tr1", 32, 96), v("m1", 0, 64))
+        ts(v("m1"), v("tab"), S(1), A.add)
+        tr(v("tr1", 32, 128), v("m1"))
         red(S(2), v("tr1", 31, 64), A.max)
         count_at(S(2), S(3))
         if k == 0:
             constants(1)
-        red(c1("tr2", 96), v("tr1", 64, 97), A.max)
+        red(c1("tr2", 96), v("tr1", 64, 96), A.max)
         ts(S(4), S(2), -0.5, A.mult, S(2), A.max)
-        ts(S(6), c1("tr2", 96), -0.5, A.mult, c1("tr2", 96), A.max)
+        red(c1("tr2", 31), v("tr1", 96, 129), A.max)
         ts(S(5), S(4), 2.0 ** -72, A.max, 0.125, A.mult)
-        ts(S(7), S(6), 2.0 ** -72, A.max, 0.125, A.mult)
         ts(v("cand"), v("rat"), S(5), A.mult, S(2), A.add)
-        ts(c1("tr2", 31), RP1, S(7), A.mult, c1("tr2", 96), A.add)
-        tt(v("cand2"), v("cand"), v("mbig"), A.min)
-        ts(S(8), S(3), -64.0, A.is_gt, -2 * BIG, A.mult)
-        ts(v("m1", 0, 64), v("cand2"), S(8), A.add)
-        tr(v("tr2", 32, 96), v("m1", 0, 64))
+        ts(v("cand2"), v("mc"), S(3), A.is_lt, -2 * BIG, A.mult)
+        tt(v("m2"), v("cand"), v("cand2"), A.add)
+        tr(v("tr2", 32, 96), v("m2"))
         red(S(20), v("tr2", 31, 64), A.max)
         RW = S(12)
         for i in range(5):
@@ -319,11 +325,10 @@ def rank_program(g, core, T, topo):
             if i == 0:
                 if k == 0:
                     constants(2)
-                red(S(9), v("tr2", 64, 97), A.max)
+                red(S(9), v("tr2", 64, 98), A.max)
                 ts(S(10), S(9), -0.5, A.mult, S(9), A.max)
-                ts(S(11), S(10), 2.0 ** -72, A.max, 0.125, A.mult)
-                ts(RW, RP1, S(11), A.mult)
-                ts(v("steps"), v("btab", 198, 219, 4), S(11), A.mult)
+                ts(RW, thr, S(9), A.subtract)
+                ts(c1("steps", 5), S(10), 2.0 ** -72, A.max, 0.125, A.mult)
                 ts(c1("tr3", 32), RW, 1.0 / 16, A.mult, S(9), A.add)
             else:
                 ts(c1("tr3", 32), RW, -15.0 / 16 * 16.0 ** -i, A.mult, thr, A.add)
@@ -332,72 +337,105 @@ def rank_program(g, core, T, topo):
                     constants(i + 2)
                 else:
                     cp(v("ff", C * (i - 1), C * i), v("b%d" % (1 + i), 0, C))
-            ts(v("m1", 0, 32), v("mc"), cnt, A.is_ge, c1("steps", 5 - i), A.mult)
-            tr(v("tr3", 0, 32), v("m1", 0, 32))
+            ts(v("m3"), v("mc", 0, 32), cnt, A.is_ge, c1("steps", 5 - i), A.mult)
+            if i == 0:
+                ts(v("steps", 0, 5), v("btab", 198, 215, 4), c1("steps", 5), A.mult)
+            tr(v("tr3", 0, 32), v("m3"))
             red(S(21 + i), v("tr3", 0, 33), A.add)
         thr, cnt, cge, TH, NEED = S(25), S(35), S(36), S(38), S(39)
         count_at(thr, cnt)
         ts(v("ge"), P1, thr, A.is_ge)
         ts(c1("tr4", 31), RW, -16.0 ** -5, A.mult, thr, A.add)
         red(cge, v("ge"), A.add)
+        ts(v("m4", 0, 32), v("mge"), cge, A.is_le, c1("steps", 0), A.mult)
         ts(S(37), cge, cnt, A.add, EPS, A.mult)
-        ts(v("m1", 0, 32), v("mge"), cge, A.is_le, c1("steps", 0), A.mult)
-        ts(v("m1", 64, 96), v("m448"), cge, A.subtract, EPS, A.mult)
-        ts(v("m1", 32, 64), v("mge"), cge, A.is_le, S(37), A.mult)
-        tr(v("tr4", 32, 128), v("m1"))
+        ts(v("m4", 64, 96), v("m448"), cge, A.subtract, EPS, A.mult)
+        tr(v("tr4", 32, 64), v("m4", 0, 32))
+        ts(v("m4", 32, 64), v("mge"), cge, A.is_le, S(37), A.mult)
         red(TH, v("tr4", 31, 64), A.add)
-        red(NEED, v("tr4", 64, 128), A.max)
+        tr(v("tr4", 64, 128), v("m4", 32, 96))
         act(v("sig"), P0, ACT.Sign, bias=TH, scale=-1.0)
-        ts(v("neq"), P1, TH, A.is_equal, -EPS, A.mult)
+        ts(v("neq", 0, H), v("b1", 0, H), TH, A.is_equal, -EPS, A.mult)
+        red(NEED, v("tr4", 64, 128), A.max)
+        ts(v("neq", H, C), v("b1", H, C), TH, A.is_equal, -EPS, A.mult)
         if k == 0:
             constants(7)
         scan(v("ns"), v("neq"), v("ctie"), NEED, A.add, A.add)
-        M0 = v("mt", 0, 4 * C, 4)
-        tt(M0, v("sig"), v("ns"), A.is_le)
-        quant(v("qm"), v("sm"), v("mt"))
-        mm(v("b6", 0, C), v("qc", 0, 128), v("scc", 0, 128), v("qm"), v("sm"))
-        mm(v("b7", 0, C), v("qc", 128, 256), v("scc", 128, 256), v("qm"), v("sm"))
-        scan(v("vs"), M0, v("c1024"), -225.0 * EPS, A.add, A.add)
-        scan(v("cap"), v("b6", 0, C), v("zer"), OFF, A.add, A.add)
-        scan(v("vv"), v("b7", 0, C), v("cap"), OFF, A.add, A.min)
+        M0 = [v("mt", 4 * H * h, 4 * H * (h + 1), 4) for h in range(2)]
+        hv = lambda n, h: v(n, H * h, H * (h + 1))
+        for h in range(2):
+            tt(M0[h], hv("sig", h), hv("ns", h), A.is_le)
+        for h in range(2):
+            quant(hv("qm", h), hv("sm", h), v("mt", 4 * H * h, 4 * H * (h + 1)))
+            mm(v("b%d" % (6, 2)[h], 0, H), v("qc", 0, 128), v("scc", 0, 128), hv("qm", h), hv("sm", h))
+            mm(v("b%d" % (7, 3)[h], 0, H), v("qc", 128, 256), v("scc", 128, 256), hv("qm", h), hv("sm", h))
         MC, NM = S(40), S(41)
-        scan(v("cs"), v("csum", 0, C), v("vv"), OFF, A.mult, A.add)
-        act(MC, c1("vv", C - 1), ACT.Identity, bias=0.5 - 2 * OFF - 1538.0, scale=2.0)
+
+        def decode(h, step):
+            w = lambda n: v(n, 14 * h, 14 * h + 14)
+            t3 = lambda n, j: v(n, 42 * h + j, 42 * h + 42, 3)
+            if step == 0:
+                tt(w("x1"), v("cs", H * h + 14, H * h + H, 16), v("cs", H * h + 15, H * h + H, 16), A.max)
+            if step == 1:
+                ts(w("xi"), w("x1"), UNC, A.mult, 1024.0 * (2 * OFF + 513) + 1, A.add)
+            if step == 2:
+                ts(w("ai"), w("xi"), 10, A.logical_shift_right, 1022, A.bitwise_and)
+                ts(w("ni"), w("xi"), 1, A.bitwise_and)
+                ts(w("zi"), w("xi"), 2047, A.bitwise_and)
+            if step == 3:
+                tt(t3("tri", 2), w("zi"), w("ai"), A.add)
+                tt(t3("tri", 1), w("ni"), w("k2"), A.mult)
+                ts(t3("tri", 0), w("ai"), -1.0, A.mult, NM, A.add)
+            if step == 4:
+                scan(v("x3", 42 * h, 42 * h + 42), v("c3"), v("tri", 42 * h, 42 * h + 42), 0.0, A.min, A.max)
+            if step == 5:
+                ts(v("pos", 16 * h, 16 * h + 14), t3("x3", 2), MC, A.add, 0.5, A.mult)
+            if step == 6:
+                scat(v("t0"), v("pos", 16 * h, 16 * h + 14), hv("vs", h))
+
+        scan(hv("vs", 0), M0[0], hv("c1024", 0), -1024.0, A.add, A.add)
+        scan(hv("cap", 0), v("b6", 0, H), hv("zer", 0), OFF, A.add, A.add)
+        scan(hv("vs", 1), M0[1], hv("c1024", 1), c1("vs", H - 1), A.add, A.add)
+        scan(hv("vv", 0), v("b7", 0, H), hv("cap", 0), OFF, A.add, A.min)
+        scan(hv("cap", 1), v("b2", 0, H), hv("zer", 1), c1("cap", H - 1), A.add, A.add)
+        scan(hv("cs", 0), hv("csum", 0), hv("vv", 0), OFF, A.mult, A.add)
+        scan(hv("vv", 1), v("b3", 0, H), hv("cap", 1), c1("vv", H - 1), A.add, A.min)
         act(NM, c1("vv", C - 1), ACT.Identity, bias=2 * OFF + 2049.5, scale=-2.0)
-        tt(v("x1"), v("cs", 14, C, 16), v("cs", 15, C, 16), A.max)
-        ts(v("xi"), v("x1"), UNC, A.mult, 1024.0 * (2 * OFF + 513) + 1, A.add)
-        ts(v("ai"), v("xi"), 10, A.logical_shift_right, 1022, A.bitwise_and)
-        ts(v("ni"), v("xi"), 1, A.bitwise_and)
-        ts(v("zi"), v("xi"), 2047, A.bitwise_and)
-        ts(v("u1"), v("ai"), -1.0, A.mult, NM, A.add)
-        tt(v("o1"), v("ni"), v("k2"), A.mult)
-        tt(v("e1"), v("zi"), v("ai"), A.add)
-        tt(v("x2"), v("u1"), v("o1"), A.max)
-        tt(v("x3"), v("x2"), v("e1"), A.max)
-        ts(v("pos"), v("x3"), MC, A.add, 0.5, A.mult)
-        scat(v("t0"), v("pos"), v("vs"))
+        act(MC, c1("vv", C - 1), ACT.Identity, bias=0.5 - 2 * OFF - 1538.0, scale=2.0)
+        decode(0, 0)
+        scan(hv("cs", 1), hv("csum", 1), hv("vv", 1), c1("vv", H - 1), A.mult, A.add)
+        for step in range(1, 7):
+            decode(0, step)
+            decode(1, step - 1)
+        decode(1, 6)
         scan(v("cs2"), v("cmul", 0, K), v("t0", 0, K), 0.0, A.mult, A.max)
-        tt(v("g1", 16, 112), v("cs2"), v("mg", 16, 112), A.mult, off=v("o15", 0, 6))
-        HI, LO = v("bt", 64, 448, 4), v("bt", 65, 448, 4)
-        ts(HI, v("g1", 16, 112), 1.5 * 2.0 ** 27, A.add, -1.5 * 2.0 ** 27, A.add)
-        ts(v("g2", 16, 112), v("g1", 16, 112), 1.5 * 2.0 ** 23, A.add, -1.5 * 2.0 ** 23, A.add)
-        tt(LO, v("g2", 16, 112), HI, A.subtract)
+        part = ((64, 112), (16, 64))
+        for a, b in part:
+            tt(v("g1", a, b), v("cs2"), v("mg", a, b), A.mult, off=v("o15", 0, 3))
+        for a, b in part:
+            ts(v("gh", a, b), v("g1", a, b), 496, A.bitwise_and)
+            ts(v("gl", a, b), v("g1", a, b), 15, A.bitwise_and)
+        for a, b in part:
+            cp(v("bt", 4 * a, 4 * b, 4), v("gh", a, b))
+            cp(v("bt", 4 * a + 1, 4 * b, 4), v("gl", a, b))
         quant(v("qb"), v("sb"), v("bt"))
         mm(v("b6", 0, 128), v("qc", 256, 384), v("scc", 256, 384), v("qb"), v("sb"))
         if k == 0:
             ms(v("thf"), 1.0)
-        tt(v("l1", 16, 112), v("b6", 16, 112), v("idt", 16, 112), A.add)
-        cp(v("loff", 16, 112), v("l1", 16, 112))
+        for a, b in part:
+            tt(v("l1", a, b), v("b6", a, b), v("idt", a, b), A.add)
+        for a, b in part:
+            cp(v("loff", a, b), v("l1", a, b))
         src = "t0"
         for h in range(6, 0, -1):
             dst = "ta" if h % 2 == 0 else "tb"
             cp(v(dst, 0, 128), v(src, 0, K), off=v("loff", 16 * h, 16 * h + 8))
             act(v(dst, 128, K), v(src, 0, K), ACT.Copy, off=v("loff", 16 * h + 8, 16 * h + 16))
             src = dst
-        scan(v("cs3"), v("cmul", 0, K), v(src), 0.0, A.mult, A.max)
-        ts(v("ci"), v("cs3", 15, K, 16), UNA, A.mult, 224.0, A.add)
-        ts(v("cj"), v("ci"), 1023, A.bitwise_and)
-        cp(v("offc"), v("cj"))
+        for h in range(2):
+            scan(v("cs3", 128 * h, 128 * h + 128), v("cmul", 0, 128), v(src, 128 * h, 128 * h + 128), 0.0, A.mult, A.max)
+        for h in range(2):
+            ts(v("offc", 8 * h, 8 * h + 8), v("cs3", 128 * h + 15, 128 * h + 128, 16), UNA, A.mult)
         qh, sh, ql, sl, arr = "qh%d" % k, "sh%d" % k, "ql%d" % k, "sl%d" % k, "arr%d" % k
         rid, pid, _ = topo.addr(partner)
         mask, ne = topo.mask(core, partner), len(topo.engines(core, partner))
@@ -407,18 +445,20 @@ def rank_program(g, core, T, topo):
             for b in range(2):
                 act(v("zt", 4 * lo + 2 + b, 4 * hi, 4), v("ff", C * (2 + b), C * (3 + b)), ACT.Copy, off=off)
                 cp(v("zt", 4 * lo + b, 4 * hi, 4), v("ff", C * b, C * (b + 1)), off=off)
-            quant(v("qz", lo, hi), v("sz", lo, hi), v("zt", 4 * lo, 4 * hi))
-            if h == 0:
-                for b in (0, 2, 1, 3):
-                    mm(v("b%d" % banks[0][b], 0, 128), v("qw", 128 * b, 128 * b + 128), v("sw", 128 * b, 128 * b + 128), v("qz", lo, hi), v("sz", lo, hi))
+                if h == 1 and b == 0:
+                    quant(v("qz", 0, 128), v("sz", 0, 128), v("zt", 0, 512))
+                    for b2 in (0, 2, 1, 3):
+                        mm(v("b%d" % banks[0][b2], 0, 128), v("qw", 128 * b2, 128 * b2 + 128), v("sw", 128 * b2, 128 * b2 + 128), v("qz", 0, 128), v("sz", 0, 128))
+        quant(v("qz", 128, K), v("sz", 128, K), v("zt", 512, 4 * K))
+        ts(v("ht", 0, 512, 4), v("b0", 0, 128), 0.0, A.max, 0.015625, A.mult)
+        for b2 in (1, 3, 2, 0):
+            mm(v("b%d" % banks[1][b2], 0, 128), v("qw", 128 * b2, 128 * b2 + 128), v("sw", 128 * b2, 128 * b2 + 128), v("qz", 128, K), v("sz", 128, K))
+        ts(v("ht", 1, 512, 4), v("b1", 0, 128), 0.0, A.max, 0.015625, A.mult)
+        for h, b in ((0, 2), (0, 3), (1, 3), (1, 2)):
+            act(v("ht", 512 * h + b, 512 * h + 512, 4), v("b%d" % banks[h][b], 0, 128), ACT.Relu, scale=0.015625)
         for h in range(2):
             lo, hi = 128 * h, 128 * h + 128
-            for b in ((0, 1), (1, 0))[h]:
-                ts(v("ht", 4 * lo + b, 4 * hi, 4), v("b%d" % banks[h][b], 0, 128), 0.0, A.max, 0.015625, A.mult)
-                act(v("ht", 4 * lo + 2 + b, 4 * hi, 4), v("b%d" % banks[h][2 + b], 0, 128), ACT.Relu, scale=0.015625)
-                if h == 0 and b == 0:
-                    for b2 in (3, 1, 2, 0):
-                        mm(v("b%d" % banks[1][b2], 0, 128), v("qw", 128 * b2, 128 * b2 + 128), v("sw", 128 * b2, 128 * b2 + 128), v("qz", 128, K), v("sz", 128, K))
+            ts(v("ht", 513 - h, 4 * K, 4), v("b%d" % banks[1][1 - h], 0, 128), 0.0, A.max, 0.015625, A.mult)
             quant(v(qh, lo, hi), v(sh, lo, hi), v("ht", 4 * lo, 4 * hi))
             wait("G", "sV", count["sV"])
             g.remote_dma(T[ql][:, lo:hi].bitcast(dt.uint8), T[qh][:, lo:hi].bitcast(dt.uint8), T.sem[arr], T.sem.snd, pid, rid, mask)
@@ -429,9 +469,9 @@ def rank_program(g, core, T, topo):
         if k == 0:
             quant(v("qv"), v("sv"), v("vin"))
         if k == 2:
-            ts(v("pa"), v(src), 1024.0, A.mult, 224.0, A.add)
-            ts(v("pb"), v("pa"), 1023, A.bitwise_and)
-            cp(v("pf"), v("pb"))
+            ts(v("pb"), v(src), EPS, A.mult)
+            cp(v("pa"), v("pb"))
+            cp(v("pf"), v("pa"))
             dma("Y", T.pl[:], T.pf[0:128:16, :], [v("pf")], [])
         wait("P", arr, 3 * ne)
         for b in range(4):
@@ -445,10 +485,10 @@ def rank_program(g, core, T, topo):
 
     quant(v("qx"), v("sx"), v("xt"))
     for h in range(2):
-        mm(v("b%d" % h, 0, C // 2), v("qv"), v("sv"), v("qx", h * C // 2, (h + 1) * C // 2), v("sx", h * C // 2, (h + 1) * C // 2))
+        mm(v("b%d" % h, 0, H), v("qv"), v("sv"), v("qx", h * H, (h + 1) * H), v("sx", h * H, (h + 1) * H))
     dma("Y", T.oc[:], T.qx[:].bitcast(dt.uint8), [v("qx")], [])
-    cp(v("yo", 0, C // 2), v("b0", 0, C // 2))
-    act(v("yo", C // 2, C), v("b1", 0, C // 2), ACT.Copy)
+    cp(v("yo", 0, H), v("b0", 0, H))
+    act(v("yo", H, C), v("b1", 0, H), ACT.Copy)
     dma("Y", T.y[:], T.yo[:], [v("yo")], [])
     for i in range(4):
         dma("S", T.osc[4 * i:4 * i + 4, :], T.sx[32 * i:32 * i + 4, :], [v("sx")], [])

@@ -5,11 +5,11 @@ F32, BF, I32, U16, Q4, U8 = "float32", "bfloat16", "int32", "uint16", "float8_e4
 SB = {
     "xin": (4 * C, BF), "uin": (512, BF), "vin": (512, BF), "qu0": (128, Q4), "su0": (128, U8), "qu": (128, Q4), "su": (128, U8),
     "qv": (128, Q4), "sv": (128, U8), "qw": (512, Q4), "sw": (512, U8),
-    "o16": (8, U16), "o15": (8, U16), "et": (516, BF), "qe": (512, Q4), "se": (512, U8),
-    "ct": (1536, BF), "qc": (384, Q4), "scc": (384, U8), "ctie": (C, BF),
+    "o16": (8, U16), "et": (516, BF), "qe": (512, Q4), "se": (512, U8),
+    "ct": (1920, BF), "qc": (480, Q4), "scc": (480, U8), "zb": (C, BF),
     "xt": (4 * C, BF), "qx": (C, Q4), "sx": (C, U8), "ff": (4 * C, BF),
-    "junk": (C, BF), "ge": (C, BF), "sig": (C, BF), "neq": (C, BF), "ns": (C, BF),
-    "mt": (4 * C, BF), "qm": (C, Q4), "sm": (C, U8), "pos": (32, U16), "t0": (960, F32), "ta": (K, F32), "tb": (K, F32), "cs2": (K, F32),
+    "junk": (C, BF), "ge": (C, BF), "gs": (C, BF), "hb": (8, BF), "sig": (C, BF), "neq": (C, BF), "ns": (C, BF),
+    "mt": (4 * C, BF), "qm": (C, Q4), "sm": (C, U8), "pos": (32, U16), "t0": (960, F32), "ta": (K, F32), "tb": (K, F32),
     "bt": (512, BF), "qb": (128, Q4), "sb": (128, U8), "loff": (128, U16), "offc": (16, U16), "thf": (C, F32), "offt": (28, U16), "pf": (K, F32),
     "zt": (4 * K, BF), "qz": (K, Q4), "sz": (K, U8), "ht": (4 * K, BF), "dp": (4 * 272, BF), "d3": (C, BF), "yo": (C, F32),
 }
@@ -17,12 +17,12 @@ for _k in range(3):
     SB["qh%d" % _k], SB["sh%d" % _k], SB["ql%d" % _k], SB["sl%d" % _k] = (K, Q4), (K, U8), (K, Q4), (K, U8)
 POOLS = {
     "kf": (F32, {"kc": 16, "half": 145, "two": 145, "zer": C, "btab": 290, "ya": 64, "yt": 64, "j16": 16, "nn": 16, "ra": 16, "rb": 16, "rc": 16,
-                 "t2": 16, "t3": 16, "tab": 96, "mbig": 64, "rat": 64, "mc": 64, "mge": 32, "m448": 32, "rep": 128, "ca": 16, "cb": 16, "cd": 16,
-                 "ce": 16, "cmul": 512, "csum": 512, "c1024": C, "kk": 28, "k2": 28, "mg": 128, "ia": 128, "ic": 128, "idt": 128, "kio": K, "c3": 42}),
+                 "t2": 16, "t3": 16, "tab": 96, "mbig": 64, "rat": 64, "mc": 64, "ml": 32, "m0": 32, "ca": 16, "cb": 16, "cd": 16,
+                 "ce": 16, "cmul": 512, "csum": 512, "c1024": C, "kk": 28, "k2": 28, "kio": K, "c3": 42}),
     "ki": (I32, {"pint": 2, "rint": 2, "hint": 1, "o16i": 8}),
-    "wf": (F32, {"sc": 64, "m1": 96, "m2": 64, "m3": 32, "m4": 96, "tr1": 136, "tr2": 128, "tr3": 64, "tr4": 128, "cand": 64, "cand2": 64, "steps": 6,
-                 "vs": C, "cap": C, "vv": C, "cs": C, "x1": 28, "tri": 84, "x3": 84, "l1": 128, "cs3": K, "cs4": C, "pb": K}),
-    "wi": (I32, {"xi": 28, "zi": 28, "ai": 28, "ni": 28, "g1": 128, "gh": 128, "gl": 128, "pa": K}),
+    "wf": (F32, {"sc": 64, "m1": 96, "m2": 64, "m3": 32, "m4": 96, "mlc": 32, "m0c": 32, "tr1": 136, "tr2": 128, "tr3": 64, "tr4": 128, "cand": 64,
+                 "cand2": 64, "steps": 6, "vs": C, "cap": C, "vv": C, "cs": C, "x1": 28, "tri": 84, "x3": 84, "cs2": K, "cs3": K, "cs4": C, "pb": K}),
+    "wi": (I32, {"xi": 28, "zi": 28, "ai": 28, "ni": 28, "g1": 16, "gh": 16, "gl": 16}),
 }
 AT = {}
 for _p, (_d, _m) in POOLS.items():
@@ -39,6 +39,7 @@ SEMAPHORES = ["sV", "sS", "sP", "sG", "snd", "arr0", "arr1", "arr2"] + ["d%d" % 
 BIG = 2.0 ** 80
 EPS = 2.0 ** -10
 OFF = 1024.0
+RUNS = ((0, 320), (320, C))
 
 
 def rank_program(g, core, T, topo):
@@ -165,23 +166,27 @@ def rank_program(g, core, T, topo):
     def dma(e, o, i, reads, writes):
         op(e, lambda: Q[e].dma_start(o, i), reads, writes, dma=True)
 
+    H = C // 2
+    hv = lambda n, h: v(n, H * h, H * (h + 1))
     dma("S", T.uin[:], T.u[:], [], [v("uin")])
-    dma("Y", T.xin[:], T.x[:], [], [v("xin")])
+    for a, b in RUNS:
+        dma("Y", T.xin[:, 4 * a:4 * b], T.x[:, 4 * a:4 * b], [], [v("xin", 4 * a, 4 * b)])
     dma("Y", T.qw[:].bitcast(dt.uint8), T.wc[:], [v("xin")], [v("qw")])
     dma("Y", T.sw[:], T.ws[:], [], [v("sw")])
     dma("Y", T.vin[:], T.v[:], [], [v("vin")])
 
-    RF, RM1, RP1, HM0, HM1, R0, UN0, UNA, UNB, UNC, TA, TW, O15 = [c1("kc", i) for i in range(13)]
+    RF, RM1, RP1, HM0, HM1, R0, UN0, UNA, UNB, UNC, TA, TW = [c1("kc", i) for i in range(12)]
     G16 = [[-16, 8], [0, 16]]
-    ms(v("et"), 0.0)
     iota(v("pint"), [[15, 2]], 0, 1)
     iota(v("o16i"), [[16, 8]], 0, 0)
     iota(v("j16"), [[1, 16]], 0, 0)
-    sel(v("et"), v("et"), [[1, 516]], A.not_equal, 1.0, -3, -4)
-    iota(v("ct"), [[0, 1536]], 0, 0)
     ms(v("half"), 0.5)
     ms(v("two"), 2.0)
-    ms(v("zer"), 0.0)
+    ms(v("zer", 0, 152), 0.0)
+    ms(v("et"), 0.0)
+    sel(v("et"), v("et"), [[1, 516]], A.not_equal, 1.0, -3, -4)
+    iota(v("zer", 152, C), [[0, C - 152]], 0, 0)
+    iota(v("ct"), [[0, 1920]], 0, 0)
     scan(v("btab", 0, 145), v("half"), v("zer", 0, 145), -2.0 ** 72, A.mult, A.add)
     scan(v("btab", 145, 290), v("two"), v("zer", 0, 145), 2.0 ** -74, A.mult, A.add)
     ts(v("rint"), v("pint"), 15, A.bitwise_and)
@@ -201,110 +206,121 @@ def rank_program(g, core, T, topo):
     ts(v("cb"), v("j16"), RP1, A.is_equal, 2.0 ** 20, A.mult)
     ts(v("cd"), v("j16"), RM1, A.not_equal)
     ts(v("ce"), v("j16"), RP1, A.is_equal, 2.0 ** 40, A.mult)
-    ts(v("rep", 0, 16), v("j16"), RF, A.is_equal)
-    ts(UN0, RF, 15.0, A.is_equal)
     ts(v("ra"), v("nn"), 144.5 / 17, A.is_gt, 3.0, A.mult)
     ts(v("rb"), v("nn"), 143.5 / 17, A.is_gt, -1.5, A.mult)
     tt(v("cmul", 0, 16), v("ca"), v("cb"), A.max)
     tt(v("csum", 0, 16), v("cd"), v("ce"), A.max)
-    ts(UNB, UN0, 2.0 ** -20, A.max)
-    quant(v("qu0"), v("su0"), v("uin"))
     tt(v("rc"), v("ra"), v("rb"), A.add)
-    for w in (16, 32, 64):
-        for n in ("rep", "cmul", "csum"):
-            act(v(n, w, 2 * w), v(n, 0, w), ACT.Copy)
-    op("V", lambda: g.vector.tensor_copy(T.qu[:, 0:128].bitcast(dt.uint32), T.qu0[:, 0:128].bitcast(dt.uint32).indirect(T.o16[:, 0:8])),
-       [v("qu0"), v("o16")], [v("qu")])
-    ts(v("ra"), v("rc"), 0.5, A.add)
-    act(v("su"), v("su0"), ACT.Copy, off=v("o16"))
     ts(TA, T1, -0.5, A.mult, T1, A.max)
     for i in range(4):
         ts(v("mbig", 16 * i, 16 * i + 16), v("zer", 0, 16), (HM0, HM1)[i % 2], A.add)
+    ts(v("ra"), v("rc"), 0.5, A.add)
     ts(TW, TA, 2.0 ** -72, A.max, 0.125, A.mult)
     ms(v("rat", 32, 64), 0.0)
     for i in range(2):
         ts(v("rat", 16 * i, 16 * i + 16), v("j16"), 1.0, A.add)
-    scan(v("t2"), v("ra"), v("zer", 0, 16), T1, A.mult, A.add)
-    cp(c1("tr1", 31), c1("yt", 32))
-    ts(v("t3"), v("rat", 0, 16), TW, A.mult, T1, A.add)
-    ts(c1("tr1", 128), RP1, 2.0 ** 67, A.mult, -2.0 ** 71, A.add)
-    ms(c1("tr2", 97), -2.0 ** 71)
-    ts(v("tab", 32, 64), v("mbig", 0, 32), T1, A.min)
-    for i in range(2):
-        ts(v("tab", 16 * i, 16 * i + 16), v("t2"), (HM0, HM1)[i], A.min)
-        ts(v("tab", 64 + 16 * i, 80 + 16 * i), v("t3"), (HM0, HM1)[i], A.min)
-    act(v("mg"), v("zer", 0, 128), ACT.Identity, bias=UNB)
-    for w in (128, 256):
+    quant(v("qu0"), v("su0"), v("uin"))
+    for w in (16, 32, 64):
         for n in ("cmul", "csum"):
             act(v(n, w, 2 * w), v(n, 0, w), ACT.Copy)
-    ts(v("mc"), v("mbig"), -64.0, A.min, -1000.0, A.max)
+    scan(v("t2"), v("ra"), v("zer", 0, 16), T1, A.mult, A.add)
+    cp(c1("tr1", 31), c1("yt", 32))
+    op("V", lambda: g.vector.tensor_copy(T.qu[:, 0:128].bitcast(dt.uint32), T.qu0[:, 0:128].bitcast(dt.uint32).indirect(T.o16[:, 0:8])),
+       [v("qu0"), v("o16")], [v("qu")])
+    act(v("su"), v("su0"), ACT.Copy, off=v("o16"))
+    for n in ("cmul", "csum"):
+        act(v(n, 128, 256), v(n, 0, 128), ACT.Copy)
     for o in (0, 512):
         sel(v("ct", o, o + 512, 4), v("ct", o, o + 512, 4), G16, A.not_equal, -EPS, -8, 1)
     sel(v("ct", 0, 64, 4), v("ct", 0, 64, 4), [[0, 16]], A.not_equal, 1.0, 0, 1)
     sel(v("ct", 64, 512, 4), v("ct", 64, 512, 4), [[-16, 7], [0, 16]], A.not_equal, 1.0, 0, 1)
     sel(v("ct", 512, 1024, 4), v("ct", 512, 1024, 4), G16, A.not_equal, 1.0, 0, 1)
     for t in range(2):
-        sel(v("ct", 1024 + t, 1536, 4), v("rep"), [[16, 8], [0, 16]], A.is_gt, 0.0, 0, -1)
+        sel(v("ct", 1024 + t, 1408, 4), v("ct", 1024 + t, 1408, 4), [[0, 6], [-1, 16]], A.not_equal, 1.0, 0, 1)
+        sel(v("ct", 1408 + t, 1920, 4), v("ct", 1408 + t, 1920, 4), [[-1, 128]], A.not_equal, 1.0, 0, 1)
     iota(v("kk"), [[32, 28]], 2050, 0)
     iota(v("c3"), [[0, 14], [30000, 3]], 0, 0)
-    iota(v("ia"), [[0, 8], [16, 16]], 0, 0)
-    sel(v("mg"), v("mg"), G16, A.is_ge, 0.0, 0, 1)
-    sel(v("mg"), v("mg"), [[16, 8], [0, 16]], A.is_ge, 0.0, 15, -1)
     iota(v("kio"), [[1, K]], 2, 0)
 
     def constants(i):
+        if i == -1:
+            ts(v("t3"), v("rat", 0, 16), TW, A.mult, T1, A.add)
+            ts(c1("tr1", 128), RP1, 2.0 ** 67, A.mult, -2.0 ** 71, A.add)
+            ms(c1("tr2", 97), -2.0 ** 71)
+            ts(v("tab", 32, 64), v("mbig", 0, 32), T1, A.min)
+            for j in range(2):
+                ts(v("tab", 16 * j, 16 * j + 16), v("t2"), (HM0, HM1)[j], A.min)
+                ts(v("tab", 64 + 16 * j, 80 + 16 * j), v("t3"), (HM0, HM1)[j], A.min)
+            ts(v("mc"), v("mbig"), -64.0, A.min, -1000.0, A.max)
         if i == 0:
-            for b in range(4):
+            for b in range(2):
                 quant(v("qe", 128 * b, 128 * b + 128), v("se", 128 * b, 128 * b + 128), v("et", 3 - b, 515 - b))
             act(v("c1024"), v("zer"), ACT.Identity, bias=1024.0)
         if i == 1:
-            act(v("ctie"), v("zer"), ACT.Copy)
+            act(v("zb"), v("zer"), ACT.Copy)
         if i == 2:
             act(v("bt", 0, C), v("zer"), ACT.Copy)
         if i in (3, 4):
             ms(v("mt", 2 * C * (i - 3), 2 * C * (i - 2)), 0.0)
         if i == 3:
-            ms(c1("ctie", 0), -0.1875)
             ms(v("bt", C, 512), 0.0)
         if i == 4:
             ms(v("dp", 0, 4 * 272, 272), 0.0)
-            ts(v("k2"), v("kk"), RF, A.add, RF, A.add)
+            ts(UN0, RF, 15.0, A.is_equal)
         if i == 5:
-            ts(R0, RF, 0.0, A.is_equal, 1448.0, A.mult)
-            ts(v("mge"), v("mbig", 0, 32), -1.0, A.mult, 256.0, A.max)
-            ts(O15, RF, 16.0, A.mult, 15.0, A.add)
+            ts(R0, RF, 0.5, A.is_gt, -2 * BIG, A.mult)
+            ts(v("ml"), v("mbig", 0, 32), 192.0, A.min, -1000.0, A.max)
+            ts(UNB, UN0, 2.0 ** -20, A.max)
             ts(UNC, UN0, 2.0 ** -40, A.max, -1024.0, A.mult)
             ts(UNA, UN0, 2.0 ** -20, A.max, EPS, A.mult)
-            ts(v("m448"), v("mbig", 0, 32), R0, A.min, -1000.0, A.add)
-            ts(v("o15"), v("zer", 0, 8), O15, A.add)
+            ts(v("m0"), v("mbig", 0, 32), R0, A.add)
+            ts(v("k2"), v("kk"), RF, A.add, RF, A.add)
         if i == 6:
             quant(v("qc"), v("scc"), v("ct"))
         if i == 7:
-            act(v("ic"), v("ia"), ACT.Identity, bias=RF)
-            sel(v("idt"), v("ic"), [[16, 8], [0, 16]], A.is_ge, -1.0, 15, -1)
+            for n in ("csum", "cmul"):
+                act(v(n, 256, C), v(n, 0, C - 256), ACT.Copy)
 
     S = lambda i: c1("sc", i)
     P0, P1 = v("b0", 0, C), v("b1", 0, C)
-    H = C // 2
 
     def count_at(thr, c):
         act(v("junk"), P0, ACT.Sign, bias=thr, scale=-1.0, acc=c)
 
+    def new_run(k, h):
+        a, b = RUNS[h]
+        quant(v("qx", a, b), v("sx", a, b), v("xin" if k == 0 else "xt", 4 * a, 4 * b))
+        bank = v("b%d" % (4, 2)[h], 0, b - a)
+        if k < 3:
+            mm(bank, v("qu"), v("su"), v("qx", a, b), v("sx", a, b))
+            act(v("junk", a, b), bank, ACT.Sign, bias=T1, scale=-1.0, acc=S(42 + h))
+        else:
+            mm(bank, v("qv"), v("sv"), v("qx", a, b), v("sx", a, b))
+            dma("Y", T.oc[:, 4 * a:4 * b], T.qx[:, a:b].bitcast(dt.uint8), [v("qx", a, b)], [])
+            if h == 1:
+                for i in range(4):
+                    dma("YS"[i % 2], T.osc[4 * i:4 * i + 4, :], T.sx[32 * i:32 * i + 4, :], [v("sx")], [])
+                cp(v("yo", a, b), bank)
+            else:
+                act(v("yo", a, b), bank, ACT.Copy)
+            dma("SY"[h], T.y[:, a:b], T.yo[:, a:b], [v("yo", a, b)], [])
+
+    for b in range(2, 4):
+        quant(v("qe", 128 * b, 128 * b + 128), v("se", 128 * b, 128 * b + 128), v("et", 3 - b, 515 - b))
+    new_run(0, 0)
+    constants(-1)
+    new_run(0, 1)
+    constants(0)
     for k, e in enumerate(ROUNDS):
         partner = T.cores[rank ^ e]
-        quant(v("qx"), v("sx"), v("xin" if k == 0 else "xt"))
         mm(P0, v("qu"), v("su"), v("qx"), v("sx"))
         mm(P1, v("qu"), v("su"), v("qx"), v("sx"))
-        count_at(T1, S(0))
-        if k == 0:
-            constants(0)
-        else:
-            ms(v("thf"), 1.0)
-        for b in range(4):
-            mm(v("b%d" % (2 + b), 0, C), v("qe", 128 * b, 128 * b + 128), v("se", 128 * b, 128 * b + 128), v("qx"), v("sx"))
-        ts(S(1), S(0), -64.0, A.is_gt, -2 * BIG, A.mult)
-        ts(v("m1"), v("tab"), S(1), A.add)
-        tr(v("tr1", 32, 128), v("m1"))
+        ts(S(0), S(42), -1.0, A.mult, -64.0, A.add)
+        ts(S(1), S(43), S(0), A.is_gt, -2 * BIG, A.mult)
+        ts(v("m1", 0, 32), v("tab", 0, 32), S(1), A.add)
+        ts(v("m1", 32, 96), v("tab", 32, 96), S(1), A.add)
+        tr(v("tr1", 32, 64), v("m1", 0, 32))
+        tr(v("tr1", 64, 128), v("m1", 32, 96))
         red(S(2), v("tr1", 31, 64), A.max)
         count_at(S(2), S(3))
         if k == 0:
@@ -315,8 +331,10 @@ def rank_program(g, core, T, topo):
         ts(S(5), S(4), 2.0 ** -72, A.max, 0.125, A.mult)
         ts(v("cand"), v("rat"), S(5), A.mult, S(2), A.add)
         ts(v("cand2"), v("mc"), S(3), A.is_lt, -2 * BIG, A.mult)
-        tt(v("m2"), v("cand"), v("cand2"), A.add)
-        tr(v("tr2", 32, 96), v("m2"))
+        for j in range(2):
+            tt(v("m2", 32 * j, 32 * j + 32), v("cand", 32 * j, 32 * j + 32), v("cand2", 32 * j, 32 * j + 32), A.add)
+        for j in range(2):
+            tr(v("tr2", 32 + 32 * j, 64 + 32 * j), v("m2", 32 * j, 32 * j + 32))
         red(S(20), v("tr2", 31, 64), A.max)
         RW = S(12)
         for i in range(5):
@@ -326,6 +344,8 @@ def rank_program(g, core, T, topo):
                 if k == 0:
                     constants(2)
                 red(S(9), v("tr2", 64, 98), A.max)
+                for b in range(4):
+                    mm(v("b%d" % (2 + b), 0, C), v("qe", 128 * b, 128 * b + 128), v("se", 128 * b, 128 * b + 128), v("qx"), v("sx"))
                 ts(S(10), S(9), -0.5, A.mult, S(9), A.max)
                 ts(RW, thr, S(9), A.subtract)
                 ts(c1("steps", 5), S(10), 2.0 ** -72, A.max, 0.125, A.mult)
@@ -340,29 +360,32 @@ def rank_program(g, core, T, topo):
             ts(v("m3"), v("mc", 0, 32), cnt, A.is_ge, c1("steps", 5 - i), A.mult)
             if i == 0:
                 ts(v("steps", 0, 5), v("btab", 198, 215, 4), c1("steps", 5), A.mult)
+            if i == 1:
+                cp(c1("hb", 0), c1("steps", 0))
             tr(v("tr3", 0, 32), v("m3"))
             red(S(21 + i), v("tr3", 0, 33), A.add)
-        thr, cnt, cge, TH, NEED = S(25), S(35), S(36), S(38), S(39)
+        thr, cnt, GT, TH, NEED = S(25), S(35), c1("gs", C - 1), S(38), S(39)
         count_at(thr, cnt)
-        ts(v("ge"), P1, thr, A.is_ge)
+        if k == 0:
+            constants(7)
+        ts(v("ge"), P1, thr, A.is_gt)
         ts(c1("tr4", 31), RW, -16.0 ** -5, A.mult, thr, A.add)
-        red(cge, v("ge"), A.add)
-        ts(v("m4", 0, 32), v("mge"), cge, A.is_le, c1("steps", 0), A.mult)
-        ts(S(37), cge, cnt, A.add, EPS, A.mult)
-        ts(v("m4", 64, 96), v("m448"), cge, A.subtract, EPS, A.mult)
+        scan(v("gs"), v("ge"), v("ge"), 0.0, A.add, A.max)
+        ts(v("mlc"), v("ml"), cnt, A.subtract)
+        ts(v("m0c"), v("m0"), cnt, A.min, -192.0, A.add)
+        ts(v("m4", 0, 32), v("mlc"), GT, A.is_ge, c1("hb", 0), A.mult)
+        ts(c1("hb", 1), GT, -EPS, A.mult, K * EPS, A.add)
+        ts(v("m4", 64, 96), v("m0c"), GT, A.add, EPS, A.mult)
         tr(v("tr4", 32, 64), v("m4", 0, 32))
-        ts(v("m4", 32, 64), v("mge"), cge, A.is_le, S(37), A.mult)
+        ts(v("m4", 32, 64), v("mlc"), GT, A.is_ge, c1("hb", 1), A.mult)
         red(TH, v("tr4", 31, 64), A.add)
         tr(v("tr4", 64, 128), v("m4", 32, 96))
         act(v("sig"), P0, ACT.Sign, bias=TH, scale=-1.0)
-        ts(v("neq", 0, H), v("b1", 0, H), TH, A.is_equal, -EPS, A.mult)
+        ts(hv("neq", 0), hv("b1", 0), TH, A.is_equal, -EPS, A.mult)
         red(NEED, v("tr4", 64, 128), A.max)
-        ts(v("neq", H, C), v("b1", H, C), TH, A.is_equal, -EPS, A.mult)
-        if k == 0:
-            constants(7)
-        scan(v("ns"), v("neq"), v("ctie"), NEED, A.add, A.add)
+        ts(hv("neq", 1), hv("b1", 1), TH, A.is_equal, -EPS, A.mult)
+        scan(v("ns"), v("neq"), v("zb"), NEED, A.add, A.add)
         M0 = [v("mt", 4 * H * h, 4 * H * (h + 1), 4) for h in range(2)]
-        hv = lambda n, h: v(n, H * h, H * (h + 1))
         for h in range(2):
             tt(M0[h], hv("sig", h), hv("ns", h), A.is_le)
         for h in range(2):
@@ -409,28 +432,26 @@ def rank_program(g, core, T, topo):
             decode(1, step - 1)
         decode(1, 6)
         scan(v("cs2"), v("cmul", 0, K), v("t0", 0, K), 0.0, A.mult, A.max)
-        part = ((64, 112), (16, 64))
-        for a, b in part:
-            tt(v("g1", a, b), v("cs2"), v("mg", a, b), A.mult, off=v("o15", 0, 3))
-        for a, b in part:
-            ts(v("gh", a, b), v("g1", a, b), 496, A.bitwise_and)
-            ts(v("gl", a, b), v("g1", a, b), 15, A.bitwise_and)
-        for a, b in part:
-            cp(v("bt", 4 * a, 4 * b, 4), v("gh", a, b))
-            cp(v("bt", 4 * a + 1, 4 * b, 4), v("gl", a, b))
+        ts(v("g1"), v("cs2", 15, K, 16), UNB, A.mult)
+        ts(v("gh"), v("g1"), 496, A.bitwise_and)
+        ts(v("gl"), v("g1"), 15, A.bitwise_and)
+        cp(v("bt", 0, 64, 4), v("gh"))
+        cp(v("bt", 1, 64, 4), v("gl"))
         quant(v("qb"), v("sb"), v("bt"))
-        mm(v("b6", 0, 128), v("qc", 256, 384), v("scc", 256, 384), v("qb"), v("sb"))
+        lb = (0, 1, 2, 3, 4, 6)
+        for s in range(6):
+            mm(v("b%d" % lb[s], 0, 128), v("qc", 336 - 16 * s, 464 - 16 * s), v("scc", 336 - 16 * s, 464 - 16 * s), v("qb"), v("sb"))
         if k == 0:
             ms(v("thf"), 1.0)
-        for a, b in part:
-            tt(v("l1", a, b), v("b6", a, b), v("idt", a, b), A.add)
-        for a, b in part:
-            cp(v("loff", a, b), v("l1", a, b))
+        for s in range(2):
+            ts(v("loff", 16 * s, 16 * s + 16), v("b%d" % lb[s], 0, 16), -1.0, A.add)
         src = "t0"
-        for h in range(6, 0, -1):
-            dst = "ta" if h % 2 == 0 else "tb"
-            cp(v(dst, 0, 128), v(src, 0, K), off=v("loff", 16 * h, 16 * h + 8))
-            act(v(dst, 128, K), v(src, 0, K), ACT.Copy, off=v("loff", 16 * h + 8, 16 * h + 16))
+        for s in range(6):
+            dst = "ta" if s % 2 == 0 else "tb"
+            cp(v(dst, 0, 128), v(src, 0, K), off=v("loff", 16 * s, 16 * s + 8))
+            act(v(dst, 128, K), v(src, 0, K), ACT.Copy, off=v("loff", 16 * s + 8, 16 * s + 16))
+            if s < 4:
+                ts(v("loff", 16 * s + 32, 16 * s + 48), v("b%d" % lb[s + 2], 0, 16), -1.0, A.add)
             src = dst
         for h in range(2):
             scan(v("cs3", 128 * h, 128 * h + 128), v("cmul", 0, 128), v(src, 128 * h, 128 * h + 128), 0.0, A.mult, A.max)
@@ -468,30 +489,39 @@ def rank_program(g, core, T, topo):
         ts(v("offt"), v("cs4", 15, C, 16), UNB, A.mult, -1.0, A.add)
         if k == 0:
             quant(v("qv"), v("sv"), v("vin"))
+        if k < 2:
+            ms(v("thf"), 1.0)
         if k == 2:
-            ts(v("pb"), v(src), EPS, A.mult)
-            cp(v("pa"), v("pb"))
-            cp(v("pf"), v("pa"))
+            act(v("pb"), v(src), ACT.Identity, bias=1.5 * 2.0 ** 23, scale=EPS)
+            act(v("pf"), v("pb"), ACT.Identity, bias=-1.5 * 2.0 ** 23)
             dma("Y", T.pl[:], T.pf[0:128:16, :], [v("pf")], [])
         wait("P", arr, 3 * ne)
-        for b in range(4):
+
+        def gather_add(h, b):
+            lo, hi = RUNS[h]
+            out, off = v("xt", 4 * lo + b, 4 * hi, 4), v("offt", lo // 16, hi // 16)
+            if b < 3:
+                tt(out, v("dp", 272 * b, 272 * b + 257), v("ff", C * b + lo, C * b + hi), A.add, off=off)
+            else:
+                tt(out, v("b5", lo, hi), v("d3", lo, hi), A.add)
+
+        for h in range(2):
+            mm(v("b%d" % (0, 3)[h], 0, 128), v("qe", 0, 128), v("se", 0, 128), v(ql, 128 * h, 128 * h + 128), v(sl, 128 * h, 128 * h + 128))
+        act(v("dp", 1, 129), v("b0", 0, 128), ACT.Copy)
+        cp(v("dp", 129, 257), v("b3", 0, 128))
+        for b in range(1, 4):
             bank = v("b%d" % (0, 1, 6, 7)[b], 0, K)
             mm(bank, v("qe", 128 * b, 128 * b + 128), v("se", 128 * b, 128 * b + 128), v(ql), v(sl))
             act(v("dp", 272 * b + 1, 272 * b + 1 + K), bank, ACT.Copy)
-            if b < 3:
-                tt(v("xt", b, 4 * C, 4), v("dp", 272 * b, 272 * b + 257), v("ff", C * b, C * (b + 1)), A.add, off=v("offt"))
-        act(v("d3"), v("dp", 272 * 3, 272 * 3 + 257), ACT.Copy, off=v("offt"))
-        tt(v("xt", 3, 4 * C, 4), v("b5", 0, C), v("d3"), A.add)
+        for lo, hi in RUNS:
+            act(v("d3", lo, hi), v("dp", 272 * 3, 272 * 3 + 257), ACT.Copy, off=v("offt", lo // 16, hi // 16))
+        for h, b in ((0, 0), (0, 1), (0, 2), (1, 0), (0, 3), (1, 1)):
+            gather_add(h, b)
+        new_run(k + 1, 0)
+        gather_add(1, 2)
+        gather_add(1, 3)
+        new_run(k + 1, 1)
 
-    quant(v("qx"), v("sx"), v("xt"))
-    for h in range(2):
-        mm(v("b%d" % h, 0, H), v("qv"), v("sv"), v("qx", h * H, (h + 1) * H), v("sx", h * H, (h + 1) * H))
-    dma("Y", T.oc[:], T.qx[:].bitcast(dt.uint8), [v("qx")], [])
-    cp(v("yo", 0, H), v("b0", 0, H))
-    act(v("yo", H, C), v("b1", 0, H), ACT.Copy)
-    dma("Y", T.y[:], T.yo[:], [v("yo")], [])
-    for i in range(4):
-        dma("S", T.osc[4 * i:4 * i + 4, :], T.sx[32 * i:32 * i + 4, :], [v("sx")], [])
     wait("G", "snd", 9 * ne)
     for i in range(ndma[0]):
         wait("G", "d%d" % i, 16)

@@ -1,28 +1,32 @@
 from concourse.mybir import dt, AluOpType, AxisListType, ActivationFunctionType
 
 C, K, ROUNDS = 448, 256, (1, 2, 3)
+H = C // 2
+FW = C + K
 F32, BF, I32, U16, Q4, U8 = "float32", "bfloat16", "int32", "uint16", "float8_e4m3fn_x4", "uint8"
 SB = {
-    "xin": (4 * C, BF), "uin": (512, BF), "vin": (512, BF), "qu0": (128, Q4), "su0": (128, U8), "qu": (128, Q4), "su": (128, U8),
-    "qv": (128, Q4), "sv": (128, U8), "qw": (512, Q4), "sw": (512, U8),
-    "o16": (8, U16), "et": (516, BF), "qe": (512, Q4), "se": (512, U8),
-    "ct": (1920, BF), "qc": (480, Q4), "scc": (480, U8), "zb": (C, BF),
-    "xt": (4 * C, BF), "qx": (C, Q4), "sx": (C, U8), "ff": (4 * C, BF),
-    "junk": (C, BF), "ge": (C, BF), "gs": (C, BF), "hb": (8, BF), "sig": (C, BF), "neq": (C, BF), "ns": (C, BF),
-    "mt": (4 * C, BF), "qm": (C, Q4), "sm": (C, U8), "pos": (32, U16), "t0": (960, F32), "ta": (K, F32), "tb": (K, F32),
-    "bt": (512, BF), "qb": (128, Q4), "sb": (128, U8), "loff": (128, U16), "offc": (16, U16), "thf": (C, F32), "offt": (28, U16), "pf": (K, F32),
-    "zt": (4 * K, BF), "qz": (K, Q4), "sz": (K, U8), "ht": (4 * K, BF), "dp": (4 * 272, BF), "d3": (C, BF), "yo": (C, F32),
+    "xin": (4 * C, BF), "uin": (512, BF), "vin": (512, BF), "qu0": (128, Q4), "su0": (128, U8), "qu": (256, Q4), "su": (256, U8),
+    "qg": (128, Q4), "sg": (128, U8), "qv": (128, Q4), "sv": (128, U8), "qw": (512, Q4), "sw": (512, U8),
+    "ou": (24, U16), "r16": (28, U16), "et": (516, BF), "qe": (512, Q4), "se": (512, U8),
+    "ct": (516, BF), "qc": (256, Q4), "scc": (256, U8), "zb": (C, BF), "c1024": (C, BF), "m16": (32, BF), "cmul": (C, BF), "csum": (C, BF),
+    "xt": (4 * C, BF), "qx": (C, Q4), "sx": (C, U8), "ff": (4 * FW, BF),
+    "junk": (4 * C, BF), "spA": (C, F32), "spB": (C, F32), "sig": (C, BF), "neq": (C, BF), "ns": (C, BF),
+    "mt": (4 * H, BF), "qm": (H, Q4), "sm": (H, U8), "dd": (C, BF), "ll": (C, BF), "bw": (C, BF),
+    "pos": (32, U16), "t0": (1200, F32), "ta": (272, F32), "tb": (272, F32), "tq": (576, F32), "q0": (168, F32), "q1": (168, F32),
+    "loff": (108, U16), "offc": (16, U16), "thf": (C, F32), "offt": (28, U16), "pf": (K, F32),
+    "zt": (4 * K, BF), "qz": (K, Q4), "sz": (K, U8), "ht": (4 * K, BF), "yo": (C, F32),
 }
 for _k in range(3):
     SB["qh%d" % _k], SB["sh%d" % _k], SB["ql%d" % _k], SB["sl%d" % _k] = (K, Q4), (K, U8), (K, Q4), (K, U8)
+LINE = {"s": 32, "m1": 64, "t1": 64, "cand": 128, "m2": 128, "t2": 128, "wk": 16, "m3": 64, "t3": 80, "m4": 64, "t4": 80, "m5": 32, "t5": 48, "row": 16}
 POOLS = {
-    "kf": (F32, {"kc": 16, "half": 145, "two": 145, "zer": C, "btab": 290, "ya": 64, "yt": 64, "j16": 16, "nn": 16, "ra": 16, "rb": 16, "rc": 16,
-                 "t2": 16, "t3": 16, "tab": 96, "mbig": 64, "rat": 64, "mc": 64, "ml": 32, "m0": 32, "ca": 16, "cb": 16, "cd": 16,
-                 "ce": 16, "cmul": 512, "csum": 512, "c1024": C, "kk": 28, "k2": 28, "kio": K, "c3": 42}),
-    "ki": (I32, {"pint": 2, "rint": 2, "hint": 1, "o16i": 8}),
-    "wf": (F32, {"sc": 64, "m1": 96, "m2": 64, "m3": 32, "m4": 96, "mlc": 32, "m0c": 32, "tr1": 136, "tr2": 128, "tr3": 64, "tr4": 128, "cand": 64,
-                 "cand2": 64, "steps": 6, "vs": C, "cap": C, "vv": C, "cs": C, "x1": 28, "tri": 84, "x3": 84, "cs2": K, "cs3": K, "cs4": C, "pb": K}),
-    "wi": (I32, {"xi": 28, "zi": 28, "ai": 28, "ni": 28, "g1": 16, "gh": 16, "gl": 16}),
+    "kf": (F32, {"kc": 32, "dn": 16, "up": 16, "zer": 64, "lam": 64, "lt": 64, "fac": 32, "inc": 32, "edge": 40, "fx": 40, "fy": 40, "tab": 64,
+                 "ca": 16, "cb": 16, "cd": 16, "ce": 16, "cf": 16, "mc": 32, "mcf": 32, "ratA": 128, "ratB": 128, "j64": 64, "krow": 16,
+                 "i16": 32, "col": 32, "col1": C, "kio": K}),
+    "ki": (I32, {"pint": 2, "rint": 2, "hint": 1, "qint": 1, "oui": 24}),
+    "wf": (F32, dict([(n + x, w) for x in "AB" for n, w in LINE.items()],
+                     sc=8, m6=64, t6=80, vs=C, vw=C, cs=C, x3=168, l6a=16, l6b=16, l6=16, cs3=K, cs4=C, pb=K)),
+    "wi": (I32, {"xi": 48, "xa": 48}),
 }
 AT = {}
 for _p, (_d, _m) in POOLS.items():
@@ -38,8 +42,9 @@ SEMAPHORES = ["sV", "sS", "sP", "sG", "snd", "arr0", "arr1", "arr2"] + ["d%d" % 
 
 BIG = 2.0 ** 80
 EPS = 2.0 ** -10
-OFF = 1024.0
-RUNS = ((0, 320), (320, C))
+LOW = -2 ** 22
+WAKE = 240
+RUNS = ((0, 256), (256, C))
 
 
 def rank_program(g, core, T, topo):
@@ -52,18 +57,22 @@ def rank_program(g, core, T, topo):
     known = {e: {} for e in Q}
     clock = {}
     log = {}
+    calls = []
     ndma = [0]
 
-    def v(n, a=0, b=None, s=1):
+    def v(n, a=0, b=None, s=1, p=(0, 128)):
         buf, o, w = AT[n] if n in AT else (n, 0, T[n].shape[1])
         b = w if b is None else b
-        return (T[buf][:, o + a:o + b:s] if s > 1 else T[buf][:, o + a:o + b], n, a, b, s)
+        return (T[buf][p[0]:p[1], o + a:o + b:s] if s > 1 else T[buf][p[0]:p[1], o + a:o + b], n, a, b, s, p)
 
     def c1(n, a):
         return v(n, a, a + 1)
 
+    def part(x, p):
+        return v(x[1], x[2], x[3], x[4], p)
+
     def meet(x, y):
-        if x[3] <= y[2] or y[3] <= x[2]:
+        if x[3] <= y[2] or y[3] <= x[2] or x[5][1] <= y[5][0] or y[5][1] <= x[5][0]:
             return False
         return not (x[4] == y[4] and x[4] > 1 and (x[2] - y[2]) % x[4])
 
@@ -76,31 +85,70 @@ def rank_program(g, core, T, topo):
             if known[e].get(s2, 0) < v2:
                 known[e][s2] = v2
 
-    def op(e, call, reads, writes, dma=False):
-        need = {}
+    def op(e, call, reads, writes, cost, late=0, kind="calc"):
+        deps = set()
         both = [(x, False) for x in reads] + [(x, True) for x in writes]
         for view, wr in both:
             psum = view[1][0] == "b" and view[1][1:].isdigit()
-            for (o, ow, oe, sem, val) in log.get(view[1], []):
-                if (psum and oe != e) or ((wr or ow) and meet(view, o)):
-                    need[sem] = max(need.get(sem, 0), val)
-        for sem, val in need.items():
-            wait(e, sem, val)
-        if dma:
-            sem, val = "d%d" % ndma[0], 16
-            ndma[0] += 1
-            call().then_inc(T.sem[sem], 16)
-        else:
-            sem = "s" + e
-            count[sem] += 1
-            val = count[sem]
-            call().then_inc(T.sem[sem], 1)
-        clock[(sem, val)] = dict(known[e])
+            for (o, ow, i) in log.get(view[1], []):
+                if (psum and calls[i][0] != e) or ((wr or ow) and meet(view, o)):
+                    deps.add(i)
         for view, wr in both:
             old = log.get(view[1], [])
-            if wr and view[4] == 1:
+            if wr and view[4] == 1 and view[5] == (0, 128):
                 old = [r for r in old if not (view[2] <= r[0][2] and r[0][3] <= view[3])]
-            log[view[1]] = old + [(view, wr, e, sem, val)]
+            log[view[1]] = old + [(view, wr, len(calls))]
+        calls.append((e, call, sorted(deps), cost, late, kind))
+
+    def in_order():
+        n = len(calls)
+        tail, users, left = [0] * n, [[] for _ in calls], [len(c[2]) for c in calls]
+        for i in range(n - 1, -1, -1):
+            tail[i] += calls[i][3] + calls[i][4]
+            for d in calls[i][2]:
+                tail[d] = max(tail[d], tail[i] + WAKE)
+                users[d].append(i)
+        ready, free, order = [0] * n, {e: 0 for e in Q}, []
+        todo = [i for i in range(n) if not left[i]]
+        while todo:
+            e = calls[min(todo, key=lambda i: max(ready[i], free[calls[i][0]]))][0]
+            mine = [i for i in todo if calls[i][0] == e]
+            t = max(free[e], min(ready[i] for i in mine))
+            x = max((i for i in mine if ready[i] <= t), key=lambda i: (tail[i], -i))
+            soon = [y for y in mine if t < ready[y] < t + calls[x][3]
+                    and max(ready[y] + tail[y], ready[y] + calls[y][3] + tail[x]) < max(t + calls[x][3] + tail[y], t + tail[x])]
+            if soon:
+                free[e] = min(ready[y] for y in soon)
+                continue
+            todo.remove(x)
+            order.append(x)
+            free[e] = t + calls[x][3]
+            for u in users[x]:
+                ready[u] = max(ready[u], free[e] + calls[x][4] + WAKE)
+                left[u] -= 1
+                if not left[u]:
+                    todo.append(u)
+        return order
+
+    def issue():
+        mark = {}
+        for i in in_order():
+            e, call, deps, _, _, kind = calls[i]
+            for d in deps:
+                if d in mark:
+                    wait(e, *mark[d])
+            if kind == "bare":
+                call()
+                continue
+            if kind == "dma":
+                mark[i] = ("d%d" % ndma[0], 16)
+                ndma[0] += 1
+                call().then_inc(T.sem[mark[i][0]], 16)
+            else:
+                count["s" + e] += 1
+                mark[i] = ("s" + e, count["s" + e])
+                call().then_inc(T.sem["s" + e], 1)
+            clock[mark[i]] = dict(known[e])
 
     def aps(*xs):
         return [x for x in xs if isinstance(x, tuple)]
@@ -108,40 +156,48 @@ def rank_program(g, core, T, topo):
     def ap(x):
         return x[0] if isinstance(x, tuple) else x
 
+    def size(x):
+        return len(range(x[2], x[3], x[4]))
+
+    def wide(*xs):
+        return max(64, size(xs[0]) // (2 if all(SB.get(x[1], (0, F32))[1] == BF for x in xs) else 1))
+
     def ts(o, i, s1, op0, s2=None, op1=None):
         if op1 is None:
-            op("V", lambda: g.vector.tensor_scalar(o[0], i[0], ap(s1), None, op0), aps(i, s1), [o])
+            op("V", lambda: g.vector.tensor_scalar(o[0], i[0], ap(s1), None, op0), aps(i, s1), [o], wide(o, i))
         else:
-            op("V", lambda: g.vector.tensor_scalar(o[0], i[0], ap(s1), ap(s2), op0, op1), aps(i, s1, s2), [o])
+            op("V", lambda: g.vector.tensor_scalar(o[0], i[0], ap(s1), ap(s2), op0, op1), aps(i, s1, s2), [o], wide(o, i))
 
-    def tt(o, a, b, op0, off=None):
-        src = a[0].indirect(off[0]) if off else a[0]
-        op("V", lambda: g.vector.tensor_tensor(o[0], src, b[0], op0), aps(a, b, off), [o])
+    def tt(o, a, b, op0):
+        op("V", lambda: g.vector.tensor_tensor(o[0], a[0], b[0], op0), aps(a, b), [o], max(64, size(o)))
 
     def cp(o, i, off=None):
         src = i[0].indirect(off[0]) if off else i[0]
-        op("V", lambda: g.vector.tensor_copy(o[0], src), aps(i, off), [o])
+        op("V", lambda: g.vector.tensor_copy(o[0], src), aps(i, off), [o], 60 + 1.5 * size(o) if off else wide(o, i))
+
+    def pick(o, i, off):
+        op("V", lambda: g.vector.tensor_copy(o[0].bitcast(dt.uint32), i[0].bitcast(dt.uint32).indirect(off[0])), [i, off], [o], 60 + 1.5 * size(o))
 
     def scat(o, off, i):
-        op("V", lambda: g.vector.tensor_copy(o[0].indirect(off[0]), i[0]), [i, off], [o])
+        op("V", lambda: g.vector.tensor_copy(o[0].indirect(off[0]), i[0]), [i, off], [o], 60 + 3.5 * size(i))
 
     def scan(o, d0, d1, init, op0, op1):
-        op("V", lambda: g.vector.tensor_tensor_scan(o[0], d0[0], d1[0], ap(init), op0, op1), aps(d0, d1, init), [o])
+        op("V", lambda: g.vector.tensor_tensor_scan(o[0], d0[0], d1[0], ap(init), op0, op1), aps(d0, d1, init), [o], wide(o, d0, d1))
 
     def red(o, i, op0):
-        op("V", lambda: g.vector.tensor_reduce(o[0], i[0], AxisListType.X, op0), [i], [o])
+        op("V", lambda: g.vector.tensor_reduce(o[0], i[0], AxisListType.X, op0), [i], [o], max(64, size(i)))
 
     def tr(o, i):
-        op("V", lambda: g.vector.transpose(o[0], i[0]), [i], [o])
+        op("V", lambda: g.vector.transpose(o[0], i[0]), [i], [o], wide(o, i))
 
     def ms(o, val):
-        op("V", lambda: g.vector.memset(o[0], val), [], [o])
+        op("V", lambda: g.vector.memset(o[0], val), [], [o], wide(o))
 
     def quant(q, s, i):
-        op("V", lambda: g.vector.quantize_mx(q[0], s[0], i[0]), [i], [q, s])
+        op("V", lambda: g.vector.quantize_mx(q[0], s[0], i[0]), [i], [q, s], 15 + size(i) // 4)
 
     def mm(o, lq, ls, rq, rs):
-        op("P", lambda: g.tensor.matmul_mx(o[0], lq[0], ls[0], rq[0], rs[0], True, True), [lq, ls, rq, rs], [o])
+        op("P", lambda: g.tensor.matmul_mx(o[0], lq[0], ls[0], rq[0], rs[0], True, True), [lq, ls, rq, rs], [o], 16 + size(o))
 
     def act(o, i, func, bias=None, scale=None, acc=None, off=None):
         src = i[0].indirect(off[0]) if off else i[0]
@@ -152,376 +208,340 @@ def rank_program(g, core, T, topo):
             kw["scale"] = ap(scale)
         if acc is not None:
             kw["accum_out"] = acc[0]
-        op("S", lambda: g.scalar.activation(o[0], src, func, **kw), aps(i, bias, scale, off), aps(o, acc))
+        op("S", lambda: g.scalar.activation(o[0], src, func, **kw), aps(i, bias, scale, off), aps(o, acc), 80 + max(64, size(o)) * (1.5 if off else 1))
 
-    def iota(o, pat, base, cm):
+    def iota(o, pat, base, cm=0):
         if o[1] in POOLS["ki"][1]:
-            op("G", lambda: g.iota(o[0], pat, base, cm), [], [o])
+            op("G", lambda: g.iota(o[0], pat, base, cm), [], [o], 160 + 2 * size(o))
         else:
-            op("G", lambda: g.iota(o[0], pat, base, cm, allow_small_or_imprecise_dtypes=True), [], [o])
+            op("G", lambda: g.iota(o[0], pat, base, cm, allow_small_or_imprecise_dtypes=True), [], [o], 160 + 2 * size(o))
 
-    def sel(o, i, pat, cmp, fill, base, cm):
-        op("G", lambda: g.affine_select(o[0], i[0], pat, cmp, fill, base, cm), [i], [o])
+    def fill(o, val):
+        iota(o, [[0, size(o)]], val)
 
-    def dma(e, o, i, reads, writes):
-        op(e, lambda: Q[e].dma_start(o, i), reads, writes, dma=True)
+    def sel(o, pat, val, base, cm):
+        op("G", lambda: g.affine_select(o[0], o[0], pat, A.not_equal, val, base, cm), [o], [o], 200 + 2 * size(o))
 
-    H = C // 2
+    def dma(e, o, i, reads, writes, late=2000):
+        op(e, lambda: Q[e].dma_start(o, i), reads, writes, 60, late, "dma")
+
     hv = lambda n, h: v(n, H * h, H * (h + 1))
+    bank = lambda i, a, b=None: v("b%d" % i, 0, a) if b is None else v("b%d" % i, a, b)
+    blk = lambda n, i: v(n, 128 * i, 128 * i + 128)
     dma("S", T.uin[:], T.u[:], [], [v("uin")])
     for a, b in RUNS:
-        dma("Y", T.xin[:, 4 * a:4 * b], T.x[:, 4 * a:4 * b], [], [v("xin", 4 * a, 4 * b)])
+        dma("Y", T.xin[:, 4 * a:4 * b], T.x[:, 4 * a:4 * b], [], [v("xin", 4 * a, 4 * b)], 2000 + 3 * b)
     dma("Y", T.qw[:].bitcast(dt.uint8), T.wc[:], [v("xin")], [v("qw")])
-    dma("Y", T.sw[:], T.ws[:], [], [v("sw")])
-    dma("Y", T.vin[:], T.v[:], [], [v("vin")])
+    dma("Y", T.sw[:], T.ws[:], [v("xin")], [v("sw")])
+    dma("Y", T.vin[:], T.v[:], [v("xin")], [v("vin")])
 
-    RF, RM1, RP1, HM0, HM1, R0, UN0, UNA, UNB, UNC, TA, TW = [c1("kc", i) for i in range(12)]
-    G16 = [[-16, 8], [0, 16]]
+    (RF, RM1, RP1, OD, EV, J, SG, FM, D0, MCF, UN0, UNA, UNB, NB, S14, S15, N14, N15, O2, O3, R0, RN) = [c1("kc", i) for i in range(22)]
     iota(v("pint"), [[15, 2]], 0, 1)
-    iota(v("o16i"), [[16, 8]], 0, 0)
-    iota(v("j16"), [[1, 16]], 0, 0)
-    ms(v("half"), 0.5)
-    ms(v("two"), 2.0)
-    ms(v("zer", 0, 152), 0.0)
-    ms(v("et"), 0.0)
-    sel(v("et"), v("et"), [[1, 516]], A.not_equal, 1.0, -3, -4)
-    iota(v("zer", 152, C), [[0, C - 152]], 0, 0)
-    iota(v("ct"), [[0, 1920]], 0, 0)
-    scan(v("btab", 0, 145), v("half"), v("zer", 0, 145), -2.0 ** 72, A.mult, A.add)
-    scan(v("btab", 145, 290), v("two"), v("zer", 0, 145), 2.0 ** -74, A.mult, A.add)
+    iota(v("oui", 0, 16), [[16, 2], [32, 4], [0, 2]], 0)
+    iota(v("oui", 16, 24), [[16, 8]], 0)
+    iota(v("j64"), [[1, 64]], 0)
+    iota(v("i16"), [[16, 32]], 0)
+    iota(v("col1"), [[1, C]], 1)
+    iota(v("kio"), [[1, K]], C + 1)
+    fill(v("zb"), 0)
+    fill(v("c1024"), 1024)
+    ms(v("zer"), 0.0)
     ts(v("rint"), v("pint"), 15, A.bitwise_and)
     ts(v("hint"), c1("pint", 0), 16, A.bitwise_and)
-    cp(v("o16"), v("o16i"))
-    for i in range(2):
-        act(v("ya", 16 * i, 16 * i + 16), v("btab", 17, 289, 17), ACT.Copy)
-        act(v("ya", 32 + 16 * i, 48 + 16 * i), v("btab", 1, 17), ACT.Copy)
+    ts(v("qint"), c1("pint", 0), 31, A.bitwise_and)
     cp(v("kc", 0, 2), v("rint"))
+    cp(J, v("qint"))
     ts(RP1, c1("rint", 0), 1.0, A.add)
-    ts(HM1, v("hint"), 8.0, A.subtract, BIG / 8, A.mult)
-    ts(HM0, v("hint"), 8.0, A.subtract, -BIG / 8, A.mult)
-    ts(v("nn"), v("j16"), 1.0 / 17, A.mult, RP1, A.add)
-    tr(v("yt"), v("ya"))
-    T1 = c1("yt", 0)
-    ts(v("ca"), v("j16"), RF, A.not_equal)
-    ts(v("cb"), v("j16"), RP1, A.is_equal, 2.0 ** 20, A.mult)
-    ts(v("cd"), v("j16"), RM1, A.not_equal)
-    ts(v("ce"), v("j16"), RP1, A.is_equal, 2.0 ** 40, A.mult)
-    ts(v("ra"), v("nn"), 144.5 / 17, A.is_gt, 3.0, A.mult)
-    ts(v("rb"), v("nn"), 143.5 / 17, A.is_gt, -1.5, A.mult)
-    tt(v("cmul", 0, 16), v("ca"), v("cb"), A.max)
-    tt(v("csum", 0, 16), v("cd"), v("ce"), A.max)
-    tt(v("rc"), v("ra"), v("rb"), A.add)
-    ts(TA, T1, -0.5, A.mult, T1, A.max)
-    for i in range(4):
-        ts(v("mbig", 16 * i, 16 * i + 16), v("zer", 0, 16), (HM0, HM1)[i % 2], A.add)
-    ts(v("ra"), v("rc"), 0.5, A.add)
-    ts(TW, TA, 2.0 ** -72, A.max, 0.125, A.mult)
-    ms(v("rat", 32, 64), 0.0)
-    for i in range(2):
-        ts(v("rat", 16 * i, 16 * i + 16), v("j16"), 1.0, A.add)
-    quant(v("qu0"), v("su0"), v("uin"))
-    for w in (16, 32, 64):
-        for n in ("cmul", "csum"):
-            act(v(n, w, 2 * w), v(n, 0, w), ACT.Copy)
-    scan(v("t2"), v("ra"), v("zer", 0, 16), T1, A.mult, A.add)
-    cp(c1("tr1", 31), c1("yt", 32))
-    op("V", lambda: g.vector.tensor_copy(T.qu[:, 0:128].bitcast(dt.uint32), T.qu0[:, 0:128].bitcast(dt.uint32).indirect(T.o16[:, 0:8])),
-       [v("qu0"), v("o16")], [v("qu")])
-    act(v("su"), v("su0"), ACT.Copy, off=v("o16"))
-    for n in ("cmul", "csum"):
-        act(v(n, 128, 256), v(n, 0, 128), ACT.Copy)
-    for o in (0, 512):
-        sel(v("ct", o, o + 512, 4), v("ct", o, o + 512, 4), G16, A.not_equal, -EPS, -8, 1)
-    sel(v("ct", 0, 64, 4), v("ct", 0, 64, 4), [[0, 16]], A.not_equal, 1.0, 0, 1)
-    sel(v("ct", 64, 512, 4), v("ct", 64, 512, 4), [[-16, 7], [0, 16]], A.not_equal, 1.0, 0, 1)
-    sel(v("ct", 512, 1024, 4), v("ct", 512, 1024, 4), G16, A.not_equal, 1.0, 0, 1)
+    ts(OD, v("hint"), 1.0 / 16, A.mult)
+    ts(EV, v("hint"), -1.0 / 16, A.mult, 1.0, A.add)
+    ts(v("col"), v("i16"), RF, A.add)
+    ts(v("r16"), v("zer", 0, 28), RF, A.add)
+    fill(v("et"), 0)
+    sel(v("et"), [[1, 516]], 1.0, -3, -4)
+    for b in range(4):
+        quant(blk("qe", b), blk("se", b), v("et", 3 - b, 515 - b))
+    fill(v("ct"), 0)
+    sel(v("ct", 65, 513, 4), [[-16, 7], [0, 16]], 1.0, -16, 1)
+    sel(v("ct", 65, 513, 4), [[-16, 7], [0, 16]], -1.0, 0, 1)
     for t in range(2):
-        sel(v("ct", 1024 + t, 1408, 4), v("ct", 1024 + t, 1408, 4), [[0, 6], [-1, 16]], A.not_equal, 1.0, 0, 1)
-        sel(v("ct", 1408 + t, 1920, 4), v("ct", 1408 + t, 1920, 4), [[-1, 128]], A.not_equal, 1.0, 0, 1)
-    iota(v("kk"), [[32, 28]], 2050, 0)
-    iota(v("c3"), [[0, 14], [30000, 3]], 0, 0)
-    iota(v("kio"), [[1, K]], 2, 0)
+        quant(blk("qc", t), blk("scc", t), v("ct", 1 - t, 513 - t))
+        fill(v("mt", 2 + t, 4 * H, 4), 0)
+    cp(v("ou"), v("oui"))
+    quant(v("qu0"), v("su0"), v("uin"))
+    for q, s, off in (("qu", "su", v("ou", 0, 16)), ("qg", "sg", v("ou", 16, 24))):
+        pick(v(q), v("qu0"), off)
+        act(v(s), v("su0"), ACT.Copy, off=off)
+    quant(v("qv"), v("sv"), v("vin"))
+    ms(v("dn"), 2.0 ** -8)
+    ms(v("up"), 2.0 ** 8)
+    for i in range(2):
+        scan(v("lam", 32 * i, 32 * i + 16), v("dn"), v("zer", 0, 16), -2.0 ** 79, A.mult, A.add)
+        scan(v("lam", 32 * i + 16 + i, 32 * i + 32), v("up", i, 16), v("zer", i, 16), 2.0 ** (8 * i - 65), A.mult, A.add)
+    ms(c1("lam", 48), 0.0)
+    tr(v("lt"), v("lam"))
+    E0, T1 = c1("lt", 0), c1("lt", 32)
+    ts(SG, v("hint"), 0.125, A.mult, -1.0, A.add)
+    ts(FM, v("hint"), 1.5 / 16, A.mult, 0.5, A.add)
+    ts(D0, v("hint"), 0.375 / 16, A.mult, -0.125, A.add)
+    ts(D0, D0, E0, A.mult)
+    ms(v("fac"), 1.0)
+    ts(v("fac", 4, 32, 4), v("zer", 0, 7), FM, A.add)
+    scan(v("inc"), v("fac"), v("zer", 0, 32), D0, A.mult, A.add)
+    cp(c1("edge", 0), E0)
+    scan(v("edge", 1, 33), v("inc"), v("zer", 0, 32), E0, A.add, A.add)
+    ts(v("fx", 0, 33), v("edge", 0, 33), SG, A.mult, 2.0 ** -56, A.subtract)
+    ts(v("fy", 0, 33), v("fx", 0, 33), 0.0, A.min, SG, A.mult)
+    for j in range(2):
+        tt(v("tab", 32 * j, 32 * j + 32), v("edge", j, j + 32), v("fy", j, j + 32), A.add)
+    ms(v("mc"), -64.0)
+    ts(MCF, v("qint"), 0.5, A.is_lt, BIG, A.mult)
+    ts(MCF, MCF, -64.0, A.add)
+    ts(v("mcf"), v("zer", 0, 32), MCF, A.add)
+    for x, n in (("A", 32), ("B", 64)):
+        ts(v("rat" + x, 0, 64), v("j64"), 1.0 / n, A.mult)
+        ms(v("rat" + x, 64, 96), 0.0)
+        ms(v("rat" + x, 96, 128), 1.0)
+    for j, (a, b) in enumerate(((0, 2 ** 18), (0, 2 ** 17), (0, 2 ** 12), (0, 2 ** 7), (0, 4),
+                                (2 ** 12 - 2 ** 18, -2 ** 18), (2 ** 12 - 2 ** 18, -2 ** 17), (2 ** 12 - 2 ** 17, -2 ** 17),
+                                (2 ** 7 - 2 ** 12, 2 ** 7 - 2 ** 12 - 3), (4 - 2 ** 7, 4 - 2 ** 7), (-4, -1))):
+        act(c1("krow", j), J, ACT.Identity, bias=float(b), scale=float(a))
+    j16 = v("j64", 0, 16)
+    ts(v("ca"), j16, RF, A.not_equal)
+    ts(v("cb"), j16, RP1, A.is_equal, 2.0 ** 20, A.mult)
+    ts(v("cd"), j16, RM1, A.not_equal)
+    ts(v("ce"), j16, RP1, A.is_equal, 2.0 ** 48, A.mult)
+    ts(v("cf"), j16, RF, A.is_equal, 2.0 ** -8 - 2.0, A.mult)
+    tt(v("m16", 0, 16), v("ca"), v("cb"), A.max)
+    tt(v("cd"), v("cd"), v("ce"), A.max)
+    tt(v("m16", 16, 32), v("cd"), v("cf"), A.add)
+    act(v("cmul"), v("m16", 0, 16), ACT.Copy, off=v("r16"))
+    act(v("csum"), v("m16", 16, 32), ACT.Copy, off=v("r16"))
+    ts(UN0, RF, 15.0, A.is_equal)
+    ts(R0, RF, 0.0, A.is_equal)
+    ts(RN, RF, 0.0, A.not_equal)
+    ts(UNB, UN0, 2.0 ** -20, A.max)
+    ts(UNA, UN0, 2.0 ** -20, A.max, EPS, A.mult)
+    ts(NB, UN0, 2.0 ** -20, A.max, -4096.0, A.mult)
+    ts(S14, R0, 2.0 ** -40, A.mult)
+    ts(N14, R0, -2.0 ** -40, A.mult)
+    ts(S15, UN0, 256.0, A.mult, 2.0 ** -40, A.max)
+    ts(S15, S15, RN, A.mult)
+    ts(N15, S15, -1.0, A.mult)
+    for n, j, val in (("q0", 0, LOW), ("q0", 5, 0), ("q1", 2, LOW), ("q1", 3, LOW)):
+        fill(v(n, j, 168, 6), val)
+    ts(v("q0", 1, 168, 6), v("col", 0, 28), 1025.0, A.mult, 737.0, A.add)
+    ts(v("q0", 2, 168, 6), v("col", 0, 28), -1024.0, A.mult, -1.0, A.add)
+    for a in (0, 272):
+        fill(v("t0", a, a + 16), 1)
+    ts(O2, OD, 272.0, A.mult, 15.0, A.add)
+    ts(O3, EV, 16.0, A.mult, -1.0, A.add)
+    ts(v("loff", 18, 35), v("col", 0, 17), O2, A.add, O3, A.subtract)
+    for s in range(2, 5):
+        cp(v("loff", 18 * s, 18 * s + 17), v("col", 0, 17))
+    ts(v("loff", 90, 106), v("col", 0, 16), O3, A.add, 1.0, A.add)
 
-    def constants(i):
-        if i == -1:
-            ts(v("t3"), v("rat", 0, 16), TW, A.mult, T1, A.add)
-            ts(c1("tr1", 128), RP1, 2.0 ** 67, A.mult, -2.0 ** 71, A.add)
-            ms(c1("tr2", 97), -2.0 ** 71)
-            ts(v("tab", 32, 64), v("mbig", 0, 32), T1, A.min)
-            for j in range(2):
-                ts(v("tab", 16 * j, 16 * j + 16), v("t2"), (HM0, HM1)[j], A.min)
-                ts(v("tab", 64 + 16 * j, 80 + 16 * j), v("t3"), (HM0, HM1)[j], A.min)
-            ts(v("mc"), v("mbig"), -64.0, A.min, -1000.0, A.max)
-        if i == 0:
-            for b in range(2):
-                quant(v("qe", 128 * b, 128 * b + 128), v("se", 128 * b, 128 * b + 128), v("et", 3 - b, 515 - b))
-            act(v("c1024"), v("zer"), ACT.Identity, bias=1024.0)
-        if i == 1:
-            act(v("zb"), v("zer"), ACT.Copy)
-        if i == 2:
-            act(v("bt", 0, C), v("zer"), ACT.Copy)
-        if i in (3, 4):
-            ms(v("mt", 2 * C * (i - 3), 2 * C * (i - 2)), 0.0)
-        if i == 3:
-            ms(v("bt", C, 512), 0.0)
-        if i == 4:
-            ms(v("dp", 0, 4 * 272, 272), 0.0)
-            ts(UN0, RF, 15.0, A.is_equal)
-        if i == 5:
-            ts(R0, RF, 0.5, A.is_gt, -2 * BIG, A.mult)
-            ts(v("ml"), v("mbig", 0, 32), 192.0, A.min, -1000.0, A.max)
-            ts(UNB, UN0, 2.0 ** -20, A.max)
-            ts(UNC, UN0, 2.0 ** -40, A.max, -1024.0, A.mult)
-            ts(UNA, UN0, 2.0 ** -20, A.max, EPS, A.mult)
-            ts(v("m0"), v("mbig", 0, 32), R0, A.add)
-            ts(v("k2"), v("kk"), RF, A.add, RF, A.add)
-        if i == 6:
-            quant(v("qc"), v("scc"), v("ct"))
-        if i == 7:
-            for n in ("csum", "cmul"):
-                act(v(n, 256, C), v(n, 0, C - 256), ACT.Copy)
-
-    S = lambda i: c1("sc", i)
-    P0, P1 = v("b0", 0, C), v("b1", 0, C)
-
-    def count_at(thr, c):
-        act(v("junk"), P0, ACT.Sign, bias=thr, scale=-1.0, acc=c)
+    def count_at(src, thr, c, slot):
+        act(v("junk", C * slot, C * slot + size(src)), src, ACT.Sign, bias=thr, scale=-1.0, acc=c)
 
     def new_run(k, h):
         a, b = RUNS[h]
         quant(v("qx", a, b), v("sx", a, b), v("xin" if k == 0 else "xt", 4 * a, 4 * b))
-        bank = v("b%d" % (4, 2)[h], 0, b - a)
         if k < 3:
-            mm(bank, v("qu"), v("su"), v("qx", a, b), v("sx", a, b))
-            act(v("junk", a, b), bank, ACT.Sign, bias=T1, scale=-1.0, acc=S(42 + h))
+            for i, x in enumerate("AB"):
+                mm(bank(2 + 2 * h + i, b - a), blk("qu", i), blk("su", i), v("qx", a, b), v("sx", a, b))
+                count_at(bank(2 + 2 * h + i, b - a), T1, c1("s" + x, h), i + 2 * h)
         else:
-            mm(bank, v("qv"), v("sv"), v("qx", a, b), v("sx", a, b))
+            out = bank(2 + 2 * h, b - a)
+            mm(out, v("qv"), v("sv"), v("qx", a, b), v("sx", a, b))
             dma("Y", T.oc[:, 4 * a:4 * b], T.qx[:, a:b].bitcast(dt.uint8), [v("qx", a, b)], [])
             if h == 1:
                 for i in range(4):
                     dma("YS"[i % 2], T.osc[4 * i:4 * i + 4, :], T.sx[32 * i:32 * i + 4, :], [v("sx")], [])
-                cp(v("yo", a, b), bank)
+                cp(v("yo", a, b), out)
             else:
-                act(v("yo", a, b), bank, ACT.Copy)
+                act(v("yo", a, b), out, ACT.Copy)
             dma("SY"[h], T.y[:, a:b], T.yo[:, a:b], [v("yo", a, b)], [])
 
-    for b in range(2, 4):
-        quant(v("qe", 128 * b, 128 * b + 128), v("se", 128 * b, 128 * b + 128), v("et", 3 - b, 515 - b))
+    def search(i, x):
+        s = lambda j: c1("s" + x, j)
+        w = lambda n, a=0, b=None: v(n + x, a, b)
+        wk = lambda j: c1("wk" + x, j)
+        raw, rel = bank(i, C), v("sp" + x)
+        T2, NX, WP, T3, T3B, LO, HI, W, T4, T4B, T5, T6 = [s(j) for j in range(8, 20)]
+        n3, n4 = 32 * (1 + i), 32 * (2 - i)
+        ts(s(2), s(0), -1.0, A.mult, MCF, A.add)
+        ts(s(3), s(1), s(2), A.is_gt, -2 * BIG, A.mult)
+        ts(w("m1"), v("tab"), s(3), A.add)
+        tr(w("t1"), w("m1"))
+        red(T2, w("t1", 0, 32), A.max)
+        red(NX, w("t1", 32, 64), A.max)
+        count_at(raw, T2, s(4), i)
+        ts(WP, NX, T2, A.subtract)
+        ts(w("cand"), v("rat" + x), WP, A.mult, T2, A.add)
+        ts(s(5), s(4), MCF, A.is_gt, -2 * BIG, A.mult)
+        for a in (0, 64):
+            ts(w("m2", a, a + 64), w("cand", a, a + 64), s(5), A.add)
+            tr(w("t2", a, a + 64), w("m2", a, a + 64))
+        red(T3, w("t2", 0, 32), A.max)
+        red(LO, w("t2", 64, 96), A.max)
+        red(HI, w("t2", 96, 128), A.max)
+        ts(W, HI, LO, A.subtract, 2.0 ** -23, A.mult)
+        ts(w("wk", 0, 11), v("krow", 0, 11), W, A.mult)
+        for h in range(2):
+            ts(hv("sp" + x, h), bank(6 + i, H * h, H * h + H), LO, A.subtract)
+        count_at(raw, T3, s(6), i)
+        ts(w("t3", 7, 8), T3, wk(5 + 2 * i), A.add)
+        ts(w("m3", 0, 32), v("mcf"), s(6), A.is_ge, wk(i), A.mult)
+        if x == "B":
+            red(T3B, w("t2", 32, 64), A.max)
+            count_at(raw, T3B, s(7), 2 + i)
+            ts(w("m3", 32, 64), v("mc"), s(7), A.is_ge, wk(i), A.mult)
+        tr(w("t3", 8, 8 + n3), w("m3", 0, n3))
+        red(T4, w("t3", 7, 8 + n3), A.add)
+        count_at(raw, T4, s(20), i)
+        ts(w("t4", 7, 8), T4, LO, A.subtract, wk(8), A.add)
+        ts(w("m4", 0, 32), v("mcf"), s(20), A.is_ge, wk(2), A.mult)
+        if x == "A":
+            ts(w("t3", 40, 41), T3, wk(6), A.add)
+            red(T4B, w("t3", 8, 41), A.add)
+            count_at(raw, T4B, s(21), 2 + i)
+            ts(w("m4", 32, 64), v("mc"), s(21), A.is_ge, wk(2), A.mult)
+        tr(w("t4", 8, 8 + n4), w("m4", 0, n4))
+        red(T5, w("t4", 7, 8 + n4), A.add)
+        count_at(rel, T5, s(22), i)
+        ts(w("t5", 7, 8), T5, wk(9), A.add)
+        ts(w("m5"), v("mc"), s(22), A.is_ge, wk(3), A.mult)
+        tr(w("t5", 8, 40), w("m5"))
+        red(T6, w("t5", 7, 40), A.add)
+        count_at(rel, T6, s(23), i)
+        ts(s(24), T6, wk(10), A.add, LO, A.add)
+        if x == "A":
+            ts(c1("sc", 0), s(24), EV, A.mult)
+        else:
+            ts(c1("t6", 7), s(24), OD, A.mult, c1("sc", 0), A.add)
+        ts(v("m6", 16 * i, 16 * i + 16), v("mc", 0, 16), s(23), A.is_ge, wk(4), A.mult)
+        ts(w("row"), v("mc", 0, 16), s(23), A.is_ge, BIG, A.mult)
+        ts(s(25), s(23), EPS / 2, A.mult, 32 * EPS, A.add)
+        ts(v("m6", 32 + 16 * i, 48 + 16 * i), w("row"), s(25), A.add)
+
     new_run(0, 0)
-    constants(-1)
     new_run(0, 1)
-    constants(0)
     for k, e in enumerate(ROUNDS):
         partner = T.cores[rank ^ e]
-        mm(P0, v("qu"), v("su"), v("qx"), v("sx"))
-        mm(P1, v("qu"), v("su"), v("qx"), v("sx"))
-        ts(S(0), S(42), -1.0, A.mult, -64.0, A.add)
-        ts(S(1), S(43), S(0), A.is_gt, -2 * BIG, A.mult)
-        ts(v("m1", 0, 32), v("tab", 0, 32), S(1), A.add)
-        ts(v("m1", 32, 96), v("tab", 32, 96), S(1), A.add)
-        tr(v("tr1", 32, 64), v("m1", 0, 32))
-        tr(v("tr1", 64, 128), v("m1", 32, 96))
-        red(S(2), v("tr1", 31, 64), A.max)
-        count_at(S(2), S(3))
-        if k == 0:
-            constants(1)
-        red(c1("tr2", 96), v("tr1", 64, 96), A.max)
-        ts(S(4), S(2), -0.5, A.mult, S(2), A.max)
-        red(c1("tr2", 31), v("tr1", 96, 129), A.max)
-        ts(S(5), S(4), 2.0 ** -72, A.max, 0.125, A.mult)
-        ts(v("cand"), v("rat"), S(5), A.mult, S(2), A.add)
-        ts(v("cand2"), v("mc"), S(3), A.is_lt, -2 * BIG, A.mult)
-        for j in range(2):
-            tt(v("m2", 32 * j, 32 * j + 32), v("cand", 32 * j, 32 * j + 32), v("cand2", 32 * j, 32 * j + 32), A.add)
-        for j in range(2):
-            tr(v("tr2", 32 + 32 * j, 64 + 32 * j), v("m2", 32 * j, 32 * j + 32))
-        red(S(20), v("tr2", 31, 64), A.max)
-        RW = S(12)
-        for i in range(5):
-            thr, cnt = S(20 + i), S(30 + i)
-            count_at(thr, cnt)
-            if i == 0:
-                if k == 0:
-                    constants(2)
-                red(S(9), v("tr2", 64, 98), A.max)
-                for b in range(4):
-                    mm(v("b%d" % (2 + b), 0, C), v("qe", 128 * b, 128 * b + 128), v("se", 128 * b, 128 * b + 128), v("qx"), v("sx"))
-                ts(S(10), S(9), -0.5, A.mult, S(9), A.max)
-                ts(RW, thr, S(9), A.subtract)
-                ts(c1("steps", 5), S(10), 2.0 ** -72, A.max, 0.125, A.mult)
-                ts(c1("tr3", 32), RW, 1.0 / 16, A.mult, S(9), A.add)
-            else:
-                ts(c1("tr3", 32), RW, -15.0 / 16 * 16.0 ** -i, A.mult, thr, A.add)
-                if k == 0:
-                    act(v("ff", C * (i - 1), C * i), v("b%d" % (1 + i), 0, C), ACT.Copy)
-                    constants(i + 2)
-                else:
-                    cp(v("ff", C * (i - 1), C * i), v("b%d" % (1 + i), 0, C))
-            ts(v("m3"), v("mc", 0, 32), cnt, A.is_ge, c1("steps", 5 - i), A.mult)
-            if i == 0:
-                ts(v("steps", 0, 5), v("btab", 198, 215, 4), c1("steps", 5), A.mult)
-            if i == 1:
-                cp(c1("hb", 0), c1("steps", 0))
-            tr(v("tr3", 0, 32), v("m3"))
-            red(S(21 + i), v("tr3", 0, 33), A.add)
-        thr, cnt, GT, TH, NEED = S(25), S(35), c1("gs", C - 1), S(38), S(39)
-        count_at(thr, cnt)
-        if k == 0:
-            constants(7)
-        ts(v("ge"), P1, thr, A.is_gt)
-        ts(c1("tr4", 31), RW, -16.0 ** -5, A.mult, thr, A.add)
-        scan(v("gs"), v("ge"), v("ge"), 0.0, A.add, A.max)
-        ts(v("mlc"), v("ml"), cnt, A.subtract)
-        ts(v("m0c"), v("m0"), cnt, A.min, -192.0, A.add)
-        ts(v("m4", 0, 32), v("mlc"), GT, A.is_ge, c1("hb", 0), A.mult)
-        ts(c1("hb", 1), GT, -EPS, A.mult, K * EPS, A.add)
-        ts(v("m4", 64, 96), v("m0c"), GT, A.add, EPS, A.mult)
-        tr(v("tr4", 32, 64), v("m4", 0, 32))
-        ts(v("m4", 32, 64), v("mlc"), GT, A.is_ge, c1("hb", 1), A.mult)
-        red(TH, v("tr4", 31, 64), A.add)
-        tr(v("tr4", 64, 128), v("m4", 32, 96))
-        act(v("sig"), P0, ACT.Sign, bias=TH, scale=-1.0)
-        ts(hv("neq", 0), hv("b1", 0), TH, A.is_equal, -EPS, A.mult)
-        red(NEED, v("tr4", 64, 128), A.max)
-        ts(hv("neq", 1), hv("b1", 1), TH, A.is_equal, -EPS, A.mult)
+        for i in (0, 1, 6, 7):
+            mm(bank(i, C), blk("qu", i % 2), blk("su", i % 2), v("qx"), v("sx"))
+        for b in range(4):
+            mm(bank(2 + b, C), blk("qe", b), blk("se", b), v("qx"), v("sx"))
+            for h in range(2):
+                cp(v("ff", FW * b + H * h, FW * b + H * h + H), bank(2 + b, H * h, H * h + H))
+        for i, x in enumerate("AB"):
+            search(i, x)
+        for i in (0, 1):
+            mm(bank(i, C), v("qg"), v("sg"), v("qx"), v("sx"))
+        TH, NEED = c1("sc", 1), c1("sc", 2)
+        tr(v("t6", 8, 40), v("m6", 0, 32))
+        red(TH, v("t6", 7, 40), A.add)
+        tr(v("t6", 40, 72), v("m6", 32, 64))
+        red(NEED, v("t6", 40, 72), A.min)
+        M0 = [v("mt", h, 4 * H, 4) for h in range(2)]
+        for h in range(2):
+            act(hv("sig", h), bank(0, H * h, H * h + H), ACT.Sign, bias=TH, scale=-1.0)
+            ts(hv("neq", h), bank(1, H * h, H * h + H), TH, A.is_equal, -EPS, A.mult)
         scan(v("ns"), v("neq"), v("zb"), NEED, A.add, A.add)
-        M0 = [v("mt", 4 * H * h, 4 * H * (h + 1), 4) for h in range(2)]
         for h in range(2):
             tt(M0[h], hv("sig", h), hv("ns", h), A.is_le)
+        quant(v("qm"), v("sm"), v("mt"))
+        LL = c1("sc", 3)
+        e6 = lambda n, j, h: v(n, 84 * h + j, 84 * h + 84, 6)
         for h in range(2):
-            quant(hv("qm", h), hv("sm", h), v("mt", 4 * H * h, 4 * H * (h + 1)))
-            mm(v("b%d" % (6, 2)[h], 0, H), v("qc", 0, 128), v("scc", 0, 128), hv("qm", h), hv("sm", h))
-            mm(v("b%d" % (7, 3)[h], 0, H), v("qc", 128, 256), v("scc", 128, 256), hv("qm", h), hv("sm", h))
-        MC, NM = S(40), S(41)
-
-        def decode(h, step):
-            w = lambda n: v(n, 14 * h, 14 * h + 14)
-            t3 = lambda n, j: v(n, 42 * h + j, 42 * h + 42, 3)
-            if step == 0:
-                tt(w("x1"), v("cs", H * h + 14, H * h + H, 16), v("cs", H * h + 15, H * h + H, 16), A.max)
-            if step == 1:
-                ts(w("xi"), w("x1"), UNC, A.mult, 1024.0 * (2 * OFF + 513) + 1, A.add)
-            if step == 2:
-                ts(w("ai"), w("xi"), 10, A.logical_shift_right, 1022, A.bitwise_and)
-                ts(w("ni"), w("xi"), 1, A.bitwise_and)
-                ts(w("zi"), w("xi"), 2047, A.bitwise_and)
-            if step == 3:
-                tt(t3("tri", 2), w("zi"), w("ai"), A.add)
-                tt(t3("tri", 1), w("ni"), w("k2"), A.mult)
-                ts(t3("tri", 0), w("ai"), -1.0, A.mult, NM, A.add)
-            if step == 4:
-                scan(v("x3", 42 * h, 42 * h + 42), v("c3"), v("tri", 42 * h, 42 * h + 42), 0.0, A.min, A.max)
-            if step == 5:
-                ts(v("pos", 16 * h, 16 * h + 14), t3("x3", 2), MC, A.add, 0.5, A.mult)
-            if step == 6:
-                scat(v("t0"), v("pos", 16 * h, 16 * h + 14), hv("vs", h))
-
-        scan(hv("vs", 0), M0[0], hv("c1024", 0), -1024.0, A.add, A.add)
-        scan(hv("cap", 0), v("b6", 0, H), hv("zer", 0), OFF, A.add, A.add)
-        scan(hv("vs", 1), M0[1], hv("c1024", 1), c1("vs", H - 1), A.add, A.add)
-        scan(hv("vv", 0), v("b7", 0, H), hv("cap", 0), OFF, A.add, A.min)
-        scan(hv("cap", 1), v("b2", 0, H), hv("zer", 1), c1("cap", H - 1), A.add, A.add)
-        scan(hv("cs", 0), hv("csum", 0), hv("vv", 0), OFF, A.mult, A.add)
-        scan(hv("vv", 1), v("b3", 0, H), hv("cap", 1), c1("vv", H - 1), A.add, A.min)
-        act(NM, c1("vv", C - 1), ACT.Identity, bias=2 * OFF + 2049.5, scale=-2.0)
-        act(MC, c1("vv", C - 1), ACT.Identity, bias=0.5 - 2 * OFF - 1538.0, scale=2.0)
-        decode(0, 0)
-        scan(hv("cs", 1), hv("csum", 1), hv("vv", 1), c1("vv", H - 1), A.mult, A.add)
-        for step in range(1, 7):
-            decode(0, step)
-            decode(1, step - 1)
-        decode(1, 6)
-        scan(v("cs2"), v("cmul", 0, K), v("t0", 0, K), 0.0, A.mult, A.max)
-        ts(v("g1"), v("cs2", 15, K, 16), UNB, A.mult)
-        ts(v("gh"), v("g1"), 496, A.bitwise_and)
-        ts(v("gl"), v("g1"), 15, A.bitwise_and)
-        cp(v("bt", 0, 64, 4), v("gh"))
-        cp(v("bt", 1, 64, 4), v("gl"))
-        quant(v("qb"), v("sb"), v("bt"))
-        lb = (0, 1, 2, 3, 4, 6)
-        for s in range(6):
-            mm(v("b%d" % lb[s], 0, 128), v("qc", 336 - 16 * s, 464 - 16 * s), v("scc", 336 - 16 * s, 464 - 16 * s), v("qb"), v("sb"))
-        if k == 0:
-            ms(v("thf"), 1.0)
-        for s in range(2):
-            ts(v("loff", 16 * s, 16 * s + 16), v("b%d" % lb[s], 0, 16), -1.0, A.add)
-        src = "t0"
-        for s in range(6):
-            dst = "ta" if s % 2 == 0 else "tb"
-            cp(v(dst, 0, 128), v(src, 0, K), off=v("loff", 16 * s, 16 * s + 8))
-            act(v(dst, 128, K), v(src, 0, K), ACT.Copy, off=v("loff", 16 * s + 8, 16 * s + 16))
-            if s < 4:
-                ts(v("loff", 16 * s + 32, 16 * s + 48), v("b%d" % lb[s + 2], 0, 16), -1.0, A.add)
-            src = dst
+            on = lambda n, first: c1(n, H - 1) if h else first
+            mm(bank(6 + h, H), blk("qc", h), blk("scc", h), v("qm"), v("sm"))
+            scan(hv("vs", h), M0[h], hv("c1024", h), on("vs", -1024.0), A.add, A.add)
+            scan(hv("bw", h), hv("cmul", h), M0[h], 0.0, A.mult, A.max)
+            scan(hv("vw", h), hv("cmul", h), hv("vs", h), 0.0, A.mult, A.max)
+            scan(hv("dd", h), bank(6 + h, H), hv("zb", h), on("dd", 0.0), A.add, A.add)
+            scan(hv("ll", h), hv("dd", h), hv("zb", h), on("ll", 0.0), A.max, A.max)
+            scan(hv("cs", h), hv("csum", h), hv("ll", h), on("ll", 0.0), A.mult, A.add)
+        cp(LL, c1("ll", C - 1))
+        ts(v("q1", 0, 168, 6), v("bw", 15, C, 16), NB, A.mult)
+        ts(v("q1", 1, 168, 6), v("vw", 15, C, 16), UNB, A.mult)
         for h in range(2):
-            scan(v("cs3", 128 * h, 128 * h + 128), v("cmul", 0, 128), v(src, 128 * h, 128 * h + 128), 0.0, A.mult, A.max)
+            x14, x15 = v("cs", H * h + 14, H * h + H, 16), v("cs", H * h + 15, H * h + H, 16)
+            ts(e6("q0", 3, h), x14, N14, A.mult)
+            ts(e6("q0", 4, h), x15, N15, A.mult)
+            ts(e6("q1", 4, h), x14, S14, A.mult, LL, A.subtract)
+            ts(e6("q1", 5, h), x15, S15, A.mult, LL, A.subtract)
+            scan(v("x3", 84 * h, 84 * h + 84), v("q0", 84 * h, 84 * h + 84), v("q1", 84 * h, 84 * h + 84), 0.0, A.add, A.max)
+            ts(v("pos", 16 * h, 16 * h + 14), e6("x3", 5, h), 16.25, A.add)
+            scat(v("t0"), v("pos", 16 * h, 16 * h + 14), hv("vs", h))
+        tr(v("tq", 0, 576, 2), v("t0", 0, 288))
+        tr(v("tq", 33, 545, 2), v("t0", 16, 272))
+        for j in range(2):
+            cp(v("xi", 24 * j, 24 * j + 17), v("tq", 32 * j, 32 * j + 529, 33))
+            ts(v("xa", 24 * j, 24 * j + 17), v("xi", 24 * j, 24 * j + 17), 1023, A.bitwise_and)
+        for s, j, a, b, n, add in ((0, 0, 0, 0, 128, 15.0), (1, 1, 0, 32, 32, O2), (1, 1, 32, 64, 32, O2), (1, 1, 64, 96, 32, O2),
+                                   (2, 0, 32, 64, 32, O3), (2, 0, 64, 96, 32, O3), (3, 1, 0, 64, 64, O3), (4, 0, 32, 96, 32, O3)):
+            ts(v("loff", 18 * s, 18 * s + 17, p=(b, b + n)), v("xa", 24 * j, 24 * j + 17, p=(a, a + n)), part(add, (a, a + n)) if s else add, A.add)
+        q = (0, 32)
+        ts(v("l6a", p=q), v("xa", 25, 41, p=q), part(EV, q), A.mult, part(O3, q), A.add)
+        ts(v("l6b", p=q), v("xa", 24, 40, p=q), part(OD, q), A.mult)
+        tt(v("l6", p=q), v("l6a", p=q), v("l6b", p=q), A.add)
+        cp(v("loff", 90, 106, p=(96, 128)), v("l6", p=q))
+        ways = ((v("t0", 0, 288), "t0", 288), (v("t0", 0, 560), "ta", 0), (v("ta"), "tb", 0), (v("tb"), "ta", 0), (v("ta"), "tb", 0), (v("tb"), "ta", 0))
+        for s, (src, dst, o) in enumerate(ways):
+            n = 17 if s < 5 else 16
+            act(v(dst, o, o + 128), src, ACT.Copy, off=v("loff", 18 * s, 18 * s + 8))
+            cp(v(dst, o + 128, o + 16 * n), src, off=v("loff", 18 * s + 8, 18 * s + n))
         for h in range(2):
+            scan(blk("cs3", h), v("cmul", 0, 128), blk("ta", h), 0.0, A.mult, A.max)
             ts(v("offc", 8 * h, 8 * h + 8), v("cs3", 128 * h + 15, 128 * h + 128, 16), UNA, A.mult)
         qh, sh, ql, sl, arr = "qh%d" % k, "sh%d" % k, "ql%d" % k, "sl%d" % k, "arr%d" % k
         rid, pid, _ = topo.addr(partner)
         mask, ne = topo.mask(core, partner), len(topo.engines(core, partner))
-        banks = ((0, 1, 2, 3), (0, 4, 6, 7))
+
+        def send(to, what, reads, lands, arr=arr, pid=pid, rid=rid, mask=mask):
+            op("G", lambda: g.remote_dma(to, what, T.sem[arr], T.sem.snd, pid, rid, mask), [reads], [lands], 120, 3000, "bare")
+
         for h in range(2):
             lo, hi, off = 128 * h, 128 * h + 128, v("offc", 8 * h, 8 * h + 8)
             for b in range(2):
-                act(v("zt", 4 * lo + 2 + b, 4 * hi, 4), v("ff", C * (2 + b), C * (3 + b)), ACT.Copy, off=off)
-                cp(v("zt", 4 * lo + b, 4 * hi, 4), v("ff", C * b, C * (b + 1)), off=off)
-                if h == 1 and b == 0:
-                    quant(v("qz", 0, 128), v("sz", 0, 128), v("zt", 0, 512))
-                    for b2 in (0, 2, 1, 3):
-                        mm(v("b%d" % banks[0][b2], 0, 128), v("qw", 128 * b2, 128 * b2 + 128), v("sw", 128 * b2, 128 * b2 + 128), v("qz", 0, 128), v("sz", 0, 128))
-        quant(v("qz", 128, K), v("sz", 128, K), v("zt", 512, 4 * K))
-        ts(v("ht", 0, 512, 4), v("b0", 0, 128), 0.0, A.max, 0.015625, A.mult)
-        for b2 in (1, 3, 2, 0):
-            mm(v("b%d" % banks[1][b2], 0, 128), v("qw", 128 * b2, 128 * b2 + 128), v("sw", 128 * b2, 128 * b2 + 128), v("qz", 128, K), v("sz", 128, K))
-        ts(v("ht", 1, 512, 4), v("b1", 0, 128), 0.0, A.max, 0.015625, A.mult)
-        for h, b in ((0, 2), (0, 3), (1, 3), (1, 2)):
-            act(v("ht", 512 * h + b, 512 * h + 512, 4), v("b%d" % banks[h][b], 0, 128), ACT.Relu, scale=0.015625)
-        for h in range(2):
-            lo, hi = 128 * h, 128 * h + 128
-            ts(v("ht", 513 - h, 4 * K, 4), v("b%d" % banks[1][1 - h], 0, 128), 0.0, A.max, 0.015625, A.mult)
-            quant(v(qh, lo, hi), v(sh, lo, hi), v("ht", 4 * lo, 4 * hi))
-            wait("G", "sV", count["sV"])
-            g.remote_dma(T[ql][:, lo:hi].bitcast(dt.uint8), T[qh][:, lo:hi].bitcast(dt.uint8), T.sem[arr], T.sem.snd, pid, rid, mask)
-        g.remote_dma(T[sl][:], T[sh][:], T.sem[arr], T.sem.snd, pid, rid, mask)
+                act(v("zt", 4 * lo + 2 + b, 4 * hi, 4), v("ff", FW * (2 + b), FW * (2 + b) + C), ACT.Copy, off=off)
+                cp(v("zt", 4 * lo + b, 4 * hi, 4), v("ff", FW * b, FW * b + C), off=off)
+            quant(blk("qz", h), blk("sz", h), v("zt", 4 * lo, 4 * hi))
+            for b in (0, 2, 1, 3):
+                out, to = bank(4 * h + b, 128), v("ht", 4 * lo + b, 4 * hi, 4)
+                mm(out, blk("qw", b), blk("sw", b), blk("qz", h), blk("sz", h))
+                if b < 2:
+                    ts(to, out, 0.0, A.max, 0.015625, A.mult)
+                else:
+                    act(to, out, ACT.Relu, scale=0.015625)
+            quant(blk(qh, h), blk(sh, h), v("ht", 4 * lo, 4 * hi))
+            send(T[ql][:, lo:hi].bitcast(dt.uint8), T[qh][:, lo:hi].bitcast(dt.uint8), blk(qh, h), blk(ql, h))
+        send(T[sl][:], T[sh][:], v(sh), v(sl))
+        act(v("thf"), v("col1"), ACT.Copy)
         scat(v("thf"), v("offc"), v("kio"))
-        scan(v("cs4"), v("cmul", 0, C), v("thf"), 0.0, A.mult, A.max)
+        scan(v("cs4"), v("cmul"), v("thf"), 0.0, A.mult, A.max)
         ts(v("offt"), v("cs4", 15, C, 16), UNB, A.mult, -1.0, A.add)
-        if k == 0:
-            quant(v("qv"), v("sv"), v("vin"))
-        if k < 2:
-            ms(v("thf"), 1.0)
         if k == 2:
-            act(v("pb"), v(src), ACT.Identity, bias=1.5 * 2.0 ** 23, scale=EPS)
+            act(v("pb"), v("ta", 0, K), ACT.Identity, bias=1.5 * 2.0 ** 23, scale=EPS)
             act(v("pf"), v("pb"), ACT.Identity, bias=-1.5 * 2.0 ** 23)
             dma("Y", T.pl[:], T.pf[0:128:16, :], [v("pf")], [])
-        wait("P", arr, 3 * ne)
-
-        def gather_add(h, b):
+        op("P", lambda arr=arr, n=3 * ne: wait("P", arr, n), [v(ql), v(sl)], [v(ql), v(sl)], 0, -WAKE, "bare")
+        for b in range(4):
+            out = bank((0, 1, 6, 7)[b], K)
+            mm(out, blk("qe", b), blk("se", b), v(ql), v(sl))
+            tt(v("ff", FW * b + C, FW * b + FW), out, v("zt", b, 4 * K, 4), A.add)
+        for e2, b, h in (("S", 0, 0), ("S", 1, 0), ("V", 2, 0), ("V", 3, 0), ("S", 0, 1), ("S", 1, 1), ("S", 2, 1), ("V", 3, 1)):
             lo, hi = RUNS[h]
-            out, off = v("xt", 4 * lo + b, 4 * hi, 4), v("offt", lo // 16, hi // 16)
-            if b < 3:
-                tt(out, v("dp", 272 * b, 272 * b + 257), v("ff", C * b + lo, C * b + hi), A.add, off=off)
+            out, win, off = v("xt", 4 * lo + b, 4 * hi, 4), v("ff", FW * b, FW * b + FW), v("offt", lo // 16, hi // 16)
+            if e2 == "V":
+                cp(out, win, off=off)
             else:
-                tt(out, v("b5", lo, hi), v("d3", lo, hi), A.add)
-
-        for h in range(2):
-            mm(v("b%d" % (0, 3)[h], 0, 128), v("qe", 0, 128), v("se", 0, 128), v(ql, 128 * h, 128 * h + 128), v(sl, 128 * h, 128 * h + 128))
-        act(v("dp", 1, 129), v("b0", 0, 128), ACT.Copy)
-        cp(v("dp", 129, 257), v("b3", 0, 128))
-        for b in range(1, 4):
-            bank = v("b%d" % (0, 1, 6, 7)[b], 0, K)
-            mm(bank, v("qe", 128 * b, 128 * b + 128), v("se", 128 * b, 128 * b + 128), v(ql), v(sl))
-            act(v("dp", 272 * b + 1, 272 * b + 1 + K), bank, ACT.Copy)
-        for lo, hi in RUNS:
-            act(v("d3", lo, hi), v("dp", 272 * 3, 272 * 3 + 257), ACT.Copy, off=v("offt", lo // 16, hi // 16))
-        for h, b in ((0, 0), (0, 1), (0, 2), (1, 0), (0, 3), (1, 1)):
-            gather_add(h, b)
+                act(out, win, ACT.Copy, off=off)
         new_run(k + 1, 0)
-        gather_add(1, 2)
-        gather_add(1, 3)
         new_run(k + 1, 1)
 
+    issue()
     wait("G", "snd", 9 * ne)
     for i in range(ndma[0]):
         wait("G", "d%d" % i, 16)

@@ -12,20 +12,22 @@ SB = {
     "xt": (4 * C, BF), "qx": (C, Q4), "sx": (C, U8), "ff": (4 * FW, BF),
     "junk": (4 * C, BF), "spA": (C, F32), "spB": (C, F32), "sig": (C, BF), "neq": (C, BF), "ns": (C, BF),
     "mt": (4 * H, BF), "qm": (H, Q4), "sm": (H, U8), "dd": (C, BF), "ll": (C, BF), "bw": (C, BF),
-    "pos": (32, U16), "t0": (1200, F32), "ta": (272, F32), "tb": (272, F32), "tq": (576, F32), "q0": (168, F32), "q1": (168, F32),
+    "kb": (2, BF), "pos": (28, U16), "t0": (1200, F32), "ta": (272, F32), "tb": (272, F32), "tq": (576, F32), "q0": (168, F32), "q1": (168, F32),
     "loff": (108, U16), "offc": (16, U16), "thf": (C, F32), "offt": (28, U16), "pf": (K, F32),
     "zt": (4 * K, BF), "qz": (K, Q4), "sz": (K, U8), "ht": (4 * K, BF), "yo": (C, F32),
 }
 for _k in range(3):
     SB["qh%d" % _k], SB["sh%d" % _k], SB["ql%d" % _k], SB["sl%d" % _k] = (K, Q4), (K, U8), (K, Q4), (K, U8)
-LINE = {"s": 32, "m1": 64, "t1": 64, "cand": 128, "m2": 128, "t2": 128, "wk": 16, "m3": 64, "t3": 80, "m4": 64, "t4": 80, "m5": 32, "t5": 48, "row": 16}
+LINE = {"s": 32, "z0": 32, "m1": 32, "t1": 32, "u": 192, "cand": 128, "candt": 128, "m2": 32, "t2": 32, "wk": 16,
+        "m3": 64, "t3": 80, "m4": 64, "t4": 80, "m5": 32, "t5": 48}
 POOLS = {
     "kf": (F32, {"kc": 32, "dn": 16, "up": 16, "zer": 64, "lam": 64, "lt": 64, "fac": 32, "inc": 32, "edge": 40, "fx": 40, "fy": 40, "tab": 64,
+                 "tabt": 64, "mcz": 32, "c64": 16, "mch": 16,
                  "ca": 16, "cb": 16, "cd": 16, "ce": 16, "cf": 16, "mc": 32, "mcf": 32, "ratA": 128, "ratB": 128, "j64": 64, "krow": 16,
                  "i16": 32, "col": 32, "col1": C, "kio": K}),
     "ki": (I32, {"pint": 2, "rint": 2, "hint": 1, "qint": 1, "oui": 24}),
     "wf": (F32, dict([(n + x, w) for x in "AB" for n, w in LINE.items()],
-                     sc=8, m6=64, t6=80, vs=C, vw=C, cs=C, x3=168, l6a=16, l6b=16, l6=16, cs3=K, cs4=C, pb=K)),
+                     sc=8, m6=96, t6=104, u6=32, vs=C, vw=C, cs=C, x3=168, l6a=16, l6b=16, l6=16, cs3=K, cs4=C, pb=K)),
     "wi": (I32, {"xi": 48, "xa": 48}),
 }
 AT = {}
@@ -38,13 +40,13 @@ for _p, (_d, _m) in POOLS.items():
 SCRATCH = {n: ("sbuf", [128, w], d) for n, (w, d) in SB.items()}
 for _k in range(8):
     SCRATCH["b%d" % _k] = ("psum", [128, 512], F32)
-SEMAPHORES = ["sV", "sS", "sP", "sG", "snd", "arr0", "arr1", "arr2"] + ["d%d" % i for i in range(16)]
+SEMAPHORES = ["sV", "sS", "sP", "sG", "snd"] + ["arr%d%s" % (k, h) for k in range(3) for h in "ab"] + ["d%d" % i for i in range(16)]
 
 BIG = 2.0 ** 80
 EPS = 2.0 ** -10
 LOW = -2 ** 22
 WAKE = 240
-RUNS = ((0, 256), (256, C))
+RUNS = ((0, 224), (224, C))
 
 
 def rank_program(g, core, T, topo):
@@ -102,33 +104,41 @@ def rank_program(g, core, T, topo):
 
     def in_order():
         n = len(calls)
-        tail, users, left = [0] * n, [[] for _ in calls], [len(c[2]) for c in calls]
-        for i in range(n - 1, -1, -1):
-            tail[i] += calls[i][3] + calls[i][4]
-            for d in calls[i][2]:
-                tail[d] = max(tail[d], tail[i] + WAKE)
+        users = [[] for _ in calls]
+        for i, c in enumerate(calls):
+            for d in c[2]:
                 users[d].append(i)
-        ready, free, order = [0] * n, {e: 0 for e in Q}, []
-        todo = [i for i in range(n) if not left[i]]
-        while todo:
-            e = calls[min(todo, key=lambda i: max(ready[i], free[calls[i][0]]))][0]
-            mine = [i for i in todo if calls[i][0] == e]
-            t = max(free[e], min(ready[i] for i in mine))
-            x = max((i for i in mine if ready[i] <= t), key=lambda i: (tail[i], -i))
-            soon = [y for y in mine if t < ready[y] < t + calls[x][3]
-                    and max(ready[y] + tail[y], ready[y] + calls[y][3] + tail[x]) < max(t + calls[x][3] + tail[y], t + tail[x])]
-            if soon:
-                free[e] = min(ready[y] for y in soon)
-                continue
-            todo.remove(x)
-            order.append(x)
-            free[e] = t + calls[x][3]
-            for u in users[x]:
-                ready[u] = max(ready[u], free[e] + calls[x][4] + WAKE)
-                left[u] -= 1
-                if not left[u]:
-                    todo.append(u)
-        return order
+
+        def lag(d, i):
+            return 0 if calls[d][5] == calls[i][5] == "bare" and calls[d][0] == calls[i][0] else calls[d][4] + WAKE
+
+        def place(order, back):
+            start, busy = [0] * n, {e: [] for e in Q}
+            for i in order:
+                e, _, deps, cost, late, _ = calls[i]
+                if back:
+                    t = max([start[u] + calls[u][3] + lag(i, u) for u in users[i]] + [late])
+                else:
+                    t = max([start[d] + calls[d][3] + lag(d, i) for d in deps] + [0])
+                slots = busy[e]
+                k = len(slots)
+                while k and slots[k - 1][1] > t:
+                    k -= 1
+                while k < len(slots) and slots[k][0] < t + cost:
+                    t = max(t, slots[k][1])
+                    k += 1
+                slots.insert(k, (t, t + cost))
+                start[i] = t
+            return start
+
+        tail = [0] * n
+        for i in range(n - 1, -1, -1):
+            tail[i] = calls[i][3] + max([tail[u] + lag(i, u) for u in users[i]] + [calls[i][4]])
+        for _ in range(3):
+            start = place(sorted(range(n), key=lambda i: (-tail[i], i)), False)
+            back = place(sorted(range(n), key=lambda i: (-start[i] - calls[i][3], -i)), True)
+            tail = [back[i] + calls[i][3] for i in range(n)]
+        return sorted(range(n), key=lambda i: (start[i], i))
 
     def issue():
         mark = {}
@@ -235,7 +245,7 @@ def rank_program(g, core, T, topo):
     dma("Y", T.sw[:], T.ws[:], [v("xin")], [v("sw")])
     dma("Y", T.vin[:], T.v[:], [v("xin")], [v("vin")])
 
-    (RF, RM1, RP1, OD, EV, J, SG, FM, D0, MCF, UN0, UNA, UNB, NB, S14, S15, N14, N15, O2, O3, R0, RN) = [c1("kc", i) for i in range(22)]
+    (RF, RM1, RP1, OD, EV, J, SG, FM, D0, MCF, UN0, UNA, UNB, NB, U15, N14, N15, O2, O3, R0, RN) = [c1("kc", i) for i in range(21)]
     iota(v("pint"), [[15, 2]], 0, 1)
     iota(v("oui", 0, 16), [[16, 2], [32, 4], [0, 2]], 0)
     iota(v("oui", 16, 24), [[16, 8]], 0)
@@ -297,13 +307,17 @@ def rank_program(g, core, T, topo):
     ts(MCF, v("qint"), 0.5, A.is_lt, BIG, A.mult)
     ts(MCF, MCF, -64.0, A.add)
     ts(v("mcf"), v("zer", 0, 32), MCF, A.add)
+    ts(v("mcz"), v("mcf"), 0.5, A.add, 4096.0, A.min)
+    ms(v("mch"), -63.5)
+    ms(v("c64"), 64.0)
+    tr(v("tabt"), v("tab"))
     for x, n in (("A", 32), ("B", 64)):
         ts(v("rat" + x, 0, 64), v("j64"), 1.0 / n, A.mult)
         ms(v("rat" + x, 64, 96), 0.0)
         ms(v("rat" + x, 96, 128), 1.0)
     for j, (a, b) in enumerate(((0, 2 ** 18), (0, 2 ** 17), (0, 2 ** 12), (0, 2 ** 7), (0, 4),
                                 (2 ** 12 - 2 ** 18, -2 ** 18), (2 ** 12 - 2 ** 18, -2 ** 17), (2 ** 12 - 2 ** 17, -2 ** 17),
-                                (2 ** 7 - 2 ** 12, 2 ** 7 - 2 ** 12 - 3), (4 - 2 ** 7, 4 - 2 ** 7), (-4, -1))):
+                                (2 ** 7 - 2 ** 12, 2 ** 7 - 2 ** 12 - 3), (-4 - 2 ** 7, 0), (4, -125))):
         act(c1("krow", j), J, ACT.Identity, bias=float(b), scale=float(a))
     j16 = v("j64", 0, 16)
     ts(v("ca"), j16, RF, A.not_equal)
@@ -322,11 +336,12 @@ def rank_program(g, core, T, topo):
     ts(UNB, UN0, 2.0 ** -20, A.max)
     ts(UNA, UN0, 2.0 ** -20, A.max, EPS, A.mult)
     ts(NB, UN0, 2.0 ** -20, A.max, -4096.0, A.mult)
+    S14, S15 = c1("kb", 0), c1("kb", 1)
     ts(S14, R0, 2.0 ** -40, A.mult)
     ts(N14, R0, -2.0 ** -40, A.mult)
-    ts(S15, UN0, 256.0, A.mult, 2.0 ** -40, A.max)
-    ts(S15, S15, RN, A.mult)
-    ts(N15, S15, -1.0, A.mult)
+    ts(U15, UN0, 256.0, A.mult, 2.0 ** -40, A.max)
+    ts(S15, U15, RN, A.mult)
+    ts(N15, U15, RN, A.mult, -1.0, A.mult)
     for n, j, val in (("q0", 0, LOW), ("q0", 5, 0), ("q1", 2, LOW), ("q1", 3, LOW)):
         fill(v(n, j, 168, 6), val)
     ts(v("q0", 1, 168, 6), v("col", 0, 28), 1025.0, A.mult, 737.0, A.add)
@@ -367,24 +382,26 @@ def rank_program(g, core, T, topo):
         w = lambda n, a=0, b=None: v(n + x, a, b)
         wk = lambda j: c1("wk" + x, j)
         raw, rel = bank(i, C), v("sp" + x)
-        T2, NX, WP, T3, T3B, LO, HI, W, T4, T4B, T5, T6 = [s(j) for j in range(8, 20)]
+        WP, W, T4, T4B, T5, T6 = [s(j) for j in range(8, 14)]
         n3, n4 = 32 * (1 + i), 32 * (2 - i)
-        ts(s(2), s(0), -1.0, A.mult, MCF, A.add)
-        ts(s(3), s(1), s(2), A.is_gt, -2 * BIG, A.mult)
-        ts(w("m1"), v("tab"), s(3), A.add)
+        T2, NX, T3, T3B, LO, HI = [c1("u" + x, 32 * j + 31) for j in range(6)]
+
+        def choose(j, z, row):
+            scan(w("u", 32 * j, 32 * j + 32), z, row, 0.0, A.max, A.min)
+
+        ts(w("z0"), v("mcz"), s(0), A.subtract)
+        ts(w("m1"), w("z0"), s(1), A.subtract, BIG, A.mult)
         tr(w("t1"), w("m1"))
-        red(T2, w("t1", 0, 32), A.max)
-        red(NX, w("t1", 32, 64), A.max)
+        choose(0, w("t1"), v("tabt", 0, 32))
+        choose(1, w("t1"), v("tabt", 32, 64))
         count_at(raw, T2, s(4), i)
         ts(WP, NX, T2, A.subtract)
         ts(w("cand"), v("rat" + x), WP, A.mult, T2, A.add)
-        ts(s(5), s(4), MCF, A.is_gt, -2 * BIG, A.mult)
-        for a in (0, 64):
-            ts(w("m2", a, a + 64), w("cand", a, a + 64), s(5), A.add)
-            tr(w("t2", a, a + 64), w("m2", a, a + 64))
-        red(T3, w("t2", 0, 32), A.max)
-        red(LO, w("t2", 64, 96), A.max)
-        red(HI, w("t2", 96, 128), A.max)
+        tr(w("candt"), w("cand"))
+        ts(w("m2"), v("mcz"), s(4), A.subtract, BIG, A.mult)
+        tr(w("t2"), w("m2"))
+        for j in (0, 1, 2, 3) if x == "B" else (0, 2, 3):
+            choose(2 + j, w("t2"), w("candt", 32 * j, 32 * j + 32))
         ts(W, HI, LO, A.subtract, 2.0 ** -23, A.mult)
         ts(w("wk", 0, 11), v("krow", 0, 11), W, A.mult)
         for h in range(2):
@@ -393,7 +410,6 @@ def rank_program(g, core, T, topo):
         ts(w("t3", 7, 8), T3, wk(5 + 2 * i), A.add)
         ts(w("m3", 0, 32), v("mcf"), s(6), A.is_ge, wk(i), A.mult)
         if x == "B":
-            red(T3B, w("t2", 32, 64), A.max)
             count_at(raw, T3B, s(7), 2 + i)
             ts(w("m3", 32, 64), v("mc"), s(7), A.is_ge, wk(i), A.mult)
         tr(w("t3", 8, 8 + n3), w("m3", 0, n3))
@@ -420,9 +436,8 @@ def rank_program(g, core, T, topo):
         else:
             ts(c1("t6", 7), s(24), OD, A.mult, c1("sc", 0), A.add)
         ts(v("m6", 16 * i, 16 * i + 16), v("mc", 0, 16), s(23), A.is_ge, wk(4), A.mult)
-        ts(w("row"), v("mc", 0, 16), s(23), A.is_ge, BIG, A.mult)
-        ts(s(25), s(23), EPS / 2, A.mult, 32 * EPS, A.add)
-        ts(v("m6", 32 + 16 * i, 48 + 16 * i), w("row"), s(25), A.add)
+        ts(v("m6", 32 + 16 * i, 48 + 16 * i), v("mch"), s(23), A.subtract, BIG, A.mult)
+        ts(v("m6", 64 + 16 * i, 80 + 16 * i), v("c64"), s(23), A.add, EPS / 2, A.mult)
 
     new_run(0, 0)
     new_run(0, 1)
@@ -432,17 +447,16 @@ def rank_program(g, core, T, topo):
             mm(bank(i, C), blk("qu", i % 2), blk("su", i % 2), v("qx"), v("sx"))
         for b in range(4):
             mm(bank(2 + b, C), blk("qe", b), blk("se", b), v("qx"), v("sx"))
-            for h in range(2):
-                cp(v("ff", FW * b + H * h, FW * b + H * h + H), bank(2 + b, H * h, H * h + H))
+            act(v("ff", FW * b, FW * b + C), bank(2 + b, C), ACT.Copy)
         for i, x in enumerate("AB"):
             search(i, x)
         for i in (0, 1):
             mm(bank(i, C), v("qg"), v("sg"), v("qx"), v("sx"))
-        TH, NEED = c1("sc", 1), c1("sc", 2)
+        TH, NEED = c1("sc", 1), c1("u6", 31)
         tr(v("t6", 8, 40), v("m6", 0, 32))
         red(TH, v("t6", 7, 40), A.add)
-        tr(v("t6", 40, 72), v("m6", 32, 64))
-        red(NEED, v("t6", 40, 72), A.min)
+        tr(v("t6", 40, 104), v("m6", 32, 96))
+        scan(v("u6"), v("t6", 40, 72), v("t6", 72, 104), 0.0, A.min, A.max)
         M0 = [v("mt", h, 4 * H, 4) for h in range(2)]
         for h in range(2):
             act(hv("sig", h), bank(0, H * h, H * h + H), ACT.Sign, bias=TH, scale=-1.0)
@@ -451,8 +465,6 @@ def rank_program(g, core, T, topo):
         for h in range(2):
             tt(M0[h], hv("sig", h), hv("ns", h), A.is_le)
         quant(v("qm"), v("sm"), v("mt"))
-        LL = c1("sc", 3)
-        e6 = lambda n, j, h: v(n, 84 * h + j, 84 * h + 84, 6)
         for h in range(2):
             on = lambda n, first: c1(n, H - 1) if h else first
             mm(bank(6 + h, H), blk("qc", h), blk("scc", h), v("qm"), v("sm"))
@@ -462,18 +474,17 @@ def rank_program(g, core, T, topo):
             scan(hv("dd", h), bank(6 + h, H), hv("zb", h), on("dd", 0.0), A.add, A.add)
             scan(hv("ll", h), hv("dd", h), hv("zb", h), on("ll", 0.0), A.max, A.max)
             scan(hv("cs", h), hv("csum", h), hv("ll", h), on("ll", 0.0), A.mult, A.add)
-        cp(LL, c1("ll", C - 1))
-        ts(v("q1", 0, 168, 6), v("bw", 15, C, 16), NB, A.mult)
-        ts(v("q1", 1, 168, 6), v("vw", 15, C, 16), UNB, A.mult)
-        for h in range(2):
-            x14, x15 = v("cs", H * h + 14, H * h + H, 16), v("cs", H * h + 15, H * h + H, 16)
-            ts(e6("q0", 3, h), x14, N14, A.mult)
-            ts(e6("q0", 4, h), x15, N15, A.mult)
-            ts(e6("q1", 4, h), x14, S14, A.mult, LL, A.subtract)
-            ts(e6("q1", 5, h), x15, S15, A.mult, LL, A.subtract)
-            scan(v("x3", 84 * h, 84 * h + 84), v("q0", 84 * h, 84 * h + 84), v("q1", 84 * h, 84 * h + 84), 0.0, A.add, A.max)
-            ts(v("pos", 16 * h, 16 * h + 14), e6("x3", 5, h), 16.25, A.add)
-            scat(v("t0"), v("pos", 16 * h, 16 * h + 14), hv("vs", h))
+        e6 = lambda n, j: v(n, j, 168, 6)
+        x14, x15, LL = v("cs", 14, C, 16), v("cs", 15, C, 16), c1("ll", C - 1)
+        ts(e6("q1", 0), v("bw", 15, C, 16), NB, A.mult)
+        ts(e6("q1", 1), v("vw", 15, C, 16), UNB, A.mult)
+        ts(e6("q0", 3), x14, N14, A.mult)
+        ts(e6("q0", 4), x15, N15, A.mult)
+        ts(e6("q1", 4), x14, S14, A.mult, LL, A.subtract)
+        ts(e6("q1", 5), x15, S15, A.mult, LL, A.subtract)
+        scan(v("x3"), v("q0"), v("q1"), 0.0, A.add, A.max)
+        ts(v("pos"), e6("x3", 5), 16.25, A.add)
+        scat(v("t0"), v("pos"), v("vs"))
         tr(v("tq", 0, 576, 2), v("t0", 0, 288))
         tr(v("tq", 33, 545, 2), v("t0", 16, 272))
         for j in range(2):
@@ -499,8 +510,8 @@ def rank_program(g, core, T, topo):
         rid, pid, _ = topo.addr(partner)
         mask, ne = topo.mask(core, partner), len(topo.engines(core, partner))
 
-        def send(to, what, reads, lands, arr=arr, pid=pid, rid=rid, mask=mask):
-            op("G", lambda: g.remote_dma(to, what, T.sem[arr], T.sem.snd, pid, rid, mask), [reads], [lands], 120, 3000, "bare")
+        def send(to, what, reads, lands, cost, arr, pid=pid, rid=rid, mask=mask):
+            op("G", lambda: g.remote_dma(to, what, T.sem[arr], T.sem.snd, pid, rid, mask), [reads], [lands, c1("sc", 7)], cost, 2200, "bare")
 
         for h in range(2):
             lo, hi, off = 128 * h, 128 * h + 128, v("offc", 8 * h, 8 * h + 8)
@@ -516,8 +527,8 @@ def rank_program(g, core, T, topo):
                 else:
                     act(to, out, ACT.Relu, scale=0.015625)
             quant(blk(qh, h), blk(sh, h), v("ht", 4 * lo, 4 * hi))
-            send(T[ql][:, lo:hi].bitcast(dt.uint8), T[qh][:, lo:hi].bitcast(dt.uint8), blk(qh, h), blk(ql, h))
-        send(T[sl][:], T[sh][:], v(sh), v(sl))
+            send(T[ql][:, lo:hi].bitcast(dt.uint8), T[qh][:, lo:hi].bitcast(dt.uint8), blk(qh, h), blk(ql, h), 800, arr + "ab"[h])
+            send(T[sl][:, lo:hi], T[sh][:, lo:hi], blk(sh, h), blk(sl, h), 200, arr + "ab"[h])
         act(v("thf"), v("col1"), ACT.Copy)
         scat(v("thf"), v("offc"), v("kio"))
         scan(v("cs4"), v("cmul"), v("thf"), 0.0, A.mult, A.max)
@@ -526,11 +537,13 @@ def rank_program(g, core, T, topo):
             act(v("pb"), v("ta", 0, K), ACT.Identity, bias=1.5 * 2.0 ** 23, scale=EPS)
             act(v("pf"), v("pb"), ACT.Identity, bias=-1.5 * 2.0 ** 23)
             dma("Y", T.pl[:], T.pf[0:128:16, :], [v("pf")], [])
-        op("P", lambda arr=arr, n=3 * ne: wait("P", arr, n), [v(ql), v(sl)], [v(ql), v(sl)], 0, -WAKE, "bare")
-        for b in range(4):
-            out = bank((0, 1, 6, 7)[b], K)
-            mm(out, blk("qe", b), blk("se", b), v(ql), v(sl))
-            tt(v("ff", FW * b + C, FW * b + FW), out, v("zt", b, 4 * K, 4), A.add)
+        for h in range(2):
+            got = [blk(ql, h), blk(sl, h)]
+            op("P", lambda arr=arr + "ab"[h], n=2 * ne: wait("P", arr, n), got, got, 1, -WAKE, "bare")
+            for b in range(4):
+                out = bank(4 * h + b, 128)
+                mm(out, blk("qe", b), blk("se", b), *got)
+                tt(v("ff", FW * b + C + 128 * h, FW * b + C + 128 * h + 128), out, v("zt", 512 * h + b, 512 * h + 512, 4), A.add)
         for e2, b, h in (("S", 0, 0), ("S", 1, 0), ("V", 2, 0), ("V", 3, 0), ("S", 0, 1), ("S", 1, 1), ("S", 2, 1), ("V", 3, 1)):
             lo, hi = RUNS[h]
             out, win, off = v("xt", 4 * lo + b, 4 * hi, 4), v("ff", FW * b, FW * b + FW), v("offt", lo // 16, hi // 16)
@@ -542,7 +555,7 @@ def rank_program(g, core, T, topo):
         new_run(k + 1, 1)
 
     issue()
-    wait("G", "snd", 9 * ne)
+    wait("G", "snd", 12 * ne)
     for i in range(ndma[0]):
         wait("G", "d%d" % i, 16)
     for s in count:

@@ -10,11 +10,11 @@ SB = {
     "ou": (24, U16), "r16": (28, U16), "et": (516, BF), "qe": (512, Q4), "se": (512, U8),
     "ct": (516, BF), "qc": (256, Q4), "scc": (256, U8), "zb": (C, BF), "c1024": (C, BF), "m16": (32, BF), "cmul": (C, BF), "csum": (C, BF),
     "xt": (4 * C, BF), "qx": (C, Q4), "sx": (C, U8), "ff": (4 * FW, BF),
-    "junk": (4 * C, BF), "spA": (C, F32), "spB": (C, F32), "sig": (C, BF), "neq": (C, BF), "ns": (C, BF),
+    "junk": (4 * C, BF), "spA": (C, F32), "spB": (C, F32), "near": (C, BF), "sig": (C, BF), "neq": (C, BF), "ns": (C, BF),
     "mt": (4 * H, BF), "qm": (H, Q4), "sm": (H, U8), "dd": (C, BF), "ll": (C, BF), "bw": (C, BF),
-    "kb": (2, BF), "pos": (28, U16), "t0": (1200, F32), "ta": (272, F32), "tb": (272, F32), "tq": (576, F32), "q0": (168, F32), "q1": (168, F32),
+    "kb": (2, BF), "pos": (28, U16), "ti": (1200, I32), "t0": (560, F32), "ta": (272, F32), "tb": (272, F32), "tq": (576, I32), "q0": (168, F32), "q1": (168, F32),
     "loff": (108, U16), "offc": (16, U16), "thf": (C, F32), "offt": (28, U16), "pf": (K, F32),
-    "zt": (4 * K, BF), "qz": (K, Q4), "sz": (K, U8), "ht": (4 * K, BF), "yo": (C, F32),
+    "zt": (4 * K, BF), "qz": (128, Q4), "sz": (128, U8), "qp": (128, Q4), "sp": (128, U8), "ht": (4 * K, BF), "yo": (C, F32),
 }
 for _k in range(3):
     SB["qh%d" % _k], SB["sh%d" % _k], SB["ql%d" % _k], SB["sl%d" % _k] = (K, Q4), (K, U8), (K, Q4), (K, U8)
@@ -28,7 +28,7 @@ POOLS = {
     "ki": (I32, {"pint": 2, "rint": 2, "hint": 1, "qint": 1, "oui": 24}),
     "wf": (F32, dict([(n + x, w) for x in "AB" for n, w in LINE.items()],
                      sc=8, m6=96, t6=104, u6=32, vs=C, vw=C, cs=C, x3=168, l6a=16, l6b=16, l6=16, cs3=K, cs4=C, pb=K)),
-    "wi": (I32, {"xi": 48, "xa": 48}),
+    "wi": (I32, {"xa": 48}),
 }
 AT = {}
 for _p, (_d, _m) in POOLS.items():
@@ -40,13 +40,14 @@ for _p, (_d, _m) in POOLS.items():
 SCRATCH = {n: ("sbuf", [128, w], d) for n, (w, d) in SB.items()}
 for _k in range(8):
     SCRATCH["b%d" % _k] = ("psum", [128, 512], F32)
-SEMAPHORES = ["sV", "sS", "sP", "sG", "snd"] + ["arr%d%s" % (k, h) for k in range(3) for h in "ab"] + ["d%d" % i for i in range(16)]
+SEMAPHORES = ["sV", "sS", "sP", "sG", "snd"] + ["arr%d%s" % (k, h) for k in range(3) for h in "ab"] + ["d%d" % i for i in range(17)]
 
 BIG = 2.0 ** 80
 EPS = 2.0 ** -10
 LOW = -2 ** 22
 WAKE = 240
-RUNS = ((0, 224), (224, C))
+RUNS = ((0, 224, "SSVV"), (224, C, "SSSV"))
+LAST = ((0, 160, "SSVV"), (160, 320, "SSSV"), (320, C, "SSVV"))
 
 
 def rank_program(g, core, T, topo):
@@ -60,7 +61,8 @@ def rank_program(g, core, T, topo):
     clock = {}
     log = {}
     calls = []
-    ndma = [0]
+    soft = set()
+    ndma, sent = [0], [None]
 
     def v(n, a=0, b=None, s=1, p=(0, 128)):
         buf, o, w = AT[n] if n in AT else (n, 0, T[n].shape[1])
@@ -87,8 +89,10 @@ def rank_program(g, core, T, topo):
             if known[e].get(s2, 0) < v2:
                 known[e][s2] = v2
 
-    def op(e, call, reads, writes, cost, late=0, kind="calc"):
-        deps = set()
+    def op(e, call, reads, writes, cost, late=0, kind="calc", behind=None):
+        if behind is not None:
+            soft.add((behind, len(calls)))
+        deps = set() if behind is None else {behind}
         both = [(x, False) for x in reads] + [(x, True) for x in writes]
         for view, wr in both:
             psum = view[1][0] == "b" and view[1][1:].isdigit()
@@ -110,7 +114,7 @@ def rank_program(g, core, T, topo):
                 users[d].append(i)
 
         def lag(d, i):
-            return 0 if calls[d][5] == calls[i][5] == "bare" and calls[d][0] == calls[i][0] else calls[d][4] + WAKE
+            return 0 if (d, i) in soft else calls[d][4] + WAKE
 
         def place(order, back):
             start, busy = [0] * n, {e: [] for e in Q}
@@ -145,7 +149,7 @@ def rank_program(g, core, T, topo):
         for i in in_order():
             e, call, deps, _, _, kind = calls[i]
             for d in deps:
-                if d in mark:
+                if d in mark and (d, i) not in soft:
                     wait(e, *mark[d])
             if kind == "bare":
                 call()
@@ -181,9 +185,9 @@ def rank_program(g, core, T, topo):
     def tt(o, a, b, op0):
         op("V", lambda: g.vector.tensor_tensor(o[0], a[0], b[0], op0), aps(a, b), [o], max(64, size(o)))
 
-    def cp(o, i, off=None):
+    def cp(o, i, off=None, behind=None):
         src = i[0].indirect(off[0]) if off else i[0]
-        op("V", lambda: g.vector.tensor_copy(o[0], src), aps(i, off), [o], 60 + 1.5 * size(o) if off else wide(o, i))
+        op("V", lambda: g.vector.tensor_copy(o[0], src), aps(i, off), [o], 60 + 1.5 * size(o) if off else wide(o, i), behind=behind)
 
     def pick(o, i, off):
         op("V", lambda: g.vector.tensor_copy(o[0].bitcast(dt.uint32), i[0].bitcast(dt.uint32).indirect(off[0])), [i, off], [o], 60 + 1.5 * size(o))
@@ -191,8 +195,8 @@ def rank_program(g, core, T, topo):
     def scat(o, off, i):
         op("V", lambda: g.vector.tensor_copy(o[0].indirect(off[0]), i[0]), [i, off], [o], 60 + 3.5 * size(i))
 
-    def scan(o, d0, d1, init, op0, op1):
-        op("V", lambda: g.vector.tensor_tensor_scan(o[0], d0[0], d1[0], ap(init), op0, op1), aps(d0, d1, init), [o], wide(o, d0, d1))
+    def scan(o, d0, d1, init, op0, op1, after=None):
+        op("V", lambda: g.vector.tensor_tensor_scan(o[0], d0[0], d1[0], ap(init), op0, op1), aps(d0, d1, init, after), [o], wide(o, d0, d1))
 
     def red(o, i, op0):
         op("V", lambda: g.vector.tensor_reduce(o[0], i[0], AxisListType.X, op0), [i], [o], max(64, size(i)))
@@ -209,7 +213,7 @@ def rank_program(g, core, T, topo):
     def mm(o, lq, ls, rq, rs):
         op("P", lambda: g.tensor.matmul_mx(o[0], lq[0], ls[0], rq[0], rs[0], True, True), [lq, ls, rq, rs], [o], 16 + size(o))
 
-    def act(o, i, func, bias=None, scale=None, acc=None, off=None):
+    def act(o, i, func, bias=None, scale=None, acc=None, off=None, after=None):
         src = i[0].indirect(off[0]) if off else i[0]
         kw = {}
         if bias is not None:
@@ -218,10 +222,11 @@ def rank_program(g, core, T, topo):
             kw["scale"] = ap(scale)
         if acc is not None:
             kw["accum_out"] = acc[0]
-        op("S", lambda: g.scalar.activation(o[0], src, func, **kw), aps(i, bias, scale, off), aps(o, acc), 80 + max(64, size(o)) * (1.5 if off else 1))
+        op("S", lambda: g.scalar.activation(o[0], src, func, **kw), aps(i, bias, scale, off, after), aps(o, acc),
+           80 + max(64, size(o)) * (1.5 if off else 1))
 
     def iota(o, pat, base, cm=0):
-        if o[1] in POOLS["ki"][1]:
+        if o[1] in POOLS["ki"][1] or o[1] == "ti":
             op("G", lambda: g.iota(o[0], pat, base, cm), [], [o], 160 + 2 * size(o))
         else:
             op("G", lambda: g.iota(o[0], pat, base, cm, allow_small_or_imprecise_dtypes=True), [], [o], 160 + 2 * size(o))
@@ -239,13 +244,13 @@ def rank_program(g, core, T, topo):
     bank = lambda i, a, b=None: v("b%d" % i, 0, a) if b is None else v("b%d" % i, a, b)
     blk = lambda n, i: v(n, 128 * i, 128 * i + 128)
     dma("S", T.uin[:], T.u[:], [], [v("uin")])
-    for a, b in RUNS:
+    for a, b, _ in RUNS:
         dma("Y", T.xin[:, 4 * a:4 * b], T.x[:, 4 * a:4 * b], [], [v("xin", 4 * a, 4 * b)], 2000 + 3 * b)
     dma("Y", T.qw[:].bitcast(dt.uint8), T.wc[:], [v("xin")], [v("qw")])
     dma("Y", T.sw[:], T.ws[:], [v("xin")], [v("sw")])
     dma("Y", T.vin[:], T.v[:], [v("xin")], [v("vin")])
 
-    (RF, RM1, RP1, OD, EV, J, SG, FM, D0, MCF, UN0, UNA, UNB, NB, U15, N14, N15, O2, O3, R0, RN) = [c1("kc", i) for i in range(21)]
+    (RF, RM1, RP1, OD, EV, J, SG, FM, D0, MCF, UN0, UNA, UNB, NB, U15, N14, N15, O2, O3, R0, RN, NOD) = [c1("kc", i) for i in range(22)]
     iota(v("pint"), [[15, 2]], 0, 1)
     iota(v("oui", 0, 16), [[16, 2], [32, 4], [0, 2]], 0)
     iota(v("oui", 16, 24), [[16, 8]], 0)
@@ -263,6 +268,7 @@ def rank_program(g, core, T, topo):
     cp(J, v("qint"))
     ts(RP1, c1("rint", 0), 1.0, A.add)
     ts(OD, v("hint"), 1.0 / 16, A.mult)
+    ts(NOD, v("hint"), -1.0 / 16, A.mult)
     ts(EV, v("hint"), -1.0 / 16, A.mult, 1.0, A.add)
     ts(v("col"), v("i16"), RF, A.add)
     ts(v("r16"), v("zer", 0, 28), RF, A.add)
@@ -278,9 +284,9 @@ def rank_program(g, core, T, topo):
         fill(v("mt", 2 + t, 4 * H, 4), 0)
     cp(v("ou"), v("oui"))
     quant(v("qu0"), v("su0"), v("uin"))
-    for q, s, off in (("qu", "su", v("ou", 0, 16)), ("qg", "sg", v("ou", 16, 24))):
-        pick(v(q), v("qu0"), off)
-        act(v(s), v("su0"), ACT.Copy, off=off)
+    for i, (q, s) in enumerate(((blk("qu", 0), blk("su", 0)), (blk("qu", 1), blk("su", 1)), (v("qg"), v("sg")))):
+        pick(q, v("qu0"), v("ou", 8 * i, 8 * i + 8))
+        act(s, v("su0"), ACT.Copy, off=v("ou", 8 * i, 8 * i + 8))
     quant(v("qv"), v("sv"), v("vin"))
     ms(v("dn"), 2.0 ** -8)
     ms(v("up"), 2.0 ** 8)
@@ -317,7 +323,7 @@ def rank_program(g, core, T, topo):
         ms(v("rat" + x, 96, 128), 1.0)
     for j, (a, b) in enumerate(((0, 2 ** 18), (0, 2 ** 17), (0, 2 ** 12), (0, 2 ** 7), (0, 4),
                                 (2 ** 12 - 2 ** 18, -2 ** 18), (2 ** 12 - 2 ** 18, -2 ** 17), (2 ** 12 - 2 ** 17, -2 ** 17),
-                                (2 ** 7 - 2 ** 12, 2 ** 7 - 2 ** 12 - 3), (-4 - 2 ** 7, 0), (4, -125))):
+                                (2 ** 7 - 2 ** 12, 2 ** 7 - 2 ** 12 - 3), (-4 - 2 ** 7, 0), (-2 ** 7, 3 - 2 ** 7))):
         act(c1("krow", j), J, ACT.Identity, bias=float(b), scale=float(a))
     j16 = v("j64", 0, 16)
     ts(v("ca"), j16, RF, A.not_equal)
@@ -347,6 +353,7 @@ def rank_program(g, core, T, topo):
     ts(v("q0", 1, 168, 6), v("col", 0, 28), 1025.0, A.mult, 737.0, A.add)
     ts(v("q0", 2, 168, 6), v("col", 0, 28), -1024.0, A.mult, -1.0, A.add)
     for a in (0, 272):
+        fill(v("ti", a, a + 16), 1)
         fill(v("t0", a, a + 16), 1)
     ts(O2, OD, 272.0, A.mult, 15.0, A.add)
     ts(O3, EV, 16.0, A.mult, -1.0, A.add)
@@ -358,8 +365,7 @@ def rank_program(g, core, T, topo):
     def count_at(src, thr, c, slot):
         act(v("junk", C * slot, C * slot + size(src)), src, ACT.Sign, bias=thr, scale=-1.0, acc=c)
 
-    def new_run(k, h):
-        a, b = RUNS[h]
+    def new_run(k, h, a, b):
         quant(v("qx", a, b), v("sx", a, b), v("xin" if k == 0 else "xt", 4 * a, 4 * b))
         if k < 3:
             for i, x in enumerate("AB"):
@@ -369,13 +375,13 @@ def rank_program(g, core, T, topo):
             out = bank(2 + 2 * h, b - a)
             mm(out, v("qv"), v("sv"), v("qx", a, b), v("sx", a, b))
             dma("Y", T.oc[:, 4 * a:4 * b], T.qx[:, a:b].bitcast(dt.uint8), [v("qx", a, b)], [])
-            if h == 1:
+            if b == C:
                 for i in range(4):
                     dma("YS"[i % 2], T.osc[4 * i:4 * i + 4, :], T.sx[32 * i:32 * i + 4, :], [v("sx")], [])
                 cp(v("yo", a, b), out)
             else:
                 act(v("yo", a, b), out, ACT.Copy)
-            dma("SY"[h], T.y[:, a:b], T.yo[:, a:b], [v("yo", a, b)], [])
+            dma("SY"[b == C], T.y[:, a:b], T.yo[:, a:b], [v("yo", a, b)], [])
 
     def search(i, x):
         s = lambda j: c1("s" + x, j)
@@ -426,43 +432,56 @@ def rank_program(g, core, T, topo):
         red(T5, w("t4", 7, 8 + n4), A.add)
         count_at(rel, T5, s(22), i)
         ts(w("t5", 7, 8), T5, wk(9), A.add)
+        ts(w("t5", 40, 41), T5, wk(10), A.add, LO, A.add)
         ts(w("m5"), v("mc"), s(22), A.is_ge, wk(3), A.mult)
         tr(w("t5", 8, 40), w("m5"))
         red(T6, w("t5", 7, 40), A.add)
+        red(s(24), w("t5", 8, 41), A.add)
         count_at(rel, T6, s(23), i)
-        ts(s(24), T6, wk(10), A.add, LO, A.add)
         if x == "A":
-            ts(c1("sc", 0), s(24), EV, A.mult)
+            ts(c1("sc", 0), s(24), EV, A.mult, -1.0, A.mult)
         else:
-            ts(c1("t6", 7), s(24), OD, A.mult, c1("sc", 0), A.add)
+            ts(c1("sc", 2), s(24), NOD, A.mult, c1("sc", 0), A.add)
         ts(v("m6", 16 * i, 16 * i + 16), v("mc", 0, 16), s(23), A.is_ge, wk(4), A.mult)
         ts(v("m6", 32 + 16 * i, 48 + 16 * i), v("mch"), s(23), A.subtract, BIG, A.mult)
         ts(v("m6", 64 + 16 * i, 80 + 16 * i), v("c64"), s(23), A.add, EPS / 2, A.mult)
 
-    new_run(0, 0)
-    new_run(0, 1)
+    def layer(h, qz, sz, qh, sh):
+        for b in (0, 2, 1, 3):
+            out, to = bank(4 * h + b, 128), v("ht", 512 * h + b, 512 * h + 512, 4)
+            mm(out, blk("qw", b), blk("sw", b), qz, sz)
+            if b < 2:
+                ts(to, out, 0.0, A.max, 0.015625, A.mult)
+            else:
+                act(to, out, ACT.Relu, scale=0.015625)
+        quant(qh, sh, v("ht", 512 * h, 512 * h + 512))
+
+    for h, (a, b, _) in enumerate(RUNS):
+        new_run(0, h, a, b)
     for k, e in enumerate(ROUNDS):
         partner = T.cores[rank ^ e]
         for i in (0, 1, 6, 7):
             mm(bank(i, C), blk("qu", i % 2), blk("su", i % 2), v("qx"), v("sx"))
         for b in range(4):
             mm(bank(2 + b, C), blk("qe", b), blk("se", b), v("qx"), v("sx"))
-            act(v("ff", FW * b, FW * b + C), bank(2 + b, C), ACT.Copy)
         for i, x in enumerate("AB"):
             search(i, x)
-        for i in (0, 1):
-            mm(bank(i, C), v("qg"), v("sg"), v("qx"), v("sx"))
+        mm(bank(0, C), v("qg"), v("sg"), v("qx"), v("sx"))
+        for h in range(2):
+            act(hv("near", h), bank(0, H * h, H * h + H), ACT.Identity, bias=c1("sc", 2))
         TH, NEED = c1("sc", 1), c1("u6", 31)
         tr(v("t6", 8, 40), v("m6", 0, 32))
-        red(TH, v("t6", 7, 40), A.add)
+        red(TH, v("t6", 8, 40), A.add)
         tr(v("t6", 40, 104), v("m6", 32, 96))
         scan(v("u6"), v("t6", 40, 72), v("t6", 72, 104), 0.0, A.min, A.max)
+        for b in range(4):
+            act(v("ff", FW * b, FW * b + C), bank(2 + b, C), ACT.Copy, after=TH)
         M0 = [v("mt", h, 4 * H, 4) for h in range(2)]
         for h in range(2):
-            act(hv("sig", h), bank(0, H * h, H * h + H), ACT.Sign, bias=TH, scale=-1.0)
-            ts(hv("neq", h), bank(1, H * h, H * h + H), TH, A.is_equal, -EPS, A.mult)
-        scan(v("ns"), v("neq"), v("zb"), NEED, A.add, A.add)
+            act(hv("sig", h), hv("near", h), ACT.Sign, bias=TH, scale=-1.0)
+            ts(hv("neq", h), hv("near", h), TH, A.is_equal, -EPS, A.mult)
         for h in range(2):
+            scan(hv("ns", h), hv("neq", h), hv("zb", h), c1("ns", H - 1) if h else NEED, A.add, A.add)
             tt(M0[h], hv("sig", h), hv("ns", h), A.is_le)
         quant(v("qm"), v("sm"), v("mt"))
         for h in range(2):
@@ -484,12 +503,13 @@ def rank_program(g, core, T, topo):
         ts(e6("q1", 5), x15, S15, A.mult, LL, A.subtract)
         scan(v("x3"), v("q0"), v("q1"), 0.0, A.add, A.max)
         ts(v("pos"), e6("x3", 5), 16.25, A.add)
-        scat(v("t0"), v("pos"), v("vs"))
-        tr(v("tq", 0, 576, 2), v("t0", 0, 288))
-        tr(v("tq", 33, 545, 2), v("t0", 16, 272))
+        scat(v("ti"), v("pos"), v("vs"))
+        for a, b in ((16, 208), (208, 272)):
+            cp(v("t0", a, b), v("ti", a, b))
+        tr(v("tq", 0, 576, 2), v("ti", 0, 288))
+        tr(v("tq", 33, 545, 2), v("ti", 16, 272))
         for j in range(2):
-            cp(v("xi", 24 * j, 24 * j + 17), v("tq", 32 * j, 32 * j + 529, 33))
-            ts(v("xa", 24 * j, 24 * j + 17), v("xi", 24 * j, 24 * j + 17), 1023, A.bitwise_and)
+            ts(v("xa", 24 * j, 24 * j + 17), v("tq", 32 * j, 32 * j + 529, 33), 1023, A.bitwise_and)
         for s, j, a, b, n, add in ((0, 0, 0, 0, 128, 15.0), (1, 1, 0, 32, 32, O2), (1, 1, 32, 64, 32, O2), (1, 1, 64, 96, 32, O2),
                                    (2, 0, 32, 64, 32, O3), (2, 0, 64, 96, 32, O3), (3, 1, 0, 64, 64, O3), (4, 0, 32, 96, 32, O3)):
             ts(v("loff", 18 * s, 18 * s + 17, p=(b, b + n)), v("xa", 24 * j, 24 * j + 17, p=(a, a + n)), part(add, (a, a + n)) if s else add, A.add)
@@ -511,28 +531,25 @@ def rank_program(g, core, T, topo):
         mask, ne = topo.mask(core, partner), len(topo.engines(core, partner))
 
         def send(to, what, reads, lands, cost, arr, pid=pid, rid=rid, mask=mask):
-            op("G", lambda: g.remote_dma(to, what, T.sem[arr], T.sem.snd, pid, rid, mask), [reads], [lands, c1("sc", 7)], cost, 2200, "bare")
+            op("G", lambda: g.remote_dma(to, what, T.sem[arr], T.sem.snd, pid, rid, mask), [reads], [lands], cost, 2200, "bare", sent[0])
+            sent[0] = len(calls) - 1
 
         for h in range(2):
             lo, hi, off = 128 * h, 128 * h + 128, v("offc", 8 * h, 8 * h + 8)
             for b in range(2):
                 act(v("zt", 4 * lo + 2 + b, 4 * hi, 4), v("ff", FW * (2 + b), FW * (2 + b) + C), ACT.Copy, off=off)
-                cp(v("zt", 4 * lo + b, 4 * hi, 4), v("ff", FW * b, FW * b + C), off=off)
-            quant(blk("qz", h), blk("sz", h), v("zt", 4 * lo, 4 * hi))
-            for b in (0, 2, 1, 3):
-                out, to = bank(4 * h + b, 128), v("ht", 4 * lo + b, 4 * hi, 4)
-                mm(out, blk("qw", b), blk("sw", b), blk("qz", h), blk("sz", h))
-                if b < 2:
-                    ts(to, out, 0.0, A.max, 0.015625, A.mult)
-                else:
-                    act(to, out, ACT.Relu, scale=0.015625)
-            quant(blk(qh, h), blk(sh, h), v("ht", 4 * lo, 4 * hi))
+                cp(v("zt", 4 * lo + b, 4 * hi, 4), v("ff", FW * b, FW * b + C), off=off, behind=first if h and b else None)
+            if h == 0:
+                first = len(calls)
+                quant(blk(qh, 0), blk(sh, 0), v("zt", 0, 512))
+            else:
+                quant(v("qz"), v("sz"), v("zt", 512, 1024))
+                layer(1, v("qz"), v("sz"), blk(qh, 1), blk(sh, 1))
             send(T[ql][:, lo:hi].bitcast(dt.uint8), T[qh][:, lo:hi].bitcast(dt.uint8), blk(qh, h), blk(ql, h), 800, arr + "ab"[h])
             send(T[sl][:, lo:hi], T[sh][:, lo:hi], blk(sh, h), blk(sl, h), 200, arr + "ab"[h])
-        act(v("thf"), v("col1"), ACT.Copy)
-        scat(v("thf"), v("offc"), v("kio"))
-        scan(v("cs4"), v("cmul"), v("thf"), 0.0, A.mult, A.max)
-        ts(v("offt"), v("cs4", 15, C, 16), UNB, A.mult, -1.0, A.add)
+        act(v("thf"), v("col1"), ACT.Copy, after=v("ns"))
+        for h in range(2):
+            scat(v("thf"), v("offc", 8 * h, 8 * h + 8), blk("kio", h))
         if k == 2:
             act(v("pb"), v("ta", 0, K), ACT.Identity, bias=1.5 * 2.0 ** 23, scale=EPS)
             act(v("pf"), v("pb"), ACT.Identity, bias=-1.5 * 2.0 ** 23)
@@ -540,19 +557,24 @@ def rank_program(g, core, T, topo):
         for h in range(2):
             got = [blk(ql, h), blk(sl, h)]
             op("P", lambda arr=arr + "ab"[h], n=2 * ne: wait("P", arr, n), got, got, 1, -WAKE, "bare")
+            if h == 0:
+                layer(0, *got, v("qp"), v("sp"))
+                got = [v("qp"), v("sp")]
+                for j in range(2):
+                    scan(hv("cs4", j), hv("cmul", j), hv("thf", j), 0.0, A.mult, A.max, after=v("ht", 1, 512, 4) if j else None)
+                ts(v("offt"), v("cs4", 15, C, 16), UNB, A.mult, -1.0, A.add)
             for b in range(4):
                 out = bank(4 * h + b, 128)
                 mm(out, blk("qe", b), blk("se", b), *got)
                 tt(v("ff", FW * b + C + 128 * h, FW * b + C + 128 * h + 128), out, v("zt", 512 * h + b, 512 * h + 512, 4), A.add)
-        for e2, b, h in (("S", 0, 0), ("S", 1, 0), ("V", 2, 0), ("V", 3, 0), ("S", 0, 1), ("S", 1, 1), ("S", 2, 1), ("V", 3, 1)):
-            lo, hi = RUNS[h]
-            out, win, off = v("xt", 4 * lo + b, 4 * hi, 4), v("ff", FW * b, FW * b + FW), v("offt", lo // 16, hi // 16)
-            if e2 == "V":
-                cp(out, win, off=off)
-            else:
-                act(out, win, ACT.Copy, off=off)
-        new_run(k + 1, 0)
-        new_run(k + 1, 1)
+        for h, (lo, hi, by) in enumerate(LAST if k == 2 else RUNS):
+            for b in range(4):
+                out, win, off = v("xt", 4 * lo + b, 4 * hi, 4), v("ff", FW * b, FW * b + FW), v("offt", lo // 16, hi // 16)
+                if by[b] == "V":
+                    cp(out, win, off=off)
+                else:
+                    act(out, win, ACT.Copy, off=off)
+            new_run(k + 1, h, lo, hi)
 
     issue()
     wait("G", "snd", 12 * ne)

@@ -6,29 +6,30 @@ FW = C + K
 F32, BF, I32, U16, Q4, U8 = "float32", "bfloat16", "int32", "uint16", "float8_e4m3fn_x4", "uint8"
 SB = {
     "xin": (4 * C, BF), "uin": (512, BF), "vin": (512, BF), "qu0": (128, Q4), "su0": (128, U8), "qu": (256, Q4), "su": (256, U8),
-    "qg": (128, Q4), "sg": (128, U8), "qv": (128, Q4), "sv": (128, U8), "qw": (512, Q4), "sw": (512, U8),
-    "ou": (24, U16), "r16": (28, U16), "et": (516, BF), "qe": (512, Q4), "se": (512, U8),
-    "ct": (516, BF), "qc": (256, Q4), "scc": (256, U8), "zb": (C, BF), "c1024": (C, BF), "m16": (32, BF), "cmul": (C, BF), "csum": (C, BF),
+    "qv": (128, Q4), "sv": (128, U8), "qw": (512, Q4), "sw": (512, U8),
+    "ou": (16, U16), "r16": (28, U16), "et": (516, BF), "qe": (512, Q4), "se": (512, U8),
+    "ct": (1024, BF), "qc": (256, Q4), "scc": (256, U8), "zb": (C, BF), "c257": (C, F32), "csum": (C, F32), "m16": (32, BF), "cmul": (C, BF), "hold": (C, BF),
     "xt": (4 * C, BF), "qx": (C, Q4), "sx": (C, U8), "ff": (4 * FW, BF),
-    "junk": (4 * C, BF), "spA": (C, F32), "spB": (C, F32), "near": (C, BF), "sig": (C, BF), "neq": (C, BF), "ns": (C, BF),
-    "mt": (4 * H, BF), "qm": (H, Q4), "sm": (H, U8), "dd": (C, BF), "ll": (C, BF), "bw": (C, BF),
-    "kb": (2, BF), "pos": (28, U16), "ti": (1200, I32), "t0": (560, F32), "ta": (272, F32), "tb": (272, F32), "tq": (576, I32), "q0": (168, F32), "q1": (168, F32),
-    "loff": (108, U16), "offc": (16, U16), "thf": (C, F32), "offt": (28, U16), "pf": (K, F32),
+    "junk": (6 * C, BF), "spA": (C, F32), "spB": (C, F32),
+    "eqA": (C + 16, BF), "nsA": (C + 16, BF), "eqB": (C + 16, BF), "nsB": (C + 16, BF), "c512": (C + 16, BF),
+    "mt": (4 * C, BF), "qm": (C, Q4), "sm": (C, U8), "dd": (C, BF), "ll": (C + 16, BF), "li": (C, BF), "lp": (C, BF),
+    "pos": (28, U16), "ti": (1440, I32), "tc": (288, I32), "t0": (560, F32), "ta": (272, F32), "tb": (272, F32), "tq": (576, I32),
+    "q0": (196, F32), "q1": (196, F32), "loff": (108, U16), "offc": (16, U16), "thf": (C, F32), "offt": (28, U16),
     "zt": (4 * K, BF), "qz": (128, Q4), "sz": (128, U8), "qp": (128, Q4), "sp": (128, U8), "ht": (4 * K, BF), "yo": (C, F32),
 }
 for _k in range(3):
     SB["qh%d" % _k], SB["sh%d" % _k], SB["ql%d" % _k], SB["sl%d" % _k] = (K, Q4), (K, U8), (K, Q4), (K, U8)
-LINE = {"s": 32, "z0": 32, "m1": 32, "t1": 32, "u": 192, "cand": 128, "candt": 128, "m2": 32, "t2": 32, "wk": 16,
-        "m3": 64, "t3": 80, "m4": 64, "t4": 80, "m5": 32, "t5": 48}
+LINE = {"s": 32, "z0": 32, "m1": 32, "t1": 32, "u": 352, "cand": 256, "candt": 256, "m2": 64, "t2": 64, "wk": 16,
+        "m3": 64, "t3": 80, "u3": 72, "m4": 64, "t4": 80, "u4": 72, "m5": 64, "t5": 80, "u5": 72, "cap": 72}
+TWICE = {"A": (3,), "B": (2,)}
 POOLS = {
-    "kf": (F32, {"kc": 32, "dn": 16, "up": 16, "zer": 64, "lam": 64, "lt": 64, "fac": 32, "inc": 32, "edge": 40, "fx": 40, "fy": 40, "tab": 64,
-                 "tabt": 64, "mcz": 32, "c64": 16, "mch": 16,
-                 "ca": 16, "cb": 16, "cd": 16, "ce": 16, "cf": 16, "mc": 32, "mcf": 32, "ratA": 128, "ratB": 128, "j64": 64, "krow": 16,
+    "kf": (F32, {"kc": 32, "dn": 16, "up": 16, "zer": 72, "lam": 64, "lt": 64, "fac": 64, "inc": 64, "edge": 72, "fx": 72, "fy": 72, "tab": 96,
+                 "tabt": 96, "mcz": 32, "mch": 32,
+                 "ca": 16, "cb": 16, "cd": 16, "ce": 16, "cf": 16, "cg": 16, "mc": 32, "mcf": 32, "rat": 224, "j64": 64, "krow": 16,
                  "i16": 32, "col": 32, "col1": C, "kio": K}),
-    "ki": (I32, {"pint": 2, "rint": 2, "hint": 1, "qint": 1, "oui": 24}),
+    "ki": (I32, {"pint": 2, "rint": 2, "hint": 1, "qint": 1, "oui": 16}),
     "wf": (F32, dict([(n + x, w) for x in "AB" for n, w in LINE.items()],
-                     sc=8, m6=96, t6=104, u6=32, vs=C, vw=C, cs=C, x3=168, l6a=16, l6b=16, l6=16, cs3=K, cs4=C, pb=K)),
-    "wi": (I32, {"xa": 48}),
+                     vs=C, vw=C, x3=196, l6a=16, l6b=16, l6=16, cs3=K, cs4=C)),
 }
 AT = {}
 for _p, (_d, _m) in POOLS.items():
@@ -38,15 +39,19 @@ for _p, (_d, _m) in POOLS.items():
         _o += -(-_w // 8) * 8
     SB[_p] = (_o, _d)
 SCRATCH = {n: ("sbuf", [128, w], d) for n, (w, d) in SB.items()}
-for _k in range(8):
-    SCRATCH["b%d" % _k] = ("psum", [128, 512], F32)
-SEMAPHORES = ["sV", "sS", "sP", "sG", "snd"] + ["arr%d%s" % (k, h) for k in range(3) for h in "ab"] + ["d%d" % i for i in range(17)]
+PSUM = ["b%d" % _k for _k in range(8)]
+for _n in PSUM:
+    SCRATCH[_n] = ("psum", [128, 512], F32)
+SEMAPHORES = ["sV", "sS", "sP", "sG", "snd"] + ["arr%d%s" % (k, h) for k in range(3) for h in "ab"] + ["d%d" % i for i in range(18)]
 
 BIG = 2.0 ** 80
-EPS = 2.0 ** -10
+FRAC = 0.43
 LOW = -2 ** 22
-WAKE = 240
-RUNS = ((0, 224, "SSVV"), (224, C, "SSSV"))
+PASSES, SHAKE, STRETCH = 3000, 1500, 5000
+ORDER = []
+WAKE = 230
+PIECES = ((0, H), (H, C))
+RUNS = ((0, 192, "SSVV"), (192, 320, "SSSV"), (320, C, "SSVV"))
 LAST = ((0, 160, "SSVV"), (160, 320, "SSSV"), (320, C, "SSVV"))
 
 
@@ -55,7 +60,7 @@ def rank_program(g, core, T, topo):
     if rank is None:
         return
     A, ACT = AluOpType, ActivationFunctionType
-    Q = {"V": g.vector, "S": g.scalar, "P": g.tensor, "G": g, "Y": g.sync}
+    Q = {"V": g.vector, "S": g.scalar, "P": g.tensor, "G": g, "Y": g.sync, "D": None}
     count = {"sV": 0, "sS": 0, "sP": 0, "sG": 0}
     known = {e: {} for e in Q}
     clock = {}
@@ -63,6 +68,7 @@ def rank_program(g, core, T, topo):
     calls = []
     soft = set()
     ndma, sent = [0], [None]
+    alike = []
 
     def v(n, a=0, b=None, s=1, p=(0, 128)):
         buf, o, w = AT[n] if n in AT else (n, 0, T[n].shape[1])
@@ -95,7 +101,7 @@ def rank_program(g, core, T, topo):
         deps = set() if behind is None else {behind}
         both = [(x, False) for x in reads] + [(x, True) for x in writes]
         for view, wr in both:
-            psum = view[1][0] == "b" and view[1][1:].isdigit()
+            psum = view[1] in PSUM
             for (o, ow, i) in log.get(view[1], []):
                 if (psum and calls[i][0] != e) or ((wr or ow) and meet(view, o)):
                     deps.add(i)
@@ -108,45 +114,70 @@ def rank_program(g, core, T, topo):
 
     def in_order():
         n = len(calls)
-        users = [[] for _ in calls]
-        for i, c in enumerate(calls):
-            for d in c[2]:
-                users[d].append(i)
+        cost, late, none = [c[3] for c in calls], [c[4] for c in calls], [0] * n
+        ahead = [[(d, cost[d] + (0 if (d, i) in soft else late[d] + WAKE)) for d in c[2]] for i, c in enumerate(calls)]
+        after = [[] for _ in calls]
+        for i in range(n):
+            for d, lag in ahead[i]:
+                after[d].append((i, lag - cost[d] + cost[i]))
+        seed = [1]
 
-        def lag(d, i):
-            return 0 if (d, i) in soft else calls[d][4] + WAKE
+        def chance():
+            seed[0] = (seed[0] * 1103515245 + 12345) % 2 ** 31
+            return seed[0] / 2 ** 31
 
-        def place(order, back):
+        def place(key, links, least):
             start, busy = [0] * n, {e: [] for e in Q}
-            for i in order:
-                e, _, deps, cost, late, _ = calls[i]
-                if back:
-                    t = max([start[u] + calls[u][3] + lag(i, u) for u in users[i]] + [late])
-                else:
-                    t = max([start[d] + calls[d][3] + lag(d, i) for d in deps] + [0])
-                slots = busy[e]
+            for _, i in sorted(zip(key, range(n))):
+                t, c, slots = least[i], cost[i], busy[calls[i][0]]
+                for d, lag in links[i]:
+                    if start[d] + lag > t:
+                        t = start[d] + lag
                 k = len(slots)
                 while k and slots[k - 1][1] > t:
                     k -= 1
-                while k < len(slots) and slots[k][0] < t + cost:
+                while k < len(slots) and slots[k][0] < t + c:
                     t = max(t, slots[k][1])
                     k += 1
-                slots.insert(k, (t, t + cost))
+                slots.insert(k, (t, t + c))
                 start[i] = t
             return start
 
+        def both(start):
+            back = place([(-start[i] - cost[i], -i) for i in range(n)], after, late)
+            return place([-back[i] - cost[i] for i in range(n)], ahead, none)
+
         tail = [0] * n
         for i in range(n - 1, -1, -1):
-            tail[i] = calls[i][3] + max([tail[u] + lag(i, u) for u in users[i]] + [calls[i][4]])
-        for _ in range(3):
-            start = place(sorted(range(n), key=lambda i: (-tail[i], i)), False)
-            back = place(sorted(range(n), key=lambda i: (-start[i] - calls[i][3], -i)), True)
-            tail = [back[i] + calls[i][3] for i in range(n)]
-        return sorted(range(n), key=lambda i: (start[i], i))
+            tail[i] = max([tail[u] + lag for u, lag in after[i]] + [late[i]])
+        start = place([-tail[i] - cost[i] for i in range(n)], ahead, none)
+        best = None
+        for turn in range(PASSES):
+            end = max(start[i] + cost[i] + late[i] for i in range(n))
+            if best is None or end <= best[0]:
+                best = (end, start)
+            key = list(best[1])
+            if turn % 16 == 15:
+                a, b = ((0, 1), (1, 2), (2, 1), (1, 0), (0, 2), (2, 0))[turn // 16 % 6]
+                same = alike[a][1] - alike[a][0] if 2 in (a, b) else alike[1][0] - alike[0][0]
+                a, b = alike[a][0], alike[b][0]
+                shift = sorted(key[b + i] - key[a + i] for i in range(same))[same // 2]
+                key[b:b + same] = [t + shift for t in key[a:a + same]]
+            elif turn > 3:
+                mid, far, shake = best[0] * chance(), STRETCH * chance(), SHAKE * chance()
+                key = [t + shake * (chance() - 0.5) if abs(t - mid) < far else t for t in key]
+            for i in range(n):
+                for d, _ in ahead[i]:
+                    if key[d] >= key[i]:
+                        key[i] = key[d] + 1
+            start = both(place(key, ahead, none))
+        return sorted(range(n), key=lambda i: (best[1][i], i))
 
     def issue():
         mark = {}
-        for i in in_order():
+        if not ORDER:
+            ORDER.extend(in_order())
+        for i in ORDER:
             e, call, deps, _, _, kind = calls[i]
             for d in deps:
                 if d in mark and (d, i) not in soft:
@@ -174,7 +205,7 @@ def rank_program(g, core, T, topo):
         return len(range(x[2], x[3], x[4]))
 
     def wide(*xs):
-        return max(64, size(xs[0]) // (2 if all(SB.get(x[1], (0, F32))[1] == BF for x in xs) else 1))
+        return max(64, 30 + size(xs[0]) // (2 if all(SB.get(x[1], (0, F32))[1] == BF for x in xs) else 1))
 
     def ts(o, i, s1, op0, s2=None, op1=None):
         if op1 is None:
@@ -183,7 +214,7 @@ def rank_program(g, core, T, topo):
             op("V", lambda: g.vector.tensor_scalar(o[0], i[0], ap(s1), ap(s2), op0, op1), aps(i, s1, s2), [o], wide(o, i))
 
     def tt(o, a, b, op0):
-        op("V", lambda: g.vector.tensor_tensor(o[0], a[0], b[0], op0), aps(a, b), [o], max(64, size(o)))
+        op("V", lambda: g.vector.tensor_tensor(o[0], a[0], b[0], op0), aps(a, b), [o], max(64, size(o) * (1 if a[1] in PSUM else 2)))
 
     def cp(o, i, off=None, behind=None):
         src = i[0].indirect(off[0]) if off else i[0]
@@ -208,7 +239,7 @@ def rank_program(g, core, T, topo):
         op("V", lambda: g.vector.memset(o[0], val), [], [o], wide(o))
 
     def quant(q, s, i):
-        op("V", lambda: g.vector.quantize_mx(q[0], s[0], i[0]), [i], [q, s], 15 + size(i) // 4)
+        op("V", lambda: g.vector.quantize_mx(q[0], s[0], i[0]), [i], [q, s], 15 + 0.265 * size(i))
 
     def mm(o, lq, ls, rq, rs):
         op("P", lambda: g.tensor.matmul_mx(o[0], lq[0], ls[0], rq[0], rs[0], True, True), [lq, ls, rq, rs], [o], 16 + size(o))
@@ -223,10 +254,10 @@ def rank_program(g, core, T, topo):
         if acc is not None:
             kw["accum_out"] = acc[0]
         op("S", lambda: g.scalar.activation(o[0], src, func, **kw), aps(i, bias, scale, off, after), aps(o, acc),
-           80 + max(64, size(o)) * (1.5 if off else 1))
+           80 + max(64, size(o)) * (1.5 if off else 1) + (24 if acc else 0))
 
     def iota(o, pat, base, cm=0):
-        if o[1] in POOLS["ki"][1] or o[1] == "ti":
+        if o[1] in POOLS["ki"][1] or o[1] in ("ti", "tc"):
             op("G", lambda: g.iota(o[0], pat, base, cm), [], [o], 160 + 2 * size(o))
         else:
             op("G", lambda: g.iota(o[0], pat, base, cm, allow_small_or_imprecise_dtypes=True), [], [o], 160 + 2 * size(o))
@@ -234,32 +265,34 @@ def rank_program(g, core, T, topo):
     def fill(o, val):
         iota(o, [[0, size(o)]], val)
 
-    def sel(o, pat, val, base, cm):
-        op("G", lambda: g.affine_select(o[0], o[0], pat, A.not_equal, val, base, cm), [o], [o], 200 + 2 * size(o))
+    def sel(o, pat, val, base, cm, keep=A.not_equal):
+        op("G", lambda: g.affine_select(o[0], o[0], pat, keep, val, base, cm), [o], [o], 200 + 2 * size(o))
 
-    def dma(e, o, i, reads, writes, late=2000):
-        op(e, lambda: Q[e].dma_start(o, i), reads, writes, 60, late, "dma")
+    def dma(e, o, i, reads, writes, late=2000, behind=None):
+        op(e, lambda: Q[e].dma_start(o, i), reads, writes, 60, late, "dma", behind)
+        if not writes:
+            op("D", lambda: None, [], [], o.shape[0] * o.shape[1] * (4 if reads[0][1] in ("yo", "ta") else 1) / 200, late, "bare", len(calls) - 1)
 
     hv = lambda n, h: v(n, H * h, H * (h + 1))
     bank = lambda i, a, b=None: v("b%d" % i, 0, a) if b is None else v("b%d" % i, a, b)
     blk = lambda n, i: v(n, 128 * i, 128 * i + 128)
-    dma("S", T.uin[:], T.u[:], [], [v("uin")])
+    dma("S", T.uin[:], T.u[:], [], [v("uin")], 2600)
     for a, b, _ in RUNS:
-        dma("Y", T.xin[:, 4 * a:4 * b], T.x[:, 4 * a:4 * b], [], [v("xin", 4 * a, 4 * b)], 2000 + 3 * b)
+        dma("Y", T.xin[:, 4 * a:4 * b], T.x[:, 4 * a:4 * b], [], [v("xin", 4 * a, 4 * b)], 2600 + 5 * b, len(calls) - 1 if a else None)
     dma("Y", T.qw[:].bitcast(dt.uint8), T.wc[:], [v("xin")], [v("qw")])
     dma("Y", T.sw[:], T.ws[:], [v("xin")], [v("sw")])
     dma("Y", T.vin[:], T.v[:], [v("xin")], [v("vin")])
 
-    (RF, RM1, RP1, OD, EV, J, SG, FM, D0, MCF, UN0, UNA, UNB, NB, U15, N14, N15, O2, O3, R0, RN, NOD) = [c1("kc", i) for i in range(22)]
+    (RF, RM1, RP1, OD, EV, J, SG, FM, D0, MCF, UN0, UNB, U15, B14, B15, O2, O3, R0, RN,
+     P14, P15, M14, M15, O2F, O3F, EV9, OD9) = [c1("kc", i) for i in range(27)]
     iota(v("pint"), [[15, 2]], 0, 1)
     iota(v("oui", 0, 16), [[16, 2], [32, 4], [0, 2]], 0)
-    iota(v("oui", 16, 24), [[16, 8]], 0)
     iota(v("j64"), [[1, 64]], 0)
     iota(v("i16"), [[16, 32]], 0)
     iota(v("col1"), [[1, C]], 1)
     iota(v("kio"), [[1, K]], C + 1)
     fill(v("zb"), 0)
-    fill(v("c1024"), 1024)
+    fill(v("c257"), 257)
     ms(v("zer"), 0.0)
     ts(v("rint"), v("pint"), 15, A.bitwise_and)
     ts(v("hint"), c1("pint", 0), 16, A.bitwise_and)
@@ -268,23 +301,32 @@ def rank_program(g, core, T, topo):
     cp(J, v("qint"))
     ts(RP1, c1("rint", 0), 1.0, A.add)
     ts(OD, v("hint"), 1.0 / 16, A.mult)
-    ts(NOD, v("hint"), -1.0 / 16, A.mult)
     ts(EV, v("hint"), -1.0 / 16, A.mult, 1.0, A.add)
     ts(v("col"), v("i16"), RF, A.add)
     ts(v("r16"), v("zer", 0, 28), RF, A.add)
-    fill(v("et"), 0)
+    ms(v("et"), 0.0)
     sel(v("et"), [[1, 516]], 1.0, -3, -4)
     for b in range(4):
         quant(blk("qe", b), blk("se", b), v("et", 3 - b, 515 - b))
-    fill(v("ct"), 0)
-    sel(v("ct", 65, 513, 4), [[-16, 7], [0, 16]], 1.0, -16, 1)
-    sel(v("ct", 65, 513, 4), [[-16, 7], [0, 16]], -1.0, 0, 1)
+    ms(v("ct", 0, 576), 0.0)
+    ms(v("ct", 0, 512, 2), -0.5)
+    sel(v("ct", 0, 512, 2), [[-32, 4], [0, 64]], 0.0, 0, 1, A.is_ge)
+    sel(v("ct", 0, 512, 2), [[32, 4], [0, 64]], 0.0, 31, -1, A.is_ge)
+    sel(v("ct", 1, 512, 2), [[-32, 4], [0, 64]], 0.5, -31, 1)
+    for t in range(4):
+        sel(v("ct", t, 512, 4), [[0, 4], [1, 2], [0, 16]], 0.0, t // 2 - 1, 0)
+    for a in range(0, 448, 112):
+        tt(v("ct", 576 + a, 688 + a), v("ct", 64 + a, 176 + a), v("ct", a, 112 + a), A.subtract)
+    ts(v("ct", 0, 512), v("ct", 0, 512), 512.0, A.mult)
     for t in range(2):
-        quant(blk("qc", t), blk("scc", t), v("ct", 1 - t, 513 - t))
-        fill(v("mt", 2 + t, 4 * H, 4), 0)
+        quant(blk("qc", t), blk("scc", t), v("ct", 512 * t, 512 * t + 512))
+    for x in "AB":
+        ms(c1("eq" + x, 15), float(C))
+        ms(v("cap" + x), -BIG)
+    fill(v("c512"), 512)
     cp(v("ou"), v("oui"))
     quant(v("qu0"), v("su0"), v("uin"))
-    for i, (q, s) in enumerate(((blk("qu", 0), blk("su", 0)), (blk("qu", 1), blk("su", 1)), (v("qg"), v("sg")))):
+    for i, (q, s) in enumerate(((blk("qu", 0), blk("su", 0)), (blk("qu", 1), blk("su", 1)))):
         pick(q, v("qu0"), v("ou", 8 * i, 8 * i + 8))
         act(s, v("su0"), ACT.Copy, off=v("ou", 8 * i, 8 * i + 8))
     quant(v("qv"), v("sv"), v("vin"))
@@ -298,65 +340,77 @@ def rank_program(g, core, T, topo):
     E0, T1 = c1("lt", 0), c1("lt", 32)
     ts(SG, v("hint"), 0.125, A.mult, -1.0, A.add)
     ts(FM, v("hint"), 1.5 / 16, A.mult, 0.5, A.add)
-    ts(D0, v("hint"), 0.375 / 16, A.mult, -0.125, A.add)
+    ts(D0, v("hint"), 0.1875 / 16, A.mult, -0.0625, A.add)
     ts(D0, D0, E0, A.mult)
     ms(v("fac"), 1.0)
-    ts(v("fac", 4, 32, 4), v("zer", 0, 7), FM, A.add)
-    scan(v("inc"), v("fac"), v("zer", 0, 32), D0, A.mult, A.add)
+    ts(v("fac", 8, 64, 8), v("zer", 0, 7), FM, A.add)
+    scan(v("inc"), v("fac"), v("zer", 0, 64), D0, A.mult, A.add)
     cp(c1("edge", 0), E0)
-    scan(v("edge", 1, 33), v("inc"), v("zer", 0, 32), E0, A.add, A.add)
-    ts(v("fx", 0, 33), v("edge", 0, 33), SG, A.mult, 2.0 ** -56, A.subtract)
-    ts(v("fy", 0, 33), v("fx", 0, 33), 0.0, A.min, SG, A.mult)
-    for j in range(2):
-        tt(v("tab", 32 * j, 32 * j + 32), v("edge", j, j + 32), v("fy", j, j + 32), A.add)
+    scan(v("edge", 1, 65), v("inc"), v("zer", 0, 64), E0, A.add, A.add)
+    ts(v("fx", 0, 65), v("edge", 0, 65), SG, A.mult, 2.0 ** -56, A.subtract)
+    ts(v("fy", 0, 65), v("fx", 0, 65), 0.0, A.min, SG, A.mult)
+    for j in range(3):
+        tt(v("tab", 32 * j, 32 * j + 32), v("edge", j, j + 63, 2), v("fy", j, j + 63, 2), A.add)
     ms(v("mc"), -64.0)
     ts(MCF, v("qint"), 0.5, A.is_lt, BIG, A.mult)
     ts(MCF, MCF, -64.0, A.add)
     ts(v("mcf"), v("zer", 0, 32), MCF, A.add)
     ts(v("mcz"), v("mcf"), 0.5, A.add, 4096.0, A.min)
-    ms(v("mch"), -63.5)
-    ms(v("c64"), 64.0)
     tr(v("tabt"), v("tab"))
-    for x, n in (("A", 32), ("B", 64)):
-        ts(v("rat" + x, 0, 64), v("j64"), 1.0 / n, A.mult)
-        ms(v("rat" + x, 64, 96), 0.0)
-        ms(v("rat" + x, 96, 128), 1.0)
-    for j, (a, b) in enumerate(((0, 2 ** 18), (0, 2 ** 17), (0, 2 ** 12), (0, 2 ** 7), (0, 4),
-                                (2 ** 12 - 2 ** 18, -2 ** 18), (2 ** 12 - 2 ** 18, -2 ** 17), (2 ** 12 - 2 ** 17, -2 ** 17),
-                                (2 ** 7 - 2 ** 12, 2 ** 7 - 2 ** 12 - 3), (-4 - 2 ** 7, 0), (-2 ** 7, 3 - 2 ** 7))):
-        act(c1("krow", j), J, ACT.Identity, bias=float(b), scale=float(a))
+    ms(v("mch"), -63.5)
+    ms(v("rat", 64, 96), 0.0)
+    ms(v("rat", 96, 128), 1.0)
+    for i, x in enumerate("AB"):
+        w4 = 2 ** (12 + (5 in TWICE[x]))
+        w3 = w4 * 2 ** (5 + (4 in TWICE[x]))
+        w2 = w3 * 2 ** (5 + (3 in TWICE[x]))
+        second = 32 * (128 if 5 in TWICE[x] else w4)
+        for j, (a, b) in enumerate(((0, w3), (0, w4), (0, -128), (w4 - w3, -w3), (128 - w4, 125 - w4), (0, second), (-124, -125), (-4, 124 - w2))):
+            act(c1("krow", 8 * i + j), J, ACT.Identity, bias=float(b), scale=float(a))
+    ts(v("rat", 0, 32), v("j64", 32, 64), 1.0 / 64, A.mult)
+    ts(v("rat", 32, 64), v("j64", 0, 32), 1.0 / 64, A.mult)
+    ts(v("rat", 128, 160), v("j64", 0, 32), 1.0 / 32, A.mult)
+    cp(v("rat", 160, 224), v("rat", 64, 128))
     j16 = v("j64", 0, 16)
     ts(v("ca"), j16, RF, A.not_equal)
     ts(v("cb"), j16, RP1, A.is_equal, 2.0 ** 20, A.mult)
     ts(v("cd"), j16, RM1, A.not_equal)
     ts(v("ce"), j16, RP1, A.is_equal, 2.0 ** 48, A.mult)
-    ts(v("cf"), j16, RF, A.is_equal, 2.0 ** -8 - 2.0, A.mult)
+    ts(v("m16", 16, 32), j16, RF, A.is_equal, 1024.0, A.mult)
     tt(v("m16", 0, 16), v("ca"), v("cb"), A.max)
     tt(v("cd"), v("cd"), v("ce"), A.max)
-    tt(v("m16", 16, 32), v("cd"), v("cf"), A.add)
     act(v("cmul"), v("m16", 0, 16), ACT.Copy, off=v("r16"))
-    act(v("csum"), v("m16", 16, 32), ACT.Copy, off=v("r16"))
+    act(v("hold"), v("m16", 16, 32), ACT.Copy, off=v("r16"))
+    ts(v("cf"), j16, RF, A.is_equal, 2.0 ** -10 - 2.0, A.mult)
+    tt(v("cg"), v("cd"), v("cf"), A.add)
+    act(v("csum"), v("cg"), ACT.Copy, off=v("r16"))
     ts(UN0, RF, 15.0, A.is_equal)
     ts(R0, RF, 0.0, A.is_equal)
     ts(RN, RF, 0.0, A.not_equal)
     ts(UNB, UN0, 2.0 ** -20, A.max)
-    ts(UNA, UN0, 2.0 ** -20, A.max, EPS, A.mult)
-    ts(NB, UN0, 2.0 ** -20, A.max, -4096.0, A.mult)
-    S14, S15 = c1("kb", 0), c1("kb", 1)
-    ts(S14, R0, 2.0 ** -40, A.mult)
-    ts(N14, R0, -2.0 ** -40, A.mult)
-    ts(U15, UN0, 256.0, A.mult, 2.0 ** -40, A.max)
-    ts(S15, U15, RN, A.mult)
-    ts(N15, U15, RN, A.mult, -1.0, A.mult)
-    for n, j, val in (("q0", 0, LOW), ("q0", 5, 0), ("q1", 2, LOW), ("q1", 3, LOW)):
-        fill(v(n, j, 168, 6), val)
-    ts(v("q0", 1, 168, 6), v("col", 0, 28), 1025.0, A.mult, 737.0, A.add)
-    ts(v("q0", 2, 168, 6), v("col", 0, 28), -1024.0, A.mult, -1.0, A.add)
+    ts(U15, UN0, 2.0, A.mult, 2.0 ** -47, A.max)
+    ts(P14, R0, 2.0 ** -47, A.mult)
+    ts(M14, R0, -2.0 ** -47, A.mult)
+    ts(P15, U15, RN, A.mult)
+    ts(M15, U15, RN, A.mult, -1.0, A.mult)
+    ts(B14, RN, float(LOW), A.mult)
+    ts(B15, R0, float(LOW), A.mult)
+    fill(v("q0"), 0)
+    fill(v("q0", 0, 196, 7), LOW)
+    fill(v("q1"), LOW)
+    ts(v("q0", 3, 196, 7), v("col", 0, 28), -2.0, A.mult, -516.0, A.add)
+    ts(v("q0", 5, 196, 7), v("col", 0, 28), 2.0, A.mult, 516.0, A.add)
+    ms(c1("ll", 15), 0.0)
     for a in (0, 272):
-        fill(v("ti", a, a + 16), 1)
+        fill(v("ti", a, a + 16), 512)
+        fill(v("tc", a, a + 16), 1)
         fill(v("t0", a, a + 16), 1)
     ts(O2, OD, 272.0, A.mult, 15.0, A.add)
     ts(O3, EV, 16.0, A.mult, -1.0, A.add)
+    ts(O2F, O2, -FRAC, A.add)
+    ts(O3F, O3, -FRAC, A.add)
+    ts(EV9, EV, 2.0 ** -9, A.mult)
+    ts(OD9, OD, 2.0 ** -9, A.mult)
     ts(v("loff", 18, 35), v("col", 0, 17), O2, A.add, O3, A.subtract)
     for s in range(2, 5):
         cp(v("loff", 18 * s, 18 * s + 17), v("col", 0, 17))
@@ -388,63 +442,67 @@ def rank_program(g, core, T, topo):
         w = lambda n, a=0, b=None: v(n + x, a, b)
         wk = lambda j: c1("wk" + x, j)
         raw, rel = bank(i, C), v("sp" + x)
-        WP, W, T4, T4B, T5, T6 = [s(j) for j in range(8, 14)]
-        n3, n4 = 32 * (1 + i), 32 * (2 - i)
-        T2, NX, T3, T3B, LO, HI = [c1("u" + x, 32 * j + 31) for j in range(6)]
+        W = s(9)
+        twice = TWICE[x]
 
-        def choose(j, z, row):
-            scan(w("u", 32 * j, 32 * j + 32), z, row, 0.0, A.max, A.min)
+        def choose(a, z, row):
+            scan(w("u", a, a + size(row)), z, row, 0.0, A.max, A.min)
+            return w("u", a + size(row) - 1, a + size(row))
 
-        ts(w("z0"), v("mcz"), s(0), A.subtract)
-        ts(w("m1"), w("z0"), s(1), A.subtract, BIG, A.mult)
+        def step(n, src, thr, nxt):
+            m, t, wide_ = "m%d" % n, "t%d" % n, 32 * len(thr)
+            for j, one in enumerate(thr):
+                count_at(src, one, s(2 * n + 10 + j), i + 2 * j)
+                ts(w(m, 32 * j, 32 * j + 32), v("mc" if j else "mcf"), s(2 * n + 10 + j), A.is_ge, wk(n - 3), A.mult)
+            if n == 3:
+                ts(w(t, 7, 8), thr[0], wk(3), A.add)
+            else:
+                ts(w(t, 7, 8), thr[0], LO, A.subtract, wk(4), A.add)
+            tr(w(t, 8, 8 + wide_), w(m, 0, wide_))
+            if nxt == 2:
+                cp(w(t, 8 + wide_, 9 + wide_), wk(5))
+            scan(w("u%d" % n, 0, wide_ + nxt), w(t, 7, 7 + wide_ + nxt), v("zer", 0, wide_ + nxt), 0.0, A.add, A.add)
+            return [w("u%d" % n, wide_ + j, wide_ + j + 1) for j in range(nxt)]
+
+        ts(w("z0"), v("mcz"), s(0), A.subtract, s(1), A.subtract)
+        ts(w("m1"), w("z0"), s(2), A.subtract, BIG, A.mult)
         tr(w("t1"), w("m1"))
-        choose(0, w("t1"), v("tabt", 0, 32))
-        choose(1, w("t1"), v("tabt", 32, 64))
-        count_at(raw, T2, s(4), i)
-        ts(WP, NX, T2, A.subtract)
-        ts(w("cand"), v("rat" + x), WP, A.mult, T2, A.add)
-        tr(w("candt"), w("cand"))
-        ts(w("m2"), v("mcz"), s(4), A.subtract, BIG, A.mult)
-        tr(w("t2"), w("m2"))
-        for j in (0, 1, 2, 3) if x == "B" else (0, 2, 3):
-            choose(2 + j, w("t2"), w("candt", 32 * j, 32 * j + 32))
-        ts(W, HI, LO, A.subtract, 2.0 ** -23, A.mult)
-        ts(w("wk", 0, 11), v("krow", 0, 11), W, A.mult)
+        ends = (0, 1, 2) if 2 in twice else (0, 2)
+        edge = [choose(32 * j, w("t1"), v("tabt", 32 * j, 32 * j + 32)) for j in ends]
+        n2 = len(ends) - 1
+        n3 = 1 + (3 in twice)
+        rat = v("rat", 0, 128) if n3 == 2 else v("rat", 128, 224)
+        for j in range(n2):
+            count_at(raw, edge[j], s(4 + j), i + 2 * j)
+            ts(s(6 + j), edge[j + 1], edge[j], A.subtract)
+            ts(w("cand", 128 * j, 128 * j + size(rat)), rat, s(6 + j), A.mult, edge[j], A.add)
+            tr(v("candt" + x, j, n2 * size(rat), n2), w("cand", 128 * j, 128 * j + size(rat)))
+            ts(w("m2", 32 * j, 32 * j + 32), v("mch" if j else "mcz"), s(4 + j), A.subtract, BIG, A.mult)
+            tr(v("t2" + x, j, 32 * n2, n2), w("m2", 32 * j, 32 * j + 32))
+        got = [choose(96 + 32 * n2 * j, w("t2", 0, 32 * n2), w("candt", 32 * n2 * j, 32 * n2 * (j + 1))) for j in range(n3 + 2)]
+        T3, LO, HI = got[:n3][::-1], got[n3], got[n3 + 1]
+        ts(W, HI, LO, A.subtract, 2.0 ** (n2 - 24), A.mult)
+        ts(w("wk", 0, 8), v("krow", 8 * i, 8 * i + 8), W, A.mult)
         for h in range(2):
-            ts(hv("sp" + x, h), bank(6 + i, H * h, H * h + H), LO, A.subtract)
-        count_at(raw, T3, s(6), i)
-        ts(w("t3", 7, 8), T3, wk(5 + 2 * i), A.add)
-        ts(w("m3", 0, 32), v("mcf"), s(6), A.is_ge, wk(i), A.mult)
-        if x == "B":
-            count_at(raw, T3B, s(7), 2 + i)
-            ts(w("m3", 32, 64), v("mc"), s(7), A.is_ge, wk(i), A.mult)
-        tr(w("t3", 8, 8 + n3), w("m3", 0, n3))
-        red(T4, w("t3", 7, 8 + n3), A.add)
-        count_at(raw, T4, s(20), i)
-        ts(w("t4", 7, 8), T4, LO, A.subtract, wk(8), A.add)
-        ts(w("m4", 0, 32), v("mcf"), s(20), A.is_ge, wk(2), A.mult)
-        if x == "A":
-            ts(w("t3", 40, 41), T3, wk(6), A.add)
-            red(T4B, w("t3", 8, 41), A.add)
-            count_at(raw, T4B, s(21), 2 + i)
-            ts(w("m4", 32, 64), v("mc"), s(21), A.is_ge, wk(2), A.mult)
-        tr(w("t4", 8, 8 + n4), w("m4", 0, n4))
-        red(T5, w("t4", 7, 8 + n4), A.add)
-        count_at(rel, T5, s(22), i)
-        ts(w("t5", 7, 8), T5, wk(9), A.add)
-        ts(w("t5", 40, 41), T5, wk(10), A.add, LO, A.add)
-        ts(w("m5"), v("mc"), s(22), A.is_ge, wk(3), A.mult)
-        tr(w("t5", 8, 40), w("m5"))
-        red(T6, w("t5", 7, 40), A.add)
-        red(s(24), w("t5", 8, 41), A.add)
-        count_at(rel, T6, s(23), i)
-        if x == "A":
-            ts(c1("sc", 0), s(24), EV, A.mult, -1.0, A.mult)
-        else:
-            ts(c1("sc", 2), s(24), NOD, A.mult, c1("sc", 0), A.add)
-        ts(v("m6", 16 * i, 16 * i + 16), v("mc", 0, 16), s(23), A.is_ge, wk(4), A.mult)
-        ts(v("m6", 32 + 16 * i, 48 + 16 * i), v("mch"), s(23), A.subtract, BIG, A.mult)
-        ts(v("m6", 64 + 16 * i, 80 + 16 * i), v("c64"), s(23), A.add, EPS / 2, A.mult)
+            ts(hv("sp" + x, h), bank(6 + i, H * h, H * h + H), LO, A.subtract, -1.0, A.mult)
+        T4 = step(3, raw, T3, 1 + (4 in twice))
+        T5 = step(4, raw, T4, 1 + (5 in twice))
+        n5 = 32 * len(T5)
+        for j, one in enumerate(T5):
+            act(v("junk", C * (i + 2 * j), C * (i + 2 * j + 1)), rel, ACT.Sign, bias=one, acc=s(22 + j))
+            ts(w("m5", 32 * j, 32 * j + 32), v("mc"), s(22 + j), A.is_ge, wk(2), A.mult)
+        ts(w("t5", 7, 8), T5[0], wk(6), A.add, -1.0, A.mult)
+        ts(w("t5", 8 + n5, 9 + n5), W, -1.0, A.mult)
+        cp(w("cap", n5, n5 + 1), wk(7))
+        tr(w("t5", 8, 8 + n5), w("m5", 0, n5))
+        scan(w("u5", 0, n5 + 2), w("t5", 7, 9 + n5), w("cap", 0, n5 + 2), 0.0, A.add, A.max)
+        TV, TH, SUM = w("u5", n5, n5 + 1), w("u5", n5 + 1, n5 + 2), s(24)
+        act(v("mt", 2 * i + 1, 4 * C, 4), rel, ACT.Sign, bias=TH, scale=-1.0, acc=SUM)
+        for h, (a, b) in enumerate(PIECES):
+            ts(w("eq", 16 + a, 16 + b), w("sp", a, b), TV, A.is_equal, 2.0, A.mult)
+            lo = 16 + a if h else 15
+            scan(w("ns", lo, 16 + b), w("eq", lo, 16 + b), v("c512", lo, 16 + b), w("ns", lo - 1, lo) if h else SUM, A.add, A.min)
+            scan(v("mt", 4 * a + 2 * i, 4 * b, 4), w("ns", 15 + a, 15 + b), w("ns", 16 + a, 16 + b), 0.0, A.max, A.subtract)
 
     def layer(h, qz, sz, qh, sh):
         for b in (0, 2, 1, 3):
@@ -459,73 +517,62 @@ def rank_program(g, core, T, topo):
     for h, (a, b, _) in enumerate(RUNS):
         new_run(0, h, a, b)
     for k, e in enumerate(ROUNDS):
-        partner = T.cores[rank ^ e]
+        partner, begin = T.cores[rank ^ e], len(calls)
         for i in (0, 1, 6, 7):
             mm(bank(i, C), blk("qu", i % 2), blk("su", i % 2), v("qx"), v("sx"))
         for b in range(4):
             mm(bank(2 + b, C), blk("qe", b), blk("se", b), v("qx"), v("sx"))
         for i, x in enumerate("AB"):
             search(i, x)
-        mm(bank(0, C), v("qg"), v("sg"), v("qx"), v("sx"))
-        for h in range(2):
-            act(hv("near", h), bank(0, H * h, H * h + H), ACT.Identity, bias=c1("sc", 2))
-        TH, NEED = c1("sc", 1), c1("u6", 31)
-        tr(v("t6", 8, 40), v("m6", 0, 32))
-        red(TH, v("t6", 8, 40), A.add)
-        tr(v("t6", 40, 104), v("m6", 32, 96))
-        scan(v("u6"), v("t6", 40, 72), v("t6", 72, 104), 0.0, A.min, A.max)
         for b in range(4):
-            act(v("ff", FW * b, FW * b + C), bank(2 + b, C), ACT.Copy, after=TH)
-        M0 = [v("mt", h, 4 * H, 4) for h in range(2)]
-        for h in range(2):
-            act(hv("sig", h), hv("near", h), ACT.Sign, bias=TH, scale=-1.0)
-            ts(hv("neq", h), hv("near", h), TH, A.is_equal, -EPS, A.mult)
-        for h in range(2):
-            scan(hv("ns", h), hv("neq", h), hv("zb", h), c1("ns", H - 1) if h else NEED, A.add, A.add)
-            tt(M0[h], hv("sig", h), hv("ns", h), A.is_le)
-        quant(v("qm"), v("sm"), v("mt"))
-        for h in range(2):
-            on = lambda n, first: c1(n, H - 1) if h else first
-            mm(bank(6 + h, H), blk("qc", h), blk("scc", h), v("qm"), v("sm"))
-            scan(hv("vs", h), M0[h], hv("c1024", h), on("vs", -1024.0), A.add, A.add)
-            scan(hv("bw", h), hv("cmul", h), M0[h], 0.0, A.mult, A.max)
-            scan(hv("vw", h), hv("cmul", h), hv("vs", h), 0.0, A.mult, A.max)
-            scan(hv("dd", h), bank(6 + h, H), hv("zb", h), on("dd", 0.0), A.add, A.add)
-            scan(hv("ll", h), hv("dd", h), hv("zb", h), on("ll", 0.0), A.max, A.max)
-            scan(hv("cs", h), hv("csum", h), hv("ll", h), on("ll", 0.0), A.mult, A.add)
-        e6 = lambda n, j: v(n, j, 168, 6)
-        x14, x15, LL = v("cs", 14, C, 16), v("cs", 15, C, 16), c1("ll", C - 1)
-        ts(e6("q1", 0), v("bw", 15, C, 16), NB, A.mult)
-        ts(e6("q1", 1), v("vw", 15, C, 16), UNB, A.mult)
-        ts(e6("q0", 3), x14, N14, A.mult)
-        ts(e6("q0", 4), x15, N15, A.mult)
-        ts(e6("q1", 4), x14, S14, A.mult, LL, A.subtract)
-        ts(e6("q1", 5), x15, S15, A.mult, LL, A.subtract)
+            act(v("ff", FW * b, FW * b + C), bank(2 + b, C), ACT.Copy, after=c1("sB", 24))
+        for h, (a, b) in enumerate(PIECES):
+            on = lambda n, first: c1(n, a - 1) if h else first
+            pc = lambda n: v(n, a, b)
+            quant(pc("qm"), pc("sm"), v("mt", 4 * a, 4 * b))
+            mm(bank(h, b - a), blk("qc", 1), blk("scc", 1), pc("qm"), pc("sm"))
+            mm(bank(6 + h, b - a), blk("qc", 0), blk("scc", 0), pc("qm"), pc("sm"))
+            scan(pc("vs"), bank(6 + h, b - a), pc("c257"), on("vs", -1.0), A.add, A.add)
+            scan(pc("vw"), pc("csum"), pc("vs"), on("vs", -1.0), A.mult, A.add)
+            scan(pc("dd"), bank(h, b - a), pc("zb"), on("dd", 0.0), A.add, A.add)
+            scan(v("ll", 16 + a, 16 + b), pc("dd"), pc("zb"), c1("ll", 15 + a) if h else 0.0, A.max, A.max)
+        scan(v("lp"), v("hold"), v("ll", 15, 15 + C), 0.0, A.add, A.min)
+        scan(v("li"), v("hold"), v("ll", 16, 16 + C), 0.0, A.add, A.min)
+        e6 = lambda n, j: v(n, j, 196, 7)
+        li, lp, LL = v("li", 15, C, 16), v("lp", 15, C, 16), c1("ll", C + 15)
+        y14, y15 = v("vw", 14, C, 16), v("vw", 15, C, 16)
+        act(e6("q1", 1), y14, ACT.Identity, scale=P14, bias=-1026.0)
+        act(e6("q1", 3), y14, ACT.Identity, scale=M14, bias=B14)
+        ts(e6("q1", 2), y15, P15, A.mult, -1026.0, A.add)
+        ts(e6("q1", 4), y15, M15, A.mult, B15, A.add)
+        ts(e6("q1", 0), li, 256.0, A.mult, LL, A.subtract)
+        ts(e6("q0", 1), lp, -254.0, A.mult)
+        ts(e6("q0", 6), lp, -1.0, A.mult)
         scan(v("x3"), v("q0"), v("q1"), 0.0, A.add, A.max)
-        ts(v("pos"), e6("x3", 5), 16.25, A.add)
+        ts(v("pos"), e6("x3", 6), 16.0 - FRAC, A.add)
         scat(v("ti"), v("pos"), v("vs"))
-        for a, b in ((16, 208), (208, 272)):
-            cp(v("t0", a, b), v("ti", a, b))
+        ts(v("tc", 16, 272), v("ti", 16, 272), 511, A.bitwise_and)
+        cp(v("t0", 16, 272), v("tc", 16, 272))
         tr(v("tq", 0, 576, 2), v("ti", 0, 288))
         tr(v("tq", 33, 545, 2), v("ti", 16, 272))
-        for j in range(2):
-            ts(v("xa", 24 * j, 24 * j + 17), v("tq", 32 * j, 32 * j + 529, 33), 1023, A.bitwise_and)
-        for s, j, a, b, n, add in ((0, 0, 0, 0, 128, 15.0), (1, 1, 0, 32, 32, O2), (1, 1, 32, 64, 32, O2), (1, 1, 64, 96, 32, O2),
-                                   (2, 0, 32, 64, 32, O3), (2, 0, 64, 96, 32, O3), (3, 1, 0, 64, 64, O3), (4, 0, 32, 96, 32, O3)):
-            ts(v("loff", 18 * s, 18 * s + 17, p=(b, b + n)), v("xa", 24 * j, 24 * j + 17, p=(a, a + n)), part(add, (a, a + n)) if s else add, A.add)
+        own = lambda j, m, n, p: v("tq", 32 * j + 33 * m, 32 * j + 33 * (m + n - 1) + 1, 33, p)
+        for s, j, a, b, n, add in ((0, 0, 0, 0, 128, 15.0 - FRAC), (1, 1, 0, 32, 32, O2F), (1, 1, 32, 64, 32, O2F), (1, 1, 64, 96, 32, O2F),
+                                   (2, 0, 32, 64, 32, O3F), (2, 0, 64, 96, 32, O3F), (3, 1, 0, 64, 64, O3F), (4, 0, 32, 96, 32, O3F)):
+            ts(v("loff", 18 * s, 18 * s + 17, p=(b, b + n)), own(j, 0, 17, (a, a + n)), 2.0 ** -9, A.mult, part(add, (a, a + n)) if s else add, A.add)
         q = (0, 32)
-        ts(v("l6a", p=q), v("xa", 25, 41, p=q), part(EV, q), A.mult, part(O3, q), A.add)
-        ts(v("l6b", p=q), v("xa", 24, 40, p=q), part(OD, q), A.mult)
+        ts(v("l6a", p=q), own(1, 1, 16, q), part(EV9, q), A.mult, part(O3F, q), A.add)
+        ts(v("l6b", p=q), own(1, 0, 16, q), part(OD9, q), A.mult)
         tt(v("l6", p=q), v("l6a", p=q), v("l6b", p=q), A.add)
         cp(v("loff", 90, 106, p=(96, 128)), v("l6", p=q))
-        ways = ((v("t0", 0, 288), "t0", 288), (v("t0", 0, 560), "ta", 0), (v("ta"), "tb", 0), (v("tb"), "ta", 0), (v("ta"), "tb", 0), (v("tb"), "ta", 0))
+        ways = ((v("tc"), "t0", 288), (v("t0"), "ta", 0), (v("ta"), "tb", 0), (v("tb"), "ta", 0), (v("ta"), "tb", 0), (v("tb"), "ta", 0))
         for s, (src, dst, o) in enumerate(ways):
             n = 17 if s < 5 else 16
-            act(v(dst, o, o + 128), src, ACT.Copy, off=v("loff", 18 * s, 18 * s + 8))
-            cp(v(dst, o + 128, o + 16 * n), src, off=v("loff", 18 * s + 8, 18 * s + n))
+            m = 8 if s else 12
+            act(v(dst, o, o + 16 * m), src, ACT.Copy, off=v("loff", 18 * s, 18 * s + m))
+            cp(v(dst, o + 16 * m, o + 16 * n), src, off=v("loff", 18 * s + m, 18 * s + n))
         for h in range(2):
             scan(blk("cs3", h), v("cmul", 0, 128), blk("ta", h), 0.0, A.mult, A.max)
-            ts(v("offc", 8 * h, 8 * h + 8), v("cs3", 128 * h + 15, 128 * h + 128, 16), UNA, A.mult)
+            ts(v("offc", 8 * h, 8 * h + 8), v("cs3", 128 * h + 15, 128 * h + 128, 16), UNB, A.mult)
         qh, sh, ql, sl, arr = "qh%d" % k, "sh%d" % k, "ql%d" % k, "sl%d" % k, "arr%d" % k
         rid, pid, _ = topo.addr(partner)
         mask, ne = topo.mask(core, partner), len(topo.engines(core, partner))
@@ -547,13 +594,12 @@ def rank_program(g, core, T, topo):
                 layer(1, v("qz"), v("sz"), blk(qh, 1), blk(sh, 1))
             send(T[ql][:, lo:hi].bitcast(dt.uint8), T[qh][:, lo:hi].bitcast(dt.uint8), blk(qh, h), blk(ql, h), 800, arr + "ab"[h])
             send(T[sl][:, lo:hi], T[sh][:, lo:hi], blk(sh, h), blk(sl, h), 200, arr + "ab"[h])
-        act(v("thf"), v("col1"), ACT.Copy, after=v("ns"))
+        act(v("thf"), v("col1"), ACT.Copy, after=c1("nsB", 15))
         for h in range(2):
             scat(v("thf"), v("offc", 8 * h, 8 * h + 8), blk("kio", h))
+        alike.append((begin, len(calls)))
         if k == 2:
-            act(v("pb"), v("ta", 0, K), ACT.Identity, bias=1.5 * 2.0 ** 23, scale=EPS)
-            act(v("pf"), v("pb"), ACT.Identity, bias=-1.5 * 2.0 ** 23)
-            dma("Y", T.pl[:], T.pf[0:128:16, :], [v("pf")], [])
+            dma("Y", T.pl[:], T.ta[0:128:16, 0:K], [v("ta")], [])
         for h in range(2):
             got = [blk(ql, h), blk(sl, h)]
             op("P", lambda arr=arr + "ab"[h], n=2 * ne: wait("P", arr, n), got, got, 1, -WAKE, "bare")

@@ -1,3 +1,4 @@
+import math
 from concourse.mybir import dt, AluOpType, AxisListType, ActivationFunctionType
 
 C, K, ROUNDS = 448, 256, (1, 2, 3)
@@ -8,13 +9,14 @@ SB = {
     "xin": (4 * C, BF), "uin": (512, BF), "vin": (512, BF), "qu0": (128, Q4), "su0": (128, U8), "qu": (256, Q4), "su": (256, U8),
     "qv": (128, Q4), "sv": (128, U8), "qw": (512, Q4), "sw": (512, U8),
     "ou": (16, U16), "r16": (28, U16), "et": (516, BF), "qe": (512, Q4), "se": (512, U8),
-    "ct": (1024, BF), "qc": (256, Q4), "scc": (256, U8), "zb": (C, BF), "c257": (C, F32), "csum": (C, F32), "m16": (32, BF), "cmul": (C, BF), "hold": (C, BF),
-    "xt": (4 * C, BF), "qx": (C, Q4), "sx": (C, U8), "ff": (4 * FW, BF),
+    "ct": (576, BF), "cs": (512, BF), "qc": (128, Q4), "scc": (128, U8), "m16": (16, BF), "cmul": (C, BF),
+    "cw": (C, BF), "cpay": (256, BF), "lst": (12, U16), "opl": (16, U16),
+    "xt": (4 * C, BF), "qx": (C, Q4), "sx": (C, U8), "ff": (4 * FW, BF), "fz": (2 * FW, BF),
     "junk": (6 * C, BF), "spA": (C, F32), "spB": (C, F32),
     "eqA": (C + 16, BF), "nsA": (C + 16, BF), "eqB": (C + 16, BF), "nsB": (C + 16, BF), "c512": (C + 16, BF),
-    "mt": (4 * C, BF), "qm": (C, Q4), "sm": (C, U8), "dd": (C, BF), "ll": (C + 16, BF), "li": (C, BF), "lp": (C, BF),
-    "pos": (28, U16), "ti": (1440, I32), "tc": (288, I32), "t0": (560, F32), "ta": (272, F32), "tb": (272, F32), "tq": (576, I32),
-    "q0": (196, F32), "q1": (196, F32), "loff": (108, U16), "offc": (16, U16), "thf": (C, F32), "offt": (28, U16),
+    "mt": (4 * C, BF), "qm": (C, Q4), "sm": (C, U8), "rw": (C + 16, BF), "rt": (2 * C, BF), "pay": (C, BF),
+    "pos": (28, U16), "tb": (1104, BF), "tq": (576, BF), "tm": (576, BF), "fo": (352, BF), "ft": (640, BF), "plf": (K, F32),
+    "loff": (74, U16), "offc": (32, U16), "thf": (C, F32), "offt": (28, U16),
     "zt": (4 * K, BF), "qz": (128, Q4), "sz": (128, U8), "qp": (128, Q4), "sp": (128, U8), "ht": (4 * K, BF), "yo": (C, F32),
 }
 for _k in range(3):
@@ -25,11 +27,11 @@ TWICE = {"A": (3,), "B": (2,)}
 POOLS = {
     "kf": (F32, {"kc": 32, "dn": 16, "up": 16, "zer": 72, "lam": 64, "lt": 64, "fac": 64, "inc": 64, "edge": 72, "fx": 72, "fy": 72, "tab": 96,
                  "tabt": 96, "mcz": 32, "mch": 32,
-                 "ca": 16, "cb": 16, "cd": 16, "ce": 16, "cf": 16, "cg": 16, "mc": 32, "mcf": 32, "rat": 224, "j64": 64, "krow": 16,
-                 "i16": 32, "col": 32, "col1": C, "kio": K}),
+                 "ca": 16, "cb": 16, "mc": 32, "mcf": 32, "rat": 224, "j64": 64, "krow": 16, "kd": 16,
+                 "i16": 32, "col": 32, "col1": C, "kio": K, "ci": 64, "cj": 64, "lrow": 176, "lrow2": 176, "cq": 96,
+                 "mll": 32}),
     "ki": (I32, {"pint": 2, "rint": 2, "hint": 1, "qint": 1, "oui": 16}),
-    "wf": (F32, dict([(n + x, w) for x in "AB" for n, w in LINE.items()],
-                     vs=C, vw=C, x3=196, l6a=16, l6b=16, l6=16, cs3=K, cs4=C)),
+    "wf": (F32, dict([(n + x, w) for x in "AB" for n, w in LINE.items()], q0=96, q1=96, x3=84, llb=32, llt=32, cs4=C)),
 }
 AT = {}
 for _p, (_d, _m) in POOLS.items():
@@ -45,13 +47,18 @@ for _n in PSUM:
 SEMAPHORES = ["sV", "sS", "sP", "sG", "snd"] + ["arr%d%s" % (k, h) for k in range(3) for h in "ab"] + ["d%d" % i for i in range(18)]
 
 BIG = 2.0 ** 80
-FRAC = 0.43
-LOW = -2 ** 22
-PASSES, SHAKE, STRETCH = 3000, 1500, 5000
+FAR, LIFT = 2.0 ** 30, 2.0 ** 20
+MET = 258.0
+NUM, COL = 4, 15
+TAB = (0, 288, 560, 832, 1104)
+PASSES, SHAKE, STRETCH = 5000, 1500, 5000
 ORDER = []
 WAKE = 230
-PIECES = ((0, H), (H, C))
+PIECES = ((0, 256), (256, C))
 RUNS = ((0, 192, "SSVV"), (192, 320, "SSSV"), (320, C, "SSVV"))
+ADDED = ()
+GAT = 1.5
+MARKS = ("SS", "SS")
 LAST = ((0, 160, "SSVV"), (160, 320, "SSSV"), (320, C, "SSVV"))
 
 
@@ -84,7 +91,7 @@ def rank_program(g, core, T, topo):
     def meet(x, y):
         if x[3] <= y[2] or y[3] <= x[2] or x[5][1] <= y[5][0] or y[5][1] <= x[5][0]:
             return False
-        return not (x[4] == y[4] and x[4] > 1 and (x[2] - y[2]) % x[4])
+        return not (x[2] - y[2]) % math.gcd(x[4], y[4])
 
     def wait(e, sem, val):
         if known[e].get(sem, 0) >= val:
@@ -163,6 +170,12 @@ def rank_program(g, core, T, topo):
                 a, b = alike[a][0], alike[b][0]
                 shift = sorted(key[b + i] - key[a + i] for i in range(same))[same // 2]
                 key[b:b + same] = [t + shift for t in key[a:a + same]]
+            elif turn % 4 == 1:
+                i = int(alike[0][0] * chance())
+                key[i] *= chance()
+                for i in range(i, -1, -1):
+                    for d, _ in ahead[i]:
+                        key[d] = min(key[d], key[i] - 1)
             elif turn > 3:
                 mid, far, shake = best[0] * chance(), STRETCH * chance(), SHAKE * chance()
                 key = [t + shake * (chance() - 0.5) if abs(t - mid) < far else t for t in key]
@@ -205,16 +218,19 @@ def rank_program(g, core, T, topo):
         return len(range(x[2], x[3], x[4]))
 
     def wide(*xs):
-        return max(64, 30 + size(xs[0]) // (2 if all(SB.get(x[1], (0, F32))[1] == BF for x in xs) else 1))
+        return max(64, 30 + size(xs[0]) // (2 if all(SB.get(x[1], (0, F32))[1] == BF and x[4] == 1 for x in xs) else 1))
 
-    def ts(o, i, s1, op0, s2=None, op1=None):
+    def ts(o, i, s1, op0, s2=None, op1=None, off=None):
+        src, cost = (i[0].indirect(off[0]), 60 + 1.5 * size(o)) if off else (i[0], wide(o, i))
         if op1 is None:
-            op("V", lambda: g.vector.tensor_scalar(o[0], i[0], ap(s1), None, op0), aps(i, s1), [o], wide(o, i))
+            op("V", lambda: g.vector.tensor_scalar(o[0], src, ap(s1), None, op0), aps(i, s1, off), [o], cost)
         else:
-            op("V", lambda: g.vector.tensor_scalar(o[0], i[0], ap(s1), ap(s2), op0, op1), aps(i, s1, s2), [o], wide(o, i))
+            op("V", lambda: g.vector.tensor_scalar(o[0], src, ap(s1), ap(s2), op0, op1), aps(i, s1, s2, off), [o], cost)
 
-    def tt(o, a, b, op0):
-        op("V", lambda: g.vector.tensor_tensor(o[0], a[0], b[0], op0), aps(a, b), [o], max(64, size(o) * (1 if a[1] in PSUM else 2)))
+    def tt(o, a, b, op0, off=None):
+        src = a[0].indirect(off[0]) if off else a[0]
+        op("V", lambda: g.vector.tensor_tensor(o[0], src, b[0], op0), aps(a, b, off), [o],
+           60 + GAT * size(o) if off else max(64, 30 + size(o) * (1 if a[1] in PSUM else 2)))
 
     def cp(o, i, off=None, behind=None):
         src = i[0].indirect(off[0]) if off else i[0]
@@ -257,7 +273,7 @@ def rank_program(g, core, T, topo):
            80 + max(64, size(o)) * (1.5 if off else 1) + (24 if acc else 0))
 
     def iota(o, pat, base, cm=0):
-        if o[1] in POOLS["ki"][1] or o[1] in ("ti", "tc"):
+        if o[1] in POOLS["ki"][1]:
             op("G", lambda: g.iota(o[0], pat, base, cm), [], [o], 160 + 2 * size(o))
         else:
             op("G", lambda: g.iota(o[0], pat, base, cm, allow_small_or_imprecise_dtypes=True), [], [o], 160 + 2 * size(o))
@@ -271,7 +287,7 @@ def rank_program(g, core, T, topo):
     def dma(e, o, i, reads, writes, late=2000, behind=None):
         op(e, lambda: Q[e].dma_start(o, i), reads, writes, 60, late, "dma", behind)
         if not writes:
-            op("D", lambda: None, [], [], o.shape[0] * o.shape[1] * (4 if reads[0][1] in ("yo", "ta") else 1) / 200, late, "bare", len(calls) - 1)
+            op("D", lambda: None, [], [], o.shape[0] * o.shape[1] * (4 if reads[0][1] in ("yo", "plf") else 1) / 200, late, "bare", len(calls) - 1)
 
     hv = lambda n, h: v(n, H * h, H * (h + 1))
     bank = lambda i, a, b=None: v("b%d" % i, 0, a) if b is None else v("b%d" % i, a, b)
@@ -283,16 +299,15 @@ def rank_program(g, core, T, topo):
     dma("Y", T.sw[:], T.ws[:], [v("xin")], [v("sw")])
     dma("Y", T.vin[:], T.v[:], [v("xin")], [v("vin")])
 
-    (RF, RM1, RP1, OD, EV, J, SG, FM, D0, MCF, UN0, UNB, U15, B14, B15, O2, O3, R0, RN,
-     P14, P15, M14, M15, O2F, O3F, EV9, OD9) = [c1("kc", i) for i in range(27)]
+    (RF, RM1, RP1, OD, EV, J, SG, FM, D0, MCF, UN0, UNB, R0, MY, NB, INI, INP, CP,
+     O1, O2, O3, HQ, THM) = [c1("kc", i) for i in range(23)]
     iota(v("pint"), [[15, 2]], 0, 1)
     iota(v("oui", 0, 16), [[16, 2], [32, 4], [0, 2]], 0)
     iota(v("j64"), [[1, 64]], 0)
     iota(v("i16"), [[16, 32]], 0)
     iota(v("col1"), [[1, C]], 1)
     iota(v("kio"), [[1, K]], C + 1)
-    fill(v("zb"), 0)
-    fill(v("c257"), 257)
+    iota(v("cw"), [[1024, C]], -1024 * H)
     ms(v("zer"), 0.0)
     ts(v("rint"), v("pint"), 15, A.bitwise_and)
     ts(v("hint"), c1("pint", 0), 16, A.bitwise_and)
@@ -308,22 +323,28 @@ def rank_program(g, core, T, topo):
     sel(v("et"), [[1, 516]], 1.0, -3, -4)
     for b in range(4):
         quant(blk("qe", b), blk("se", b), v("et", 3 - b, 515 - b))
-    ms(v("ct", 0, 576), 0.0)
-    ms(v("ct", 0, 512, 2), -0.5)
-    sel(v("ct", 0, 512, 2), [[-32, 4], [0, 64]], 0.0, 0, 1, A.is_ge)
-    sel(v("ct", 0, 512, 2), [[32, 4], [0, 64]], 0.0, 31, -1, A.is_ge)
-    sel(v("ct", 1, 512, 2), [[-32, 4], [0, 64]], 0.5, -31, 1)
+    ms(v("ct"), 0.0)
+    ms(v("ct", 64, 576, 2), -0.5)
+    sel(v("ct", 64, 576, 2), [[-32, 4], [0, 64]], 0.0, -1, 1, A.is_ge)
+    sel(v("ct", 64, 576, 2), [[32, 4], [0, 64]], 0.0, 31, -1, A.is_ge)
+    sel(v("ct", 65, 576, 2), [[-32, 4], [0, 64]], 0.5, 0, 1)
     for t in range(4):
-        sel(v("ct", t, 512, 4), [[0, 4], [1, 2], [0, 16]], 0.0, t // 2 - 1, 0)
-    for a in range(0, 448, 112):
-        tt(v("ct", 576 + a, 688 + a), v("ct", 64 + a, 176 + a), v("ct", a, 112 + a), A.subtract)
-    ts(v("ct", 0, 512), v("ct", 0, 512), 512.0, A.mult)
-    for t in range(2):
-        quant(blk("qc", t), blk("scc", t), v("ct", 512 * t, 512 * t + 512))
+        sel(v("ct", 64 + t, 576, 4), [[0, 4], [1, 2], [0, 16]], 0.0, t // 2 - 1, 0)
+    cp(v("ct", 0, 64), v("ct", 64, 128))
+    ts(v("cs"), v("ct", 64, 576), -2048.0, A.mult)
+    for t in range(4):
+        to = lambda r: v("cs", 4 * r + t, 512, 64)
+        for r in (0, 2):
+            tt(to(r), v("ct", 64 + t, 576, 64), v("ct", t, 512, 64), A.subtract)
+        ts(to(1), to(0), 512.0, A.mult)
+        cp(to(3), v("ct", t, 512, 64))
+        ms(to(COL), 0.0)
+    quant(v("qc"), v("scc"), v("cs"))
     for x in "AB":
-        ms(c1("eq" + x, 15), float(C))
+        ms(c1("eq" + x, 15), C - 2.0 * K)
         ms(v("cap" + x), -BIG)
-    fill(v("c512"), 512)
+    fill(v("c512", 0, 16), 1024)
+    fill(v("c512", 16), 0)
     cp(v("ou"), v("oui"))
     quant(v("qu0"), v("su0"), v("uin"))
     for i, (q, s) in enumerate(((blk("qu", 0), blk("su", 0)), (blk("qu", 1), blk("su", 1)))):
@@ -353,6 +374,7 @@ def rank_program(g, core, T, topo):
         tt(v("tab", 32 * j, 32 * j + 32), v("edge", j, j + 63, 2), v("fy", j, j + 63, 2), A.add)
     ms(v("mc"), -64.0)
     ts(MCF, v("qint"), 0.5, A.is_lt, BIG, A.mult)
+    ts(THM, MCF, -2.0 / BIG, A.mult, -1.0, A.add)
     ts(MCF, MCF, -64.0, A.add)
     ts(v("mcf"), v("zer", 0, 32), MCF, A.add)
     ts(v("mcz"), v("mcf"), 0.5, A.add, 4096.0, A.min)
@@ -361,11 +383,9 @@ def rank_program(g, core, T, topo):
     ms(v("rat", 64, 96), 0.0)
     ms(v("rat", 96, 128), 1.0)
     for i, x in enumerate("AB"):
-        w4 = 2 ** (12 + (5 in TWICE[x]))
-        w3 = w4 * 2 ** (5 + (4 in TWICE[x]))
+        w5, w4, w3 = 4 * 31, 4 * 1022, 2 ** 17
         w2 = w3 * 2 ** (5 + (3 in TWICE[x]))
-        second = 32 * (128 if 5 in TWICE[x] else w4)
-        for j, (a, b) in enumerate(((0, w3), (0, w4), (0, -128), (w4 - w3, -w3), (128 - w4, 125 - w4), (0, second), (-124, -125), (-4, 124 - w2))):
+        for j, (a, b) in enumerate(((0, w3), (0, w4), (0, -w5), (w4 - w3, w4 - w3), (w5 - w4, w5 - 3 - w4), (0, 0), (4 - w5, -1 - w5), (-4, w5 - w2))):
             act(c1("krow", 8 * i + j), J, ACT.Identity, bias=float(b), scale=float(a))
     ts(v("rat", 0, 32), v("j64", 32, 64), 1.0 / 64, A.mult)
     ts(v("rat", 32, 64), v("j64", 0, 32), 1.0 / 64, A.mult)
@@ -374,47 +394,58 @@ def rank_program(g, core, T, topo):
     j16 = v("j64", 0, 16)
     ts(v("ca"), j16, RF, A.not_equal)
     ts(v("cb"), j16, RP1, A.is_equal, 2.0 ** 20, A.mult)
-    ts(v("cd"), j16, RM1, A.not_equal)
-    ts(v("ce"), j16, RP1, A.is_equal, 2.0 ** 48, A.mult)
-    ts(v("m16", 16, 32), j16, RF, A.is_equal, 1024.0, A.mult)
-    tt(v("m16", 0, 16), v("ca"), v("cb"), A.max)
-    tt(v("cd"), v("cd"), v("ce"), A.max)
-    act(v("cmul"), v("m16", 0, 16), ACT.Copy, off=v("r16"))
-    act(v("hold"), v("m16", 16, 32), ACT.Copy, off=v("r16"))
-    ts(v("cf"), j16, RF, A.is_equal, 2.0 ** -10 - 2.0, A.mult)
-    tt(v("cg"), v("cd"), v("cf"), A.add)
-    act(v("csum"), v("cg"), ACT.Copy, off=v("r16"))
-    ts(UN0, RF, 15.0, A.is_equal)
+    tt(v("m16"), v("ca"), v("cb"), A.max)
+    act(v("cmul"), v("m16"), ACT.Copy, off=v("r16"))
+    ts(UN0, RF, float(COL), A.is_equal)
     ts(R0, RF, 0.0, A.is_equal)
-    ts(RN, RF, 0.0, A.not_equal)
     ts(UNB, UN0, 2.0 ** -20, A.max)
-    ts(U15, UN0, 2.0, A.mult, 2.0 ** -47, A.max)
-    ts(P14, R0, 2.0 ** -47, A.mult)
-    ts(M14, R0, -2.0 ** -47, A.mult)
-    ts(P15, U15, RN, A.mult)
-    ts(M15, U15, RN, A.mult, -1.0, A.mult)
-    ts(B14, RN, float(LOW), A.mult)
-    ts(B15, R0, float(LOW), A.mult)
-    fill(v("q0"), 0)
-    fill(v("q0", 0, 196, 7), LOW)
-    fill(v("q1"), LOW)
-    ts(v("q0", 3, 196, 7), v("col", 0, 28), -2.0, A.mult, -516.0, A.add)
-    ts(v("q0", 5, 196, 7), v("col", 0, 28), 2.0, A.mult, 516.0, A.add)
-    ms(c1("ll", 15), 0.0)
+    ts(MY, RF, float(NUM), A.is_ge)
+    ts(NB, RF, 2.0, A.is_ge, MY, A.subtract)
+    ts(NB, NB, -FAR, A.mult)
+    ts(v("cw"), v("cw"), MY, A.mult, NB, A.add)
+    ts(INI, MY, -LIFT, A.mult)
+    ts(INP, UN0, -1.0 - H, A.mult)
+    ts(CP, UN0, -1023.0, A.mult, 1024.0, A.add)
+    ts(v("cpay"), v("c512", 0, 256), 0.0, A.mult, CP, A.add)
+    iota(v("ci", 0, 32), [[32, 16], [C, 2]], 0)
+    iota(v("cj", 0, 32), [[32, 16], [32 - C, 2]], C - 16)
+    fill(c1("cj", 0), 2 * C - 16)
+    for a in (32, 40):
+        iota(v("ci", a, a + 8), [[32, 2], [160, 2], [-64, 2]], 96 + COL)
+        iota(v("cj", a, a + 8, 2), [[32, 2], [160, 2]], 16 + COL)
+        iota(v("cj", a + 1, a + 8, 2), [[32, 2], [-128, 2]], 240 + COL)
+    iota(v("ci", 48, 64), [[176, 2], [16, 4], [-64, 2]], 96)
+    iota(v("cj", 48, 64), [[176, 2], [16, 4], [80, 2]], 16)
+    ts(v("ci"), v("ci"), EV, A.mult)
+    ts(v("cj"), v("cj"), OD, A.mult)
+    tt(v("ci"), v("ci"), v("cj"), A.add)
+    for a, b, s, r in ((0, 96, 3, 2), (1, 96, 3, 3), (2, 96, 3, NUM), (96, 128, 1, 1), (128, 160, 1, 0)):
+        ts(v("lrow", a, b, s), v("ci", 0, 32), 2.0 * C - 16, A.min, float(r), A.add)
+    cp(v("lrow", 160, 176), v("ci", 32, 48))
+    ts(v("opl"), v("ci", 48, 64), RF, A.add)
+    ts(O2, EV, 16.0, A.mult, -1.0, A.add)
+    scan(v("lrow2"), v("cmul", 0, 176), v("lrow"), 0.0, A.mult, A.max)
+    ts(v("lst", 0, 11), v("lrow2", 15, 176, 16), UNB, A.mult)
+    fill(v("q0", 0, 96, 3), 2 ** 23)
+    ms(v("cq", 0, 96, 3), 0.0)
+    ts(v("cq", 1, 96, 3), v("col"), -0.5, A.mult, 0.5 - MET, A.add)
+    ts(v("cq", 2, 96, 3), v("col"), -1025.0, A.mult, 1024.0 * (H + 1) - 272 - MET, A.add)
+    for i, x in enumerate((EV, OD)):
+        ts(v("mll", 16 * i, 16 * i + 16), v("zer", 0, 16), R0, A.add, x, A.mult)
     for a in (0, 272):
-        fill(v("ti", a, a + 16), 512)
-        fill(v("tc", a, a + 16), 1)
-        fill(v("t0", a, a + 16), 1)
-    ts(O2, OD, 272.0, A.mult, 15.0, A.add)
-    ts(O3, EV, 16.0, A.mult, -1.0, A.add)
-    ts(O2F, O2, -FRAC, A.add)
-    ts(O3F, O3, -FRAC, A.add)
-    ts(EV9, EV, 2.0 ** -9, A.mult)
-    ts(OD9, OD, 2.0 ** -9, A.mult)
-    ts(v("loff", 18, 35), v("col", 0, 17), O2, A.add, O3, A.subtract)
-    for s in range(2, 5):
+        fill(v("tb", a, a + 16), 2048)
+    fill(v("fo"), 0)
+    for i in range(len(ADDED)):
+        fill(v("fz", FW * i, FW * i + C), 0)
+    ts(O1, OD, TAB[1] - 16.0, A.mult, 15.0, A.add)
+    ts(O3, O2, float(TAB[3]), A.add)
+    ts(HQ, OD, 16.0, A.mult)
+    ms(part(HQ, (32, 64)), float(TAB[2]))
+    for s in (1, 2):
         cp(v("loff", 18 * s, 18 * s + 17), v("col", 0, 17))
-    ts(v("loff", 90, 106), v("col", 0, 16), O3, A.add, 1.0, A.add)
+    for h in range(2):
+        for odd in range(2):
+            ts(v("loff", 54 + 10 * h + 5 * odd, 59 + 10 * h + 4 * odd), v("col", 8 * h + odd, 8 * h + 9, 2), HQ, A.add)
 
     def count_at(src, thr, c, slot):
         act(v("junk", C * slot, C * slot + size(src)), src, ACT.Sign, bias=thr, scale=-1.0, acc=c)
@@ -453,7 +484,7 @@ def rank_program(g, core, T, topo):
             m, t, wide_ = "m%d" % n, "t%d" % n, 32 * len(thr)
             for j, one in enumerate(thr):
                 count_at(src, one, s(2 * n + 10 + j), i + 2 * j)
-                ts(w(m, 32 * j, 32 * j + 32), v("mc" if j else "mcf"), s(2 * n + 10 + j), A.is_ge, wk(n - 3), A.mult)
+                ts(w(m, 32 * j, 32 * j + 32), v("mc" if j or n == 4 else "mcf"), s(2 * n + 10 + j), A.is_ge, wk(n - 3), A.mult)
             if n == 3:
                 ts(w(t, 7, 8), thr[0], wk(3), A.add)
             else:
@@ -492,7 +523,7 @@ def rank_program(g, core, T, topo):
             act(v("junk", C * (i + 2 * j), C * (i + 2 * j + 1)), rel, ACT.Sign, bias=one, acc=s(22 + j))
             ts(w("m5", 32 * j, 32 * j + 32), v("mc"), s(22 + j), A.is_ge, wk(2), A.mult)
         ts(w("t5", 7, 8), T5[0], wk(6), A.add, -1.0, A.mult)
-        ts(w("t5", 8 + n5, 9 + n5), W, -1.0, A.mult)
+        ts(w("t5", 8 + n5, 9 + n5), W, THM, A.mult)
         cp(w("cap", n5, n5 + 1), wk(7))
         tr(w("t5", 8, 8 + n5), w("m5", 0, n5))
         scan(w("u5", 0, n5 + 2), w("t5", 7, 9 + n5), w("cap", 0, n5 + 2), 0.0, A.add, A.max)
@@ -501,8 +532,11 @@ def rank_program(g, core, T, topo):
         for h, (a, b) in enumerate(PIECES):
             ts(w("eq", 16 + a, 16 + b), w("sp", a, b), TV, A.is_equal, 2.0, A.mult)
             lo = 16 + a if h else 15
-            scan(w("ns", lo, 16 + b), w("eq", lo, 16 + b), v("c512", lo, 16 + b), w("ns", lo - 1, lo) if h else SUM, A.add, A.min)
-            scan(v("mt", 4 * a + 2 * i, 4 * b, 4), w("ns", 15 + a, 15 + b), w("ns", 16 + a, 16 + b), 0.0, A.max, A.subtract)
+            scan(w("ns", lo, 16 + b), v("c512", lo, 16 + b), w("eq", lo, 16 + b), w("ns", lo - 1, lo) if h else SUM, A.min, A.add)
+            if MARKS[i][h] == "S":
+                act(v("mt", 4 * a + 2 * i, 4 * b, 4), w("ns", 16 + a, 16 + b), ACT.Relu)
+            else:
+                ts(v("mt", 4 * a + 2 * i, 4 * b, 4), w("ns", 16 + a, 16 + b), 0.0, A.max)
 
     def layer(h, qz, sz, qh, sh):
         for b in (0, 2, 1, 3):
@@ -530,49 +564,53 @@ def rank_program(g, core, T, topo):
             on = lambda n, first: c1(n, a - 1) if h else first
             pc = lambda n: v(n, a, b)
             quant(pc("qm"), pc("sm"), v("mt", 4 * a, 4 * b))
-            mm(bank(h, b - a), blk("qc", 1), blk("scc", 1), pc("qm"), pc("sm"))
-            mm(bank(6 + h, b - a), blk("qc", 0), blk("scc", 0), pc("qm"), pc("sm"))
-            scan(pc("vs"), bank(6 + h, b - a), pc("c257"), on("vs", -1.0), A.add, A.add)
-            scan(pc("vw"), pc("csum"), pc("vs"), on("vs", -1.0), A.mult, A.add)
-            scan(pc("dd"), bank(h, b - a), pc("zb"), on("dd", 0.0), A.add, A.add)
-            scan(v("ll", 16 + a, 16 + b), pc("dd"), pc("zb"), c1("ll", 15 + a) if h else 0.0, A.max, A.max)
-        scan(v("lp"), v("hold"), v("ll", 15, 15 + C), 0.0, A.add, A.min)
-        scan(v("li"), v("hold"), v("ll", 16, 16 + C), 0.0, A.add, A.min)
-        e6 = lambda n, j: v(n, j, 196, 7)
-        li, lp, LL = v("li", 15, C, 16), v("lp", 15, C, 16), c1("ll", C + 15)
-        y14, y15 = v("vw", 14, C, 16), v("vw", 15, C, 16)
-        act(e6("q1", 1), y14, ACT.Identity, scale=P14, bias=-1026.0)
-        act(e6("q1", 3), y14, ACT.Identity, scale=M14, bias=B14)
-        ts(e6("q1", 2), y15, P15, A.mult, -1026.0, A.add)
-        ts(e6("q1", 4), y15, M15, A.mult, B15, A.add)
-        ts(e6("q1", 0), li, 256.0, A.mult, LL, A.subtract)
-        ts(e6("q0", 1), lp, -254.0, A.mult)
-        ts(e6("q0", 6), lp, -1.0, A.mult)
-        scan(v("x3"), v("q0"), v("q1"), 0.0, A.add, A.max)
-        ts(v("pos"), e6("x3", 6), 16.0 - FRAC, A.add)
-        scat(v("ti"), v("pos"), v("vs"))
-        ts(v("tc", 16, 272), v("ti", 16, 272), 511, A.bitwise_and)
-        cp(v("t0", 16, 272), v("tc", 16, 272))
-        tr(v("tq", 0, 576, 2), v("ti", 0, 288))
-        tr(v("tq", 33, 545, 2), v("ti", 16, 272))
-        own = lambda j, m, n, p: v("tq", 32 * j + 33 * m, 32 * j + 33 * (m + n - 1) + 1, 33, p)
-        for s, j, a, b, n, add in ((0, 0, 0, 0, 128, 15.0 - FRAC), (1, 1, 0, 32, 32, O2F), (1, 1, 32, 64, 32, O2F), (1, 1, 64, 96, 32, O2F),
-                                   (2, 0, 32, 64, 32, O3F), (2, 0, 64, 96, 32, O3F), (3, 1, 0, 64, 64, O3F), (4, 0, 32, 96, 32, O3F)):
-            ts(v("loff", 18 * s, 18 * s + 17, p=(b, b + n)), own(j, 0, 17, (a, a + n)), 2.0 ** -9, A.mult, part(add, (a, a + n)) if s else add, A.add)
-        q = (0, 32)
-        ts(v("l6a", p=q), own(1, 1, 16, q), part(EV9, q), A.mult, part(O3F, q), A.add)
-        ts(v("l6b", p=q), own(1, 0, 16, q), part(OD9, q), A.mult)
-        tt(v("l6", p=q), v("l6a", p=q), v("l6b", p=q), A.add)
-        cp(v("loff", 90, 106, p=(96, 128)), v("l6", p=q))
-        ways = ((v("tc"), "t0", 288), (v("t0"), "ta", 0), (v("ta"), "tb", 0), (v("tb"), "ta", 0), (v("ta"), "tb", 0), (v("tb"), "ta", 0))
-        for s, (src, dst, o) in enumerate(ways):
-            n = 17 if s < 5 else 16
-            m = 8 if s else 12
-            act(v(dst, o, o + 16 * m), src, ACT.Copy, off=v("loff", 18 * s, 18 * s + m))
-            cp(v(dst, o + 16 * m, o + 16 * n), src, off=v("loff", 18 * s + m, 18 * s + n))
+            mm(bank(h, b - a), v("qc"), v("scc"), pc("qm"), pc("sm"))
+            scan(pc("rw"), pc("cw"), bank(h, b - a), on("rw", INI), A.max, A.subtract)
+            scan(pc("pay"), v("cpay", 0, b - a), bank(h, b - a), on("pay", INP), A.add, A.subtract)
+            if h == 0:
+                act(v("rw", C, C + 16), v("rw", 0, 16), ACT.Copy)
+            tr(pc("rt"), pc("rw"))
+            a2, b2 = a - 32 if h else 0, b if h else b - 32
+            tr(v("rt", C + a2, C + b2), v("rw", a2 + 16, b2 + 16))
+        ts(v("llb"), v("mll"), c1("rw", C - 1), A.mult, 0.0, A.max)
+        tr(v("llt"), v("llb"))
+        tt(v("q1"), v("rt"), v("cq"), A.add, off=v("lst", 0, 6))
+        ts(v("q0", 1, 96, 3), v("rt"), c1("llt", 0), A.add, c1("llt", 16), A.add, off=v("lst", 6, 8))
+        act(v("q0", 2, 96, 3), v("rt"), ACT.Copy, off=v("lst", 8, 10))
+        scan(v("x3"), v("q0", 0, 84), v("q1", 0, 84), 0.0, A.add, A.min)
+        ts(v("pos"), v("x3", 2, 84, 3), -1.0, A.mult, 16.0 - MET, A.add)
+        scat(v("tb", 0, TAB[1] + C), v("pos"), v("pay"))
+
+        def lists(to, o, a, n):
+            e = 32 * ((n + 1) // 2)
+            tr(v(to, o, o + e), v("tb", a, a + e))
+            tr(v(to, o + e, o + 32 * n), v("tb", a + 16, a + 16 + 32 * n - e))
+
+        def hand(at, n, s, b, src, o, a, parts, add):
+            ts(v("loff", at, at + s * (n - 1) + 1, s, (b, b + parts)), v(src, o + NUM, o + 32 * n - 16, 32, (a, a + parts)), 2.0 ** -11, A.mult,
+               part(add, (a, a + parts)) if isinstance(add, tuple) else add, A.add)
+
+        def shared(out, o, win, at, n, m):
+            act(v(out, o, o + 16 * m), win, ACT.Copy, off=v("loff", at, at + m))
+            if m < n:
+                cp(v(out, o + 16 * m, o + 16 * n), win, off=v("loff", at + m, at + n))
+
+        lists("tq", 0, 0, 17)
+        for at, b, j, a, parts, add in ((0, 0, 0, 0, 128, 15.0), (18, 32, 1, 0, 32, O1), (18, 96, 1, 64, 32, O1), (36, 96, 0, 64, 32, O2)):
+            for odd in range(2):
+                hand(at + odd, 9 - odd, 2, b, "tq", 288 * odd + 16 * j, a, parts, add)
+        shared("tb", TAB[1], v("tb", 0, TAB[1]), 0, 17, 8)
+        shared("tb", TAB[2], v("tb", 0, TAB[2]), 18, 17, 8)
+        shared("tb", TAB[3], v("tb", TAB[2], TAB[3]), 36, 17, 17)
         for h in range(2):
-            scan(blk("cs3", h), v("cmul", 0, 128), blk("ta", h), 0.0, A.mult, A.max)
-            ts(v("offc", 8 * h, 8 * h + 8), v("cs3", 128 * h + 15, 128 * h + 128, 16), UNB, A.mult)
+            lists("tm", 288 * h, TAB[2] - 16 + 128 * h, 9)
+            hand(54 + 10 * h, 9, 1, 64, "tm", 288 * h + 16, 32, 32, O1)
+            hand(54 + 10 * h, 9, 1, 96, "tm", 288 * h + 16, 32, 32, O3)
+            shared("fo", 176 * h + 16, v("tb", 0, TAB[4]), 54 + 10 * h, 9, 4)
+            for j in range(2):
+                a = 320 * h + 160 * j
+                tr(v("ft", a, a + 160), v("fo", 176 * h + 16 * j, 176 * h + 16 * j + 160))
+            ts(v("offc", 16 * h, 16 * h + 16), v("ft", 320 * h, 320 * h + 320), float(H), A.add, off=v("lst", 10, 11))
         qh, sh, ql, sl, arr = "qh%d" % k, "sh%d" % k, "ql%d" % k, "sl%d" % k, "arr%d" % k
         rid, pid, _ = topo.addr(partner)
         mask, ne = topo.mask(core, partner), len(topo.engines(core, partner))
@@ -582,7 +620,7 @@ def rank_program(g, core, T, topo):
             sent[0] = len(calls) - 1
 
         for h in range(2):
-            lo, hi, off = 128 * h, 128 * h + 128, v("offc", 8 * h, 8 * h + 8)
+            lo, hi, off = 128 * h, 128 * h + 128, v("offc", 16 * h, 16 * h + 8)
             for b in range(2):
                 act(v("zt", 4 * lo + 2 + b, 4 * hi, 4), v("ff", FW * (2 + b), FW * (2 + b) + C), ACT.Copy, off=off)
                 cp(v("zt", 4 * lo + b, 4 * hi, 4), v("ff", FW * b, FW * b + C), off=off, behind=first if h and b else None)
@@ -596,10 +634,11 @@ def rank_program(g, core, T, topo):
             send(T[sl][:, lo:hi], T[sh][:, lo:hi], blk(sh, h), blk(sl, h), 200, arr + "ab"[h])
         act(v("thf"), v("col1"), ACT.Copy, after=c1("nsB", 15))
         for h in range(2):
-            scat(v("thf"), v("offc", 8 * h, 8 * h + 8), blk("kio", h))
+            scat(v("thf"), v("offc", 16 * h, 16 * h + 8), blk("kio", h))
         alike.append((begin, len(calls)))
         if k == 2:
-            dma("Y", T.pl[:], T.ta[0:128:16, 0:K], [v("ta")], [])
+            act(v("plf"), v("fo"), ACT.Identity, bias=float(H), off=v("opl"))
+            dma("Y", T.pl[:], T.plf[COL:128:16, :], [v("plf")], [])
         for h in range(2):
             got = [blk(ql, h), blk(sl, h)]
             op("P", lambda arr=arr + "ab"[h], n=2 * ne: wait("P", arr, n), got, got, 1, -WAKE, "bare")
@@ -612,11 +651,16 @@ def rank_program(g, core, T, topo):
             for b in range(4):
                 out = bank(4 * h + b, 128)
                 mm(out, blk("qe", b), blk("se", b), *got)
-                tt(v("ff", FW * b + C + 128 * h, FW * b + C + 128 * h + 128), out, v("zt", 512 * h + b, 512 * h + 512, 4), A.add)
+                if b in ADDED:
+                    act(v("fz", FW * ADDED.index(b) + C + 128 * h, FW * ADDED.index(b) + C + 128 * h + 128), out, ACT.Copy)
+                else:
+                    tt(v("ff", FW * b + C + 128 * h, FW * b + C + 128 * h + 128), out, v("zt", 512 * h + b, 512 * h + 512, 4), A.add)
         for h, (lo, hi, by) in enumerate(LAST if k == 2 else RUNS):
             for b in range(4):
                 out, win, off = v("xt", 4 * lo + b, 4 * hi, 4), v("ff", FW * b, FW * b + FW), v("offt", lo // 16, hi // 16)
-                if by[b] == "V":
+                if b in ADDED:
+                    tt(out, v("fz", FW * ADDED.index(b), FW * ADDED.index(b) + FW), v("ff", FW * b + lo, FW * b + hi), A.add, off=off)
+                elif by[b] == "V":
                     cp(out, win, off=off)
                 else:
                     act(out, win, ACT.Copy, off=off)

import math
from concourse.mybir import dt, AluOpType, AxisListType, ActivationFunctionType

C, K, ROUNDS = 448, 256, (1, 2, 3)
H = C // 2
FW = C + K
F32, BF, I32, U16, Q4, U8 = "float32", "bfloat16", "int32", "uint16", "float8_e4m3fn_x4", "uint8"
SB = {
    "xin": (4 * C, BF), "uin": (512, BF), "vin": (512, BF), "qu0": (128, Q4), "su0": (128, U8), "qu": (256, Q4), "su": (256, U8),
    "qv": (128, Q4), "sv": (128, U8), "qw": (512, Q4), "sw": (512, U8),
    "ou": (16, U16), "r16": (28, U16), "et": (516, BF), "qe": (512, Q4), "se": (512, U8),
    "ct": (576, BF), "cs": (512, BF), "qc": (128, Q4), "scc": (128, U8), "m16": (16, BF), "cmul": (C, BF),
    "cw": (C, BF), "cpay": (256, BF), "lst": (12, U16), "opl": (16, U16),
    "xt": (4 * C, BF), "qx": (C, Q4), "sx": (C, U8), "ff": (4 * FW, BF), "fz": (2 * FW, BF),
    "junk": (6 * C, BF), "spA": (C, F32), "spB": (C, F32),
    "eqA": (C + 16, BF), "nsA": (C + 16, BF), "eqB": (C + 16, BF), "nsB": (C + 16, BF), "c512": (C + 16, BF),
    "mt": (4 * C, BF), "qm": (C, Q4), "sm": (C, U8), "rw": (C + 16, BF), "rt": (2 * C, BF), "pay": (C, BF),
    "pos": (28, U16), "tb": (1104, BF), "tq": (576, BF), "tm": (576, BF), "fo": (352, BF), "ft": (640, BF), "plf": (K, F32),
    "loff": (74, U16), "offc": (32, U16), "thf": (C, F32), "offt": (28, U16),
    "zt": (4 * K, BF), "qz": (128, Q4), "sz": (128, U8), "qp": (128, Q4), "sp": (128, U8), "ht": (4 * K, BF), "yo": (C, F32),
}
for _k in range(3):
    SB["qh%d" % _k], SB["sh%d" % _k], SB["ql%d" % _k], SB["sl%d" % _k] = (K, Q4), (K, U8), (K, Q4), (K, U8)
LINE = {"s": 32, "z0": 32, "m1": 32, "t1": 32, "u": 352, "cand": 256, "candt": 256, "m2": 64, "t2": 64, "wk": 16,
        "m3": 64, "t3": 80, "u3": 72, "m4": 64, "t4": 80, "u4": 72, "m5": 64, "t5": 80, "u5": 72, "cap": 72}
TWICE = {"A": (3,), "B": (2,)}
POOLS = {
    "kf": (F32, {"kc": 32, "dn": 16, "up": 16, "zer": 72, "lam": 64, "lt": 64, "fac": 64, "inc": 64, "edge": 72, "fx": 72, "fy": 72, "tab": 96,
                 "tabt": 96, "mcz": 32, "mch": 32,
                 "ca": 16, "cb": 16, "mc": 32, "mcf": 32, "rat": 224, "j64": 64, "krow": 16, "kd": 16,
                 "i16": 32, "col": 32, "col1": C, "kio": K, "ci": 64, "cj": 64, "lrow": 176, "lrow2": 176, "cq": 96,
                 "mll": 32}),
    "ki": (I32, {"pint": 2, "rint": 2, "hint": 1, "qint": 1, "oui": 16}),
    "wf": (F32, dict([(n + x, w) for x in "AB" for n, w in LINE.items()], q0=96, q1=96, x3=84, llb=32, llt=32, cs4=C)),
}
AT = {}
for _p, (_d, _m) in POOLS.items():
    _o = 0
    for _n, _w in _m.items():
        AT[_n] = (_p, _o, _w)
        _o += -(-_w // 8) * 8
    SB[_p] = (_o, _d)
SCRATCH = {n: ("sbuf", [128, w], d) for n, (w, d) in SB.items()}
PSUM = ["b%d" % _k for _k in range(8)]
for _n in PSUM:
    SCRATCH[_n] = ("psum", [128, 512], F32)
SEMAPHORES = ["sV", "sS", "sP", "sG", "snd"] + ["arr%d%s" % (k, h) for k in range(3) for h in "ab"] + ["d%d" % i for i in range(18)]

BIG = 2.0 ** 80
FAR, LIFT = 2.0 ** 30, 2.0 ** 20
MET = 258.0
NUM, COL = 4, 15
TAB = (0, 288, 560, 832, 1104)
PASSES, SHAKE, STRETCH = 5000, 1500, 5000
ORDER = []
WAKE = 230
PIECES = ((0, 256), (256, C))
RUNS = ((0, 192, "SSVV"), (192, 320, "SSSV"), (320, C, "SSVV"))
ADDED = ()
GAT = 1.5
MARKS = ("SS", "SS")
LAST = ((0, 160, "SSVV"), (160, 320, "SSSV"), (320, C, "SSVV"))


def rank_program(g, core, T, topo):
    rank = T.rank_of(core)
    if rank is None:
        return
    A, ACT = AluOpType, ActivationFunctionType
    Q = {"V": g.vector, "S": g.scalar, "P": g.tensor, "G": g, "Y": g.sync, "D": None}
    count = {"sV": 0, "sS": 0, "sP": 0, "sG": 0}
    known = {e: {} for e in Q}
    clock = {}
    log = {}
    calls = []
    soft = set()
    ndma, sent = [0], [None]
    alike = []

    def v(n, a=0, b=None, s=1, p=(0, 128)):
        buf, o, w = AT[n] if n in AT else (n, 0, T[n].shape[1])
        b = w if b is None else b
        return (T[buf][p[0]:p[1], o + a:o + b:s] if s > 1 else T[buf][p[0]:p[1], o + a:o + b], n, a, b, s, p)

    def c1(n, a):
        return v(n, a, a + 1)

    def part(x, p):
        return v(x[1], x[2], x[3], x[4], p)

    def meet(x, y):
        if x[3] <= y[2] or y[3] <= x[2] or x[5][1] <= y[5][0] or y[5][1] <= x[5][0]:
            return False
        return not (x[2] - y[2]) % math.gcd(x[4], y[4])

    def wait(e, sem, val):
        if known[e].get(sem, 0) >= val:
            return
        Q[e].wait_ge(T.sem[sem], val)
        known[e][sem] = val
        for s2, v2 in clock.get((sem, val), {}).items():
            if known[e].get(s2, 0) < v2:
                known[e][s2] = v2

    def op(e, call, reads, writes, cost, late=0, kind="calc", behind=None):
        if behind is not None:
            soft.add((behind, len(calls)))
        deps = set() if behind is None else {behind}
        both = [(x, False) for x in reads] + [(x, True) for x in writes]
        for view, wr in both:
            psum = view[1] in PSUM
            for (o, ow, i) in log.get(view[1], []):
                if (psum and calls[i][0] != e) or ((wr or ow) and meet(view, o)):
                    deps.add(i)
        for view, wr in both:
            old = log.get(view[1], [])
            if wr and view[4] == 1 and view[5] == (0, 128):
                old = [r for r in old if not (view[2] <= r[0][2] and r[0][3] <= view[3])]
            log[view[1]] = old + [(view, wr, len(calls))]
        calls.append((e, call, sorted(deps), cost, late, kind))

    def in_order():
        n = len(calls)
        cost, late, none = [c[3] for c in calls], [c[4] for c in calls], [0] * n
        ahead = [[(d, cost[d] + (0 if (d, i) in soft else late[d] + WAKE)) for d in c[2]] for i, c in enumerate(calls)]
        after = [[] for _ in calls]
        for i in range(n):
            for d, lag in ahead[i]:
                after[d].append((i, lag - cost[d] + cost[i]))
        seed = [1]

        def chance():
            seed[0] = (seed[0] * 1103515245 + 12345) % 2 ** 31
            return seed[0] / 2 ** 31

        def place(key, links, least):
            start, busy = [0] * n, {e: [] for e in Q}
            for _, i in sorted(zip(key, range(n))):
                t, c, slots = least[i], cost[i], busy[calls[i][0]]
                for d, lag in links[i]:
                    if start[d] + lag > t:
                        t = start[d] + lag
                k = len(slots)
                while k and slots[k - 1][1] > t:
                    k -= 1
                while k < len(slots) and slots[k][0] < t + c:
                    t = max(t, slots[k][1])
                    k += 1
                slots.insert(k, (t, t + c))
                start[i] = t
            return start

        def both(start):
            back = place([(-start[i] - cost[i], -i) for i in range(n)], after, late)
            return place([-back[i] - cost[i] for i in range(n)], ahead, none)

        tail = [0] * n
        for i in range(n - 1, -1, -1):
            tail[i] = max([tail[u] + lag for u, lag in after[i]] + [late[i]])
        start = place([-tail[i] - cost[i] for i in range(n)], ahead, none)
        best = None
        for turn in range(PASSES):
            end = max(start[i] + cost[i] + late[i] for i in range(n))
            if best is None or end <= best[0]:
                best = (end, start)
            key = list(best[1])
            if turn % 16 == 15:
                a, b = ((0, 1), (1, 2), (2, 1), (1, 0), (0, 2), (2, 0))[turn // 16 % 6]
                same = alike[a][1] - alike[a][0] if 2 in (a, b) else alike[1][0] - alike[0][0]
                a, b = alike[a][0], alike[b][0]
                shift = sorted(key[b + i] - key[a + i] for i in range(same))[same // 2]
                key[b:b + same] = [t + shift for t in key[a:a + same]]
            elif turn % 4 == 1:
                i = int(alike[0][0] * chance())
                key[i] *= chance()
                for i in range(i, -1, -1):
                    for d, _ in ahead[i]:
                        key[d] = min(key[d], key[i] - 1)
            elif turn > 3:
                mid, far, shake = best[0] * chance(), STRETCH * chance(), SHAKE * chance()
                key = [t + shake * (chance() - 0.5) if abs(t - mid) < far else t for t in key]
            for i in range(n):
                for d, _ in ahead[i]:
                    if key[d] >= key[i]:
                        key[i] = key[d] + 1
            start = both(place(key, ahead, none))
        return sorted(range(n), key=lambda i: (best[1][i], i))

    def issue():
        mark = {}
        if not ORDER:
            ORDER.extend(in_order())
        for i in ORDER:
            e, call, deps, _, _, kind = calls[i]
            for d in deps:
                if d in mark and (d, i) not in soft:
                    wait(e, *mark[d])
            if kind == "bare":
                call()
                continue
            if kind == "dma":
                mark[i] = ("d%d" % ndma[0], 16)
                ndma[0] += 1
                call().then_inc(T.sem[mark[i][0]], 16)
            else:
                count["s" + e] += 1
                mark[i] = ("s" + e, count["s" + e])
                call().then_inc(T.sem["s" + e], 1)
            clock[mark[i]] = dict(known[e])

    def aps(*xs):
        return [x for x in xs if isinstance(x, tuple)]

    def ap(x):
        return x[0] if isinstance(x, tuple) else x

    def size(x):
        return len(range(x[2], x[3], x[4]))

    def wide(*xs):
        return max(64, 30 + size(xs[0]) // (2 if all(SB.get(x[1], (0, F32))[1] == BF and x[4] == 1 for x in xs) else 1))

    def ts(o, i, s1, op0, s2=None, op1=None, off=None):
        src, cost = (i[0].indirect(off[0]), 60 + 1.5 * size(o)) if off else (i[0], wide(o, i))
        if op1 is None:
            op("V", lambda: g.vector.tensor_scalar(o[0], src, ap(s1), None, op0), aps(i, s1, off), [o], cost)
        else:
            op("V", lambda: g.vector.tensor_scalar(o[0], src, ap(s1), ap(s2), op0, op1), aps(i, s1, s2, off), [o], cost)

    def tt(o, a, b, op0, off=None):
        src = a[0].indirect(off[0]) if off else a[0]
        op("V", lambda: g.vector.tensor_tensor(o[0], src, b[0], op0), aps(a, b, off), [o],
           60 + GAT * size(o) if off else max(64, 30 + size(o) * (1 if a[1] in PSUM else 2)))

    def cp(o, i, off=None, behind=None):
        src = i[0].indirect(off[0]) if off else i[0]
        op("V", lambda: g.vector.tensor_copy(o[0], src), aps(i, off), [o], 60 + 1.5 * size(o) if off else wide(o, i), behind=behind)

    def pick(o, i, off):
        op("V", lambda: g.vector.tensor_copy(o[0].bitcast(dt.uint32), i[0].bitcast(dt.uint32).indirect(off[0])), [i, off], [o], 60 + 1.5 * size(o))

    def scat(o, off, i):
        op("V", lambda: g.vector.tensor_copy(o[0].indirect(off[0]), i[0]), [i, off], [o], 60 + 3.5 * size(i))

    def scan(o, d0, d1, init, op0, op1, after=None):
        op("V", lambda: g.vector.tensor_tensor_scan(o[0], d0[0], d1[0], ap(init), op0, op1), aps(d0, d1, init, after), [o], wide(o, d0, d1))

    def red(o, i, op0):
        op("V", lambda: g.vector.tensor_reduce(o[0], i[0], AxisListType.X, op0), [i], [o], max(64, size(i)))

    def tr(o, i):
        op("V", lambda: g.vector.transpose(o[0], i[0]), [i], [o], wide(o, i))

    def ms(o, val):
        op("V", lambda: g.vector.memset(o[0], val), [], [o], wide(o))

    def quant(q, s, i):
        op("V", lambda: g.vector.quantize_mx(q[0], s[0], i[0]), [i], [q, s], 15 + 0.265 * size(i))

    def mm(o, lq, ls, rq, rs):
        op("P", lambda: g.tensor.matmul_mx(o[0], lq[0], ls[0], rq[0], rs[0], True, True), [lq, ls, rq, rs], [o], 16 + size(o))

    def act(o, i, func, bias=None, scale=None, acc=None, off=None, after=None):
        src = i[0].indirect(off[0]) if off else i[0]
        kw = {}
        if bias is not None:
            kw["bias"] = ap(bias)
        if scale is not None:
            kw["scale"] = ap(scale)
        if acc is not None:
            kw["accum_out"] = acc[0]
        op("S", lambda: g.scalar.activation(o[0], src, func, **kw), aps(i, bias, scale, off, after), aps(o, acc),
           80 + max(64, size(o)) * (1.5 if off else 1) + (24 if acc else 0))

    def iota(o, pat, base, cm=0):
        if o[1] in POOLS["ki"][1]:
            op("G", lambda: g.iota(o[0], pat, base, cm), [], [o], 160 + 2 * size(o))
        else:
            op("G", lambda: g.iota(o[0], pat, base, cm, allow_small_or_imprecise_dtypes=True), [], [o], 160 + 2 * size(o))

    def fill(o, val):
        iota(o, [[0, size(o)]], val)

    def sel(o, pat, val, base, cm, keep=A.not_equal):
        op("G", lambda: g.affine_select(o[0], o[0], pat, keep, val, base, cm), [o], [o], 200 + 2 * size(o))

    def dma(e, o, i, reads, writes, late=2000, behind=None):
        op(e, lambda: Q[e].dma_start(o, i), reads, writes, 60, late, "dma", behind)
        if not writes:
            op("D", lambda: None, [], [], o.shape[0] * o.shape[1] * (4 if reads[0][1] in ("yo", "plf") else 1) / 200, late, "bare", len(calls) - 1)

    hv = lambda n, h: v(n, H * h, H * (h + 1))
    bank = lambda i, a, b=None: v("b%d" % i, 0, a) if b is None else v("b%d" % i, a, b)
    blk = lambda n, i: v(n, 128 * i, 128 * i + 128)
    dma("S", T.uin[:], T.u[:], [], [v("uin")], 2600)
    for a, b, _ in RUNS:
        dma("Y", T.xin[:, 4 * a:4 * b], T.x[:, 4 * a:4 * b], [], [v("xin", 4 * a, 4 * b)], 2600 + 5 * b, len(calls) - 1 if a else None)
    dma("Y", T.qw[:].bitcast(dt.uint8), T.wc[:], [v("xin")], [v("qw")])
    dma("Y", T.sw[:], T.ws[:], [v("xin")], [v("sw")])
    dma("Y", T.vin[:], T.v[:], [v("xin")], [v("vin")])

    (RF, RM1, RP1, OD, EV, J, SG, FM, D0, MCF, UN0, UNB, R0, MY, NB, INI, INP, CP,
     O1, O2, O3, HQ, THM) = [c1("kc", i) for i in range(23)]
    iota(v("pint"), [[15, 2]], 0, 1)
    iota(v("oui", 0, 16), [[16, 2], [32, 4], [0, 2]], 0)
    iota(v("j64"), [[1, 64]], 0)
    iota(v("i16"), [[16, 32]], 0)
    iota(v("col1"), [[1, C]], 1)
    iota(v("kio"), [[1, K]], C + 1)
    iota(v("cw"), [[1024, C]], -1024 * H)
    ms(v("zer"), 0.0)
    ts(v("rint"), v("pint"), 15, A.bitwise_and)
    ts(v("hint"), c1("pint", 0), 16, A.bitwise_and)
    ts(v("qint"), c1("pint", 0), 31, A.bitwise_and)
    cp(v("kc", 0, 2), v("rint"))
    cp(J, v("qint"))
    ts(RP1, c1("rint", 0), 1.0, A.add)
    ts(OD, v("hint"), 1.0 / 16, A.mult)
    ts(EV, v("hint"), -1.0 / 16, A.mult, 1.0, A.add)
    ts(v("col"), v("i16"), RF, A.add)
    ts(v("r16"), v("zer", 0, 28), RF, A.add)
    ms(v("et"), 0.0)
    sel(v("et"), [[1, 516]], 1.0, -3, -4)
    for b in range(4):
        quant(blk("qe", b), blk("se", b), v("et", 3 - b, 515 - b))
    ms(v("ct"), 0.0)
    ms(v("ct", 64, 576, 2), -0.5)
    sel(v("ct", 64, 576, 2), [[-32, 4], [0, 64]], 0.0, -1, 1, A.is_ge)
    sel(v("ct", 64, 576, 2), [[32, 4], [0, 64]], 0.0, 31, -1, A.is_ge)
    sel(v("ct", 65, 576, 2), [[-32, 4], [0, 64]], 0.5, 0, 1)
    for t in range(4):
        sel(v("ct", 64 + t, 576, 4), [[0, 4], [1, 2], [0, 16]], 0.0, t // 2 - 1, 0)
    cp(v("ct", 0, 64), v("ct", 64, 128))
    ts(v("cs"), v("ct", 64, 576), -2048.0, A.mult)
    for t in range(4):
        to = lambda r: v("cs", 4 * r + t, 512, 64)
        for r in (0, 2):
            tt(to(r), v("ct", 64 + t, 576, 64), v("ct", t, 512, 64), A.subtract)
        ts(to(1), to(0), 512.0, A.mult)
        cp(to(3), v("ct", t, 512, 64))
        ms(to(COL), 0.0)
    quant(v("qc"), v("scc"), v("cs"))
    for x in "AB":
        ms(c1("eq" + x, 15), C - 2.0 * K)
        ms(v("cap" + x), -BIG)
    fill(v("c512", 0, 16), 1024)
    fill(v("c512", 16), 0)
    cp(v("ou"), v("oui"))
    quant(v("qu0"), v("su0"), v("uin"))
    for i, (q, s) in enumerate(((blk("qu", 0), blk("su", 0)), (blk("qu", 1), blk("su", 1)))):
        pick(q, v("qu0"), v("ou", 8 * i, 8 * i + 8))
        act(s, v("su0"), ACT.Copy, off=v("ou", 8 * i, 8 * i + 8))
    quant(v("qv"), v("sv"), v("vin"))
    ms(v("dn"), 2.0 ** -8)
    ms(v("up"), 2.0 ** 8)
    for i in range(2):
        scan(v("lam", 32 * i, 32 * i + 16), v("dn"), v("zer", 0, 16), -2.0 ** 79, A.mult, A.add)
        scan(v("lam", 32 * i + 16 + i, 32 * i + 32), v("up", i, 16), v("zer", i, 16), 2.0 ** (8 * i - 65), A.mult, A.add)
    ms(c1("lam", 48), 0.0)
    tr(v("lt"), v("lam"))
    E0, T1 = c1("lt", 0), c1("lt", 32)
    ts(SG, v("hint"), 0.125, A.mult, -1.0, A.add)
    ts(FM, v("hint"), 1.5 / 16, A.mult, 0.5, A.add)
    ts(D0, v("hint"), 0.1875 / 16, A.mult, -0.0625, A.add)
    ts(D0, D0, E0, A.mult)
    ms(v("fac"), 1.0)
    ts(v("fac", 8, 64, 8), v("zer", 0, 7), FM, A.add)
    scan(v("inc"), v("fac"), v("zer", 0, 64), D0, A.mult, A.add)
    cp(c1("edge", 0), E0)
    scan(v("edge", 1, 65), v("inc"), v("zer", 0, 64), E0, A.add, A.add)
    ts(v("fx", 0, 65), v("edge", 0, 65), SG, A.mult, 2.0 ** -56, A.subtract)
    ts(v("fy", 0, 65), v("fx", 0, 65), 0.0, A.min, SG, A.mult)
    for j in range(3):
        tt(v("tab", 32 * j, 32 * j + 32), v("edge", j, j + 63, 2), v("fy", j, j + 63, 2), A.add)
    ms(v("mc"), -64.0)
    ts(MCF, v("qint"), 0.5, A.is_lt, BIG, A.mult)
    ts(THM, MCF, -2.0 / BIG, A.mult, -1.0, A.add)
    ts(MCF, MCF, -64.0, A.add)
    ts(v("mcf"), v("zer", 0, 32), MCF, A.add)
    ts(v("mcz"), v("mcf"), 0.5, A.add, 4096.0, A.min)
    tr(v("tabt"), v("tab"))
    ms(v("mch"), -63.5)
    ms(v("rat", 64, 96), 0.0)
    ms(v("rat", 96, 128), 1.0)
    for i, x in enumerate("AB"):
        w5, w4, w3 = 4 * 31, 4 * 1022, 2 ** 17
        w2 = w3 * 2 ** (5 + (3 in TWICE[x]))
        for j, (a, b) in enumerate(((0, w3), (0, w4), (0, -w5), (w4 - w3, w4 - w3), (w5 - w4, w5 - 3 - w4), (0, 0), (4 - w5, -1 - w5), (-4, w5 - w2))):
            act(c1("krow", 8 * i + j), J, ACT.Identity, bias=float(b), scale=float(a))
    ts(v("rat", 0, 32), v("j64", 32, 64), 1.0 / 64, A.mult)
    ts(v("rat", 32, 64), v("j64", 0, 32), 1.0 / 64, A.mult)
    ts(v("rat", 128, 160), v("j64", 0, 32), 1.0 / 32, A.mult)
    cp(v("rat", 160, 224), v("rat", 64, 128))
    j16 = v("j64", 0, 16)
    ts(v("ca"), j16, RF, A.not_equal)
    ts(v("cb"), j16, RP1, A.is_equal, 2.0 ** 20, A.mult)
    tt(v("m16"), v("ca"), v("cb"), A.max)
    act(v("cmul"), v("m16"), ACT.Copy, off=v("r16"))
    ts(UN0, RF, float(COL), A.is_equal)
    ts(R0, RF, 0.0, A.is_equal)
    ts(UNB, UN0, 2.0 ** -20, A.max)
    ts(MY, RF, float(NUM), A.is_ge)
    ts(NB, RF, 2.0, A.is_ge, MY, A.subtract)
    ts(NB, NB, -FAR, A.mult)
    ts(v("cw"), v("cw"), MY, A.mult, NB, A.add)
    ts(INI, MY, -LIFT, A.mult)
    ts(INP, UN0, -1.0 - H, A.mult)
    ts(CP, UN0, -1023.0, A.mult, 1024.0, A.add)
    ts(v("cpay"), v("c512", 0, 256), 0.0, A.mult, CP, A.add)
    iota(v("ci", 0, 32), [[32, 16], [C, 2]], 0)
    iota(v("cj", 0, 32), [[32, 16], [32 - C, 2]], C - 16)
    fill(c1("cj", 0), 2 * C - 16)
    for a in (32, 40):
        iota(v("ci", a, a + 8), [[32, 2], [160, 2], [-64, 2]], 96 + COL)
        iota(v("cj", a, a + 8, 2), [[32, 2], [160, 2]], 16 + COL)
        iota(v("cj", a + 1, a + 8, 2), [[32, 2], [-128, 2]], 240 + COL)
    iota(v("ci", 48, 64), [[176, 2], [16, 4], [-64, 2]], 96)
    iota(v("cj", 48, 64), [[176, 2], [16, 4], [80, 2]], 16)
    ts(v("ci"), v("ci"), EV, A.mult)
    ts(v("cj"), v("cj"), OD, A.mult)
    tt(v("ci"), v("ci"), v("cj"), A.add)
    for a, b, s, r in ((0, 96, 3, 2), (1, 96, 3, 3), (2, 96, 3, NUM), (96, 128, 1, 1), (128, 160, 1, 0)):
        ts(v("lrow", a, b, s), v("ci", 0, 32), 2.0 * C - 16, A.min, float(r), A.add)
    cp(v("lrow", 160, 176), v("ci", 32, 48))
    ts(v("opl"), v("ci", 48, 64), RF, A.add)
    ts(O2, EV, 16.0, A.mult, -1.0, A.add)
    scan(v("lrow2"), v("cmul", 0, 176), v("lrow"), 0.0, A.mult, A.max)
    ts(v("lst", 0, 11), v("lrow2", 15, 176, 16), UNB, A.mult)
    fill(v("q0", 0, 96, 3), 2 ** 23)
    ms(v("cq", 0, 96, 3), 0.0)
    ts(v("cq", 1, 96, 3), v("col"), -0.5, A.mult, 0.5 - MET, A.add)
    ts(v("cq", 2, 96, 3), v("col"), -1025.0, A.mult, 1024.0 * (H + 1) - 272 - MET, A.add)
    for i, x in enumerate((EV, OD)):
        ts(v("mll", 16 * i, 16 * i + 16), v("zer", 0, 16), R0, A.add, x, A.mult)
    for a in (0, 272):
        fill(v("tb", a, a + 16), 2048)
    fill(v("fo"), 0)
    for i in range(len(ADDED)):
        fill(v("fz", FW * i, FW * i + C), 0)
    ts(O1, OD, TAB[1] - 16.0, A.mult, 15.0, A.add)
    ts(O3, O2, float(TAB[3]), A.add)
    ts(HQ, OD, 16.0, A.mult)
    ms(part(HQ, (32, 64)), float(TAB[2]))
    for s in (1, 2):
        cp(v("loff", 18 * s, 18 * s + 17), v("col", 0, 17))
    for h in range(2):
        for odd in range(2):
            ts(v("loff", 54 + 10 * h + 5 * odd, 59 + 10 * h + 4 * odd), v("col", 8 * h + odd, 8 * h + 9, 2), HQ, A.add)

    def count_at(src, thr, c, slot):
        act(v("junk", C * slot, C * slot + size(src)), src, ACT.Sign, bias=thr, scale=-1.0, acc=c)

    def new_run(k, h, a, b):
        quant(v("qx", a, b), v("sx", a, b), v("xin" if k == 0 else "xt", 4 * a, 4 * b))
        if k < 3:
            for i, x in enumerate("AB"):
                mm(bank(2 + 2 * h + i, b - a), blk("qu", i), blk("su", i), v("qx", a, b), v("sx", a, b))
                count_at(bank(2 + 2 * h + i, b - a), T1, c1("s" + x, h), i + 2 * h)
        else:
            out = bank(2 + 2 * h, b - a)
            mm(out, v("qv"), v("sv"), v("qx", a, b), v("sx", a, b))
            dma("Y", T.oc[:, 4 * a:4 * b], T.qx[:, a:b].bitcast(dt.uint8), [v("qx", a, b)], [])
            if b == C:
                for i in range(4):
                    dma("YS"[i % 2], T.osc[4 * i:4 * i + 4, :], T.sx[32 * i:32 * i + 4, :], [v("sx")], [])
                cp(v("yo", a, b), out)
            else:
                act(v("yo", a, b), out, ACT.Copy)
            dma("SY"[b == C], T.y[:, a:b], T.yo[:, a:b], [v("yo", a, b)], [])

    def search(i, x):
        s = lambda j: c1("s" + x, j)
        w = lambda n, a=0, b=None: v(n + x, a, b)
        wk = lambda j: c1("wk" + x, j)
        raw, rel = bank(i, C), v("sp" + x)
        W = s(9)
        twice = TWICE[x]

        def choose(a, z, row):
            scan(w("u", a, a + size(row)), z, row, 0.0, A.max, A.min)
            return w("u", a + size(row) - 1, a + size(row))

        def step(n, src, thr, nxt):
            m, t, wide_ = "m%d" % n, "t%d" % n, 32 * len(thr)
            for j, one in enumerate(thr):
                count_at(src, one, s(2 * n + 10 + j), i + 2 * j)
                ts(w(m, 32 * j, 32 * j + 32), v("mc" if j or n == 4 else "mcf"), s(2 * n + 10 + j), A.is_ge, wk(n - 3), A.mult)
            if n == 3:
                ts(w(t, 7, 8), thr[0], wk(3), A.add)
            else:
                ts(w(t, 7, 8), thr[0], LO, A.subtract, wk(4), A.add)
            tr(w(t, 8, 8 + wide_), w(m, 0, wide_))
            if nxt == 2:
                cp(w(t, 8 + wide_, 9 + wide_), wk(5))
            scan(w("u%d" % n, 0, wide_ + nxt), w(t, 7, 7 + wide_ + nxt), v("zer", 0, wide_ + nxt), 0.0, A.add, A.add)
            return [w("u%d" % n, wide_ + j, wide_ + j + 1) for j in range(nxt)]

        ts(w("z0"), v("mcz"), s(0), A.subtract, s(1), A.subtract)
        ts(w("m1"), w("z0"), s(2), A.subtract, BIG, A.mult)
        tr(w("t1"), w("m1"))
        ends = (0, 1, 2) if 2 in twice else (0, 2)
        edge = [choose(32 * j, w("t1"), v("tabt", 32 * j, 32 * j + 32)) for j in ends]
        n2 = len(ends) - 1
        n3 = 1 + (3 in twice)
        rat = v("rat", 0, 128) if n3 == 2 else v("rat", 128, 224)
        for j in range(n2):
            count_at(raw, edge[j], s(4 + j), i + 2 * j)
            ts(s(6 + j), edge[j + 1], edge[j], A.subtract)
            ts(w("cand", 128 * j, 128 * j + size(rat)), rat, s(6 + j), A.mult, edge[j], A.add)
            tr(v("candt" + x, j, n2 * size(rat), n2), w("cand", 128 * j, 128 * j + size(rat)))
            ts(w("m2", 32 * j, 32 * j + 32), v("mch" if j else "mcz"), s(4 + j), A.subtract, BIG, A.mult)
            tr(v("t2" + x, j, 32 * n2, n2), w("m2", 32 * j, 32 * j + 32))
        got = [choose(96 + 32 * n2 * j, w("t2", 0, 32 * n2), w("candt", 32 * n2 * j, 32 * n2 * (j + 1))) for j in range(n3 + 2)]
        T3, LO, HI = got[:n3][::-1], got[n3], got[n3 + 1]
        ts(W, HI, LO, A.subtract, 2.0 ** (n2 - 24), A.mult)
        ts(w("wk", 0, 8), v("krow", 8 * i, 8 * i + 8), W, A.mult)
        for h in range(2):
            ts(hv("sp" + x, h), bank(6 + i, H * h, H * h + H), LO, A.subtract, -1.0, A.mult)
        T4 = step(3, raw, T3, 1 + (4 in twice))
        T5 = step(4, raw, T4, 1 + (5 in twice))
        n5 = 32 * len(T5)
        for j, one in enumerate(T5):
            act(v("junk", C * (i + 2 * j), C * (i + 2 * j + 1)), rel, ACT.Sign, bias=one, acc=s(22 + j))
            ts(w("m5", 32 * j, 32 * j + 32), v("mc"), s(22 + j), A.is_ge, wk(2), A.mult)
        ts(w("t5", 7, 8), T5[0], wk(6), A.add, -1.0, A.mult)
        ts(w("t5", 8 + n5, 9 + n5), W, THM, A.mult)
        cp(w("cap", n5, n5 + 1), wk(7))
        tr(w("t5", 8, 8 + n5), w("m5", 0, n5))
        scan(w("u5", 0, n5 + 2), w("t5", 7, 9 + n5), w("cap", 0, n5 + 2), 0.0, A.add, A.max)
        TV, TH, SUM = w("u5", n5, n5 + 1), w("u5", n5 + 1, n5 + 2), s(24)
        act(v("mt", 2 * i + 1, 4 * C, 4), rel, ACT.Sign, bias=TH, scale=-1.0, acc=SUM)
        for h, (a, b) in enumerate(PIECES):
            ts(w("eq", 16 + a, 16 + b), w("sp", a, b), TV, A.is_equal, 2.0, A.mult)
            lo = 16 + a if h else 15
            scan(w("ns", lo, 16 + b), v("c512", lo, 16 + b), w("eq", lo, 16 + b), w("ns", lo - 1, lo) if h else SUM, A.min, A.add)
            if MARKS[i][h] == "S":
                act(v("mt", 4 * a + 2 * i, 4 * b, 4), w("ns", 16 + a, 16 + b), ACT.Relu)
            else:
                ts(v("mt", 4 * a + 2 * i, 4 * b, 4), w("ns", 16 + a, 16 + b), 0.0, A.max)

    def layer(h, qz, sz, qh, sh):
        for b in (0, 2, 1, 3):
            out, to = bank(4 * h + b, 128), v("ht", 512 * h + b, 512 * h + 512, 4)
            mm(out, blk("qw", b), blk("sw", b), qz, sz)
            if b < 2:
                ts(to, out, 0.0, A.max, 0.015625, A.mult)
            else:
                act(to, out, ACT.Relu, scale=0.015625)
        quant(qh, sh, v("ht", 512 * h, 512 * h + 512))

    for h, (a, b, _) in enumerate(RUNS):
        new_run(0, h, a, b)
    for k, e in enumerate(ROUNDS):
        partner, begin = T.cores[rank ^ e], len(calls)
        for i in (0, 1, 6, 7):
            mm(bank(i, C), blk("qu", i % 2), blk("su", i % 2), v("qx"), v("sx"))
        for b in range(4):
            mm(bank(2 + b, C), blk("qe", b), blk("se", b), v("qx"), v("sx"))
        for i, x in enumerate("AB"):
            search(i, x)
        for b in range(4):
            act(v("ff", FW * b, FW * b + C), bank(2 + b, C), ACT.Copy, after=c1("sB", 24))
        for h, (a, b) in enumerate(PIECES):
            on = lambda n, first: c1(n, a - 1) if h else first
            pc = lambda n: v(n, a, b)
            quant(pc("qm"), pc("sm"), v("mt", 4 * a, 4 * b))
            mm(bank(h, b - a), v("qc"), v("scc"), pc("qm"), pc("sm"))
            scan(pc("rw"), pc("cw"), bank(h, b - a), on("rw", INI), A.max, A.subtract)
            scan(pc("pay"), v("cpay", 0, b - a), bank(h, b - a), on("pay", INP), A.add, A.subtract)
            if h == 0:
                act(v("rw", C, C + 16), v("rw", 0, 16), ACT.Copy)
            tr(pc("rt"), pc("rw"))
            a2, b2 = a - 32 if h else 0, b if h else b - 32
            tr(v("rt", C + a2, C + b2), v("rw", a2 + 16, b2 + 16))
        ts(v("llb"), v("mll"), c1("rw", C - 1), A.mult, 0.0, A.max)
        tr(v("llt"), v("llb"))
        tt(v("q1"), v("rt"), v("cq"), A.add, off=v("lst", 0, 6))
        ts(v("q0", 1, 96, 3), v("rt"), c1("llt", 0), A.add, c1("llt", 16), A.add, off=v("lst", 6, 8))
        act(v("q0", 2, 96, 3), v("rt"), ACT.Copy, off=v("lst", 8, 10))
        scan(v("x3"), v("q0", 0, 84), v("q1", 0, 84), 0.0, A.add, A.min)
        ts(v("pos"), v("x3", 2, 84, 3), -1.0, A.mult, 16.0 - MET, A.add)
        scat(v("tb", 0, TAB[1] + C), v("pos"), v("pay"))

        def lists(to, o, a, n):
            e = 32 * ((n + 1) // 2)
            tr(v(to, o, o + e), v("tb", a, a + e))
            tr(v(to, o + e, o + 32 * n), v("tb", a + 16, a + 16 + 32 * n - e))

        def hand(at, n, s, b, src, o, a, parts, add):
            ts(v("loff", at, at + s * (n - 1) + 1, s, (b, b + parts)), v(src, o + NUM, o + 32 * n - 16, 32, (a, a + parts)), 2.0 ** -11, A.mult,
               part(add, (a, a + parts)) if isinstance(add, tuple) else add, A.add)

        def shared(out, o, win, at, n, m):
            act(v(out, o, o + 16 * m), win, ACT.Copy, off=v("loff", at, at + m))
            if m < n:
                cp(v(out, o + 16 * m, o + 16 * n), win, off=v("loff", at + m, at + n))

        lists("tq", 0, 0, 17)
        for at, b, j, a, parts, add in ((0, 0, 0, 0, 128, 15.0), (18, 32, 1, 0, 32, O1), (18, 96, 1, 64, 32, O1), (36, 96, 0, 64, 32, O2)):
            for odd in range(2):
                hand(at + odd, 9 - odd, 2, b, "tq", 288 * odd + 16 * j, a, parts, add)
        shared("tb", TAB[1], v("tb", 0, TAB[1]), 0, 17, 8)
        shared("tb", TAB[2], v("tb", 0, TAB[2]), 18, 17, 8)
        shared("tb", TAB[3], v("tb", TAB[2], TAB[3]), 36, 17, 17)
        for h in range(2):
            lists("tm", 288 * h, TAB[2] - 16 + 128 * h, 9)
            hand(54 + 10 * h, 9, 1, 64, "tm", 288 * h + 16, 32, 32, O1)
            hand(54 + 10 * h, 9, 1, 96, "tm", 288 * h + 16, 32, 32, O3)
            shared("fo", 176 * h + 16, v("tb", 0, TAB[4]), 54 + 10 * h, 9, 4)
            for j in range(2):
                a = 320 * h + 160 * j
                tr(v("ft", a, a + 160), v("fo", 176 * h + 16 * j, 176 * h + 16 * j + 160))
            ts(v("offc", 16 * h, 16 * h + 16), v("ft", 320 * h, 320 * h + 320), float(H), A.add, off=v("lst", 10, 11))
        qh, sh, ql, sl, arr = "qh%d" % k, "sh%d" % k, "ql%d" % k, "sl%d" % k, "arr%d" % k
        rid, pid, _ = topo.addr(partner)
        mask, ne = topo.mask(core, partner), len(topo.engines(core, partner))

        def send(to, what, reads, lands, cost, arr, pid=pid, rid=rid, mask=mask):
            op("G", lambda: g.remote_dma(to, what, T.sem[arr], T.sem.snd, pid, rid, mask), [reads], [lands], cost, 2200, "bare", sent[0])
            sent[0] = len(calls) - 1

        for h in range(2):
            lo, hi, off = 128 * h, 128 * h + 128, v("offc", 16 * h, 16 * h + 8)
            for b in range(2):
                act(v("zt", 4 * lo + 2 + b, 4 * hi, 4), v("ff", FW * (2 + b), FW * (2 + b) + C), ACT.Copy, off=off)
                cp(v("zt", 4 * lo + b, 4 * hi, 4), v("ff", FW * b, FW * b + C), off=off, behind=first if h and b else None)
            if h == 0:
                first = len(calls)
                quant(blk(qh, 0), blk(sh, 0), v("zt", 0, 512))
            else:
                quant(v("qz"), v("sz"), v("zt", 512, 1024))
                layer(1, v("qz"), v("sz"), blk(qh, 1), blk(sh, 1))
            send(T[ql][:, lo:hi].bitcast(dt.uint8), T[qh][:, lo:hi].bitcast(dt.uint8), blk(qh, h), blk(ql, h), 800, arr + "ab"[h])
            send(T[sl][:, lo:hi], T[sh][:, lo:hi], blk(sh, h), blk(sl, h), 200, arr + "ab"[h])
        act(v("thf"), v("col1"), ACT.Copy, after=c1("nsB", 15))
        for h in range(2):
            scat(v("thf"), v("offc", 16 * h, 16 * h + 8), blk("kio", h))
        alike.append((begin, len(calls)))
        if k == 2:
            act(v("plf"), v("fo"), ACT.Identity, bias=float(H), off=v("opl"))
            dma("Y", T.pl[:], T.plf[COL:128:16, :], [v("plf")], [])
        for h in range(2):
            got = [blk(ql, h), blk(sl, h)]
            op("P", lambda arr=arr + "ab"[h], n=2 * ne: wait("P", arr, n), got, got, 1, -WAKE, "bare")
            if h == 0:
                layer(0, *got, v("qp"), v("sp"))
                got = [v("qp"), v("sp")]
                for j in range(2):
                    scan(hv("cs4", j), hv("cmul", j), hv("thf", j), 0.0, A.mult, A.max, after=v("ht", 1, 512, 4) if j else None)
                ts(v("offt"), v("cs4", 15, C, 16), UNB, A.mult, -1.0, A.add)
            for b in range(4):
                out = bank(4 * h + b, 128)
                mm(out, blk("qe", b), blk("se", b), *got)
                if b in ADDED:
                    act(v("fz", FW * ADDED.index(b) + C + 128 * h, FW * ADDED.index(b) + C + 128 * h + 128), out, ACT.Copy)
                else:
                    tt(v("ff", FW * b + C + 128 * h, FW * b + C + 128 * h + 128), out, v("zt", 512 * h + b, 512 * h + 512, 4), A.add)
        for h, (lo, hi, by) in enumerate(LAST if k == 2 else RUNS):
            for b in range(4):
                out, win, off = v("xt", 4 * lo + b, 4 * hi, 4), v("ff", FW * b, FW * b + FW), v("offt", lo // 16, hi // 16)
                if b in ADDED:
                    tt(out, v("fz", FW * ADDED.index(b), FW * ADDED.index(b) + FW), v("ff", FW * b + lo, FW * b + hi), A.add, off=off)
                elif by[b] == "V":
                    cp(out, win, off=off)
                else:
                    act(out, win, ACT.Copy, off=off)
            new_run(k + 1, h, lo, hi)

    issue()
    wait("G", "snd", 12 * ne)
    for i in range(ndma[0]):
        wait("G", "d%d" % i, 16)
    for s in count:
        wait("G", s, count[s])
